import numpy as np
import ml_dtypes


def mxq(x, axis, fmt="e4m3"):
    dtype, down = {"e4m3": (ml_dtypes.float8_e4m3fn, 7), "e5m2": (ml_dtypes.float8_e5m2, 14)}[fmt]
    v = np.moveaxis(np.asarray(x, np.float32).astype(ml_dtypes.bfloat16).astype(np.float64), axis, -1)
    blocks = v.reshape(v.shape[:-1] + (-1, 32))
    amax = np.abs(blocks).max(-1, keepdims=True)
    byte = np.maximum(np.where(amax > 0, np.frexp(amax)[1] - 1 + 127, 0) - down, 1)
    scale = np.exp2(byte - 127.0)
    codes = (blocks / scale).astype(np.float32).astype(dtype).astype(np.float64)
    return np.moveaxis((codes * scale).reshape(v.shape), -1, axis)


WIDE = False


def mx_kscale(k):
    if not WIDE:
        return np.ones(k)
    levels = np.array([10, -10, 5, -5, 0])
    if k % 512:
        return np.exp2(np.random.permutation(np.resize(levels, k // 32))).repeat(32)
    a = np.empty((k // 512, 16))
    for p in range(k // 512):
        a[p, :8] = np.random.permutation(np.resize(levels, 8))
        for g in range(8):
            far = levels[np.abs(levels - a[p, g]) >= 10]
            a[p, g + 8] = far[np.random.randint(len(far))]
    return np.exp2(a.ravel()).repeat(32)


def f64(x):
    return np.asarray(x).astype(np.float64)


def striped(idx):
    return np.tile(idx.reshape(-1, 16).T, (8, 1)).astype(np.uint16)


def unstriped(offs):
    return offs[:16].T.reshape(-1).astype(np.int64)


def striped8(idx):
    return np.concatenate([x.reshape(-1, 16).T for x in idx]).astype(np.uint16)


def runs(offs, k):
    lists = np.stack([offs[16 * r : 16 * r + 16].T.reshape(-1) for r in range(8)]).astype(np.int64)
    return lists[np.arange(k) % 512 // 64]


def pack_weight(w):
    k, n = w.shape
    w = f64(np.asarray(w, np.float32).astype(ml_dtypes.bfloat16)).reshape(k // 32, 32, n)
    amax = np.abs(w).max(1)
    byte = np.clip(np.where(amax > 0, np.frexp(amax)[1] - 1 + 127 - 7, 1), 1, 254)
    scaled = (w * np.exp2(127.0 - byte)[:, None, :]).reshape(k, n).astype(np.float32)
    words = np.ascontiguousarray(scaled.reshape(k // 512, 128, 4, n).transpose(0, 1, 3, 2)).astype(ml_dtypes.float8_e4m3fn).view(np.uint8)
    return words, np.ascontiguousarray(byte.astype(np.uint8).reshape(k // 512, 16, n))


def unpack_weight(words, scales):
    g, p, n, _ = words.shape
    vals = np.ascontiguousarray(words).view(ml_dtypes.float8_e4m3fn).astype(np.float64) * np.repeat(np.exp2(scales.astype(np.float64) - 127.0), 8, axis=1)[..., None]
    return vals.transpose(0, 1, 3, 2).reshape(g * 512, n)


K, T, S, N, H = 512, 2048, 512, 512, 512


def setup_inputs():
    n = np.random.standard_normal
    s = mx_kscale(K)[:, None]
    u = mx_kscale(H)
    packed_xT = pack_weight(n((K, T)) * s)
    return {
        "x_words": packed_xT[0],
        "x_scales": packed_xT[1],
        "w1": (n((K, H)) / np.sqrt(K) / s).astype(np.float32),
        "q": np.random.uniform(0.5, 1.5, (H, S)).astype(np.float32),
        "gn": (np.random.uniform(0.5, 1.5, (H, 1)) * u[:, None]).astype(np.float32),
        "w2": (n((H, N)) / np.sqrt(H) / u[:, None]).astype(np.float32),
        "offs": striped(np.random.permutation(T)[:S]),
        "p1": striped8(np.stack([np.random.permutation(S) for _ in range(8)])),
        "p2": striped8(np.stack([np.random.permutation(S) for _ in range(8)])),
    }


def reference(x_words, x_scales, w1, q, gn, w2, offs, p1, p2):
    xq = unpack_weight(x_words, x_scales)[:, unstriped(offs)]
    y = mxq(f64(w1), 0, "e4m3").T @ xq
    d1 = y[np.arange(H)[:, None], runs(p1, H)] - y
    s1 = f64(q) / ((d1) ** 2 + 1)
    d2 = y[np.arange(H)[:, None], runs(p2, H)] - y
    s2 = f64(q) / ((d2) ** 2 + 1)
    z = f64(gn) * (d1 * ((s1) ** 2 - s1) + d2 * ((s2) ** 2 - s2))
    return mxq(f64(w2), 0, "e4m3").T @ mxq(z, 0, "e4m3")

@@ -1,0 +1,178 @@
+from contextlib import ExitStack
+
+import concourse.mybir as mybir
+
+K, T, S, N, H = 512, 2048, 512, 512, 512
+FLOPS = 2 * K * H * S + 2 * H * N * S
+
+F32 = mybir.dt.float32
+BF16 = mybir.dt.bfloat16
+I32 = mybir.dt.int32
+U32 = mybir.dt.uint32
+U16 = mybir.dt.uint16
+U8 = mybir.dt.uint8
+FP8X4 = mybir.dt.float8_e4m3fn_x4
+ACT = mybir.ActivationFunctionType
+ALU = mybir.AluOpType
+
+P = 128
+PACK = 4
+WINDOW = 2 * S
+BLOCK = 128
+
+
+def tile_picked_ljpot_none_p_kernel(tc, x_words, x_scales, w1, q, gn, w2, offs, p1, p2, out):
+    nc = tc.nc
+    with ExitStack() as ctx:
+        keep = ctx.enter_context(tc.tile_pool(name="keep", bufs=1))
+        work = ctx.enter_context(tc.tile_pool(name="work", bufs=3))
+        psum = ctx.enter_context(tc.psum_pool(name="psum", bufs=1))
+
+        w1_rows = w1.rearrange("(p j) c -> p j c", j=PACK)
+
+        def load_w1(half):
+            raw = keep.tile([P, PACK, H // 2], F32, name=f"stage{half}")
+            nc.sync.dma_start(raw[:], w1_rows[:, :, half * (H // 2) : (half + 1) * (H // 2)])
+            return raw
+
+        def load_list(name, lst):
+            sb = keep.tile([P, S // 16], U16, name=name)
+            nc.sync.dma_start(sb[:], lst)
+            return sb
+
+        w1_raw = [load_w1(0)]
+        xs = keep.tile([P, T], U8, name="xs")
+        nc.gpsimd.memset(xs[:].bitcast(I32), 0)
+        for quad in range(4):
+            nc.sync.dma_start(xs[32 * quad : 32 * quad + 4, :].bitcast(I32), x_scales[0, 4 * quad : 4 * quad + 4, :].bitcast(I32))
+        offs_sb = load_list("offs_sb", offs)
+        w1_raw.append(load_w1(1))
+        xw = keep.tile([P, T], I32, name="stage2")
+        nc.sync.dma_start(xw[:], x_words[0].rearrange("p n t -> p (n t)").bitcast(I32))
+        partners = [load_list("p1_sb", p1), load_list("p2_sb", p2)]
+        gn_sb = keep.tile([P, PACK], F32, name="gn_sb")
+        nc.sync.dma_start(gn_sb[:], gn.rearrange("(p t) o -> p (t o)", t=PACK))
+
+        warm_in = keep.tile([P, 1], F32, name="warm_in")
+        warm_out = keep.tile([P, 1], F32, name="warm_out")
+        nc.vector.memset(warm_in[:], 1.0)
+        nc.scalar.activation(warm_out[:], warm_in[:], ACT.Abs_reciprocal_sqrt)
+
+        windows = [keep.tile([P, WINDOW], F32, name=f"window{t}") for t in range(PACK)]
+        for t in range(PACK):
+            nc.gpsimd.memset(windows[t][:, S:], 0.0)
+
+        w1_bf = keep.tile([P, PACK, P, PACK], BF16, name="w1_bf", align_bytes=64)
+        for half, copy in enumerate((nc.scalar.copy, nc.vector.tensor_copy)):
+            copy(
+                w1_bf[:, :, half * (P // 2) : (half + 1) * (P // 2), :].rearrange("p t m j -> p m j t"),
+                w1_raw[half][:].rearrange("p j (m t) -> p m j t", t=PACK),
+            )
+        xg_s = keep.tile([P, S], U8, name="xg_s", align_bytes=64)
+        nc.vector.tensor_copy(xg_s[:], xs[:].indirect(offs_sb[:]))
+        w1_codes = keep.tile([P, H], U32, name="w1_codes", align_bytes=64)
+        w1_scale = keep.tile([P, H], U8, name="w1_scale", align_bytes=64)
+        nc.vector.quantize_mx(w1_codes[:].bitcast(FP8X4), w1_scale[:], w1_bf[:].rearrange("p t m j -> p (t m j)"))
+        xg_w = keep.tile([P, S], U32, name="xg_w", align_bytes=64)
+        for half in range(2):
+            nc.vector.tensor_copy(
+                xg_w[:, half * (S // 2) : (half + 1) * (S // 2)],
+                xw[:].bitcast(U32).indirect(offs_sb[:, half * (S // 32) : (half + 1) * (S // 32)]),
+            )
+
+        q_rows = q.rearrange("(p t) s -> p t s", t=PACK)
+        q_sb = []
+        for half in range(2):
+            qh = keep.tile([P, 2, S], F32, name=f"stage{half}")
+            nc.sync.dma_start(qh[:], q_rows[:, 2 * half : 2 * half + 2, :])
+            q_sb.extend([qh[:, 0, :], qh[:, 1, :]])
+        w2_raw = keep.tile([P, PACK, N], F32, name="stage2")
+        nc.sync.dma_start(w2_raw[:], w2.rearrange("(p j) m -> p j m", j=PACK))
+
+        y_sb = []
+        bank = 0
+        for t in range(PACK):
+            plain = keep.tile([P, S], F32, name=f"y_sb{t}")
+            feats = slice(t * P, (t + 1) * P)
+            width = S // 2 if t == 0 else S
+            for c0 in range(0, S, width):
+                cols = slice(c0, c0 + width)
+                acc = psum.tile([P, width], F32, name=f"bank{bank}")
+                bank += 1
+                nc.tensor.matmul_mx(acc[:], w1_codes[:, feats].bitcast(FP8X4), w1_scale[:, feats], xg_w[:, cols].bitcast(FP8X4), xg_s[:, cols], start=True, stop=True)
+                nc.scalar.copy(windows[t][:, cols], acc[:])
+                nc.scalar.copy(plain[:, cols], acc[:])
+            y_sb.append(plain)
+
+        pairs = [(t, i) for t in range(PACK) for i in range(2)]
+        d = {}
+        r = {}
+        for t, i in pairs:
+            d[t, i] = keep.tile([P, S], F32, name=f"d{t}{i}")
+            nc.vector.tensor_tensor(d[t, i][:], windows[t][:].indirect(partners[i][:]), y_sb[t][:], ALU.subtract)
+        for t in range(PACK):
+            e = [work.tile([P, S], F32, name="e") for i in range(2)]
+            w = [work.tile([P, S], F32, name="w") for i in range(2)]
+            for i in range(2):
+                nc.scalar.activation(e[i][:], d[t, i][:], ACT.Square)
+            for i in range(2):
+                nc.scalar.activation(w[i][:], e[i][:], ACT.Abs_reciprocal_sqrt, bias=1.0)
+            for i in range(2):
+                r[t, i] = keep.tile([P, S], F32, name=f"r{t}{i}")
+                nc.scalar.activation(r[t, i][:], w[i][:], ACT.Square)
+
+        w2_bf = keep.tile([P, N, PACK], BF16, name="w2_bf", align_bytes=64)
+        nc.scalar.copy(
+            w2_bf[:].rearrange("p (c i) j -> p c j i", i=4),
+            w2_raw[:].rearrange("p j (c i) -> p c j i", i=4),
+        )
+
+        terms = [keep.tile([P, PACK, S], F32, name=f"terms{i}") for i in range(2)]
+        for t in range(PACK):
+            s = [work.tile([P, S], F32, name="s") for i in range(2)]
+            a = [work.tile([P, S], F32, name="a") for i in range(2)]
+            for i in range(2):
+                nc.vector.tensor_tensor(s[i][:], r[t, i][:], q_sb[t], ALU.mult)
+            for i in range(2):
+                nc.vector.scalar_tensor_tensor(a[i][:], s[i][:], 1.0, s[i][:], ALU.subtract, ALU.mult)
+            for i in range(2):
+                nc.vector.scalar_tensor_tensor(terms[i][:, t, :], a[i][:], gn_sb[:, t : t + 1], d[t, i][:], ALU.mult, ALU.mult)
+
+        w2_codes = keep.tile([P, N], U32, name="w2_codes", align_bytes=64)
+        w2_scale = keep.tile([P, N], U8, name="w2_scale", align_bytes=64)
+        nc.vector.quantize_mx(w2_codes[:].bitcast(FP8X4), w2_scale[:], w2_bf[:].rearrange("p m j -> p (m j)"))
+
+        out_rows = out.rearrange("(mt p) j -> p mt j", p=P)
+        blocks = S // BLOCK
+
+        def add_terms(b):
+            cols = slice(b * BLOCK, (b + 1) * BLOCK)
+            zb = keep.tile([P, BLOCK, PACK], BF16, name=f"z_bf{b}", align_bytes=64)
+            nc.vector.tensor_tensor(
+                zb[:].rearrange("p (c i) t -> p c t i", i=4),
+                terms[0][:, :, cols].rearrange("p t (c i) -> p c t i", i=4),
+                terms[1][:, :, cols].rearrange("p t (c i) -> p c t i", i=4),
+                ALU.add,
+            )
+            return zb
+
+        def project(b, zb):
+            cols = slice(b * BLOCK, (b + 1) * BLOCK)
+            z_codes = keep.tile([P, BLOCK], U32, name=f"z_codes{b}", align_bytes=64)
+            z_scale = keep.tile([P, BLOCK], U8, name=f"z_scale{b}", align_bytes=64)
+            nc.vector.quantize_mx(z_codes[:].bitcast(FP8X4), z_scale[:], zb[:].rearrange("p c t -> p (c t)"))
+            res = keep.tile([P, N // P, BLOCK], F32, name=f"res{b}")
+            for half in range(2):
+                acc = psum.tile([P, 2, BLOCK], F32, name=f"bank{2 * b + half}")
+                for u in range(2):
+                    rows = slice((2 * half + u) * P, (2 * half + u + 1) * P)
+                    nc.tensor.matmul_mx(acc[:, u, :], w2_codes[:, rows].bitcast(FP8X4), w2_scale[:, rows], z_codes[:].bitcast(FP8X4), z_scale[:], start=True, stop=True)
+                copy = nc.vector.tensor_copy if (b == blocks - 1 and half == 1) else nc.scalar.copy
+                copy(res[:, 2 * half : 2 * half + 2, :], acc[:])
+            nc.sync.dma_start(out_rows[:, :, cols], res[:])
+
+        summed = add_terms(0)
+        for b in range(blocks):
+            ahead = add_terms(b + 1) if b + 1 < blocks else None
+            project(b, summed)
+            summed = ahead

@@ -1,6 +1,7 @@
 from contextlib import ExitStack
 
 import concourse.mybir as mybir
+from concourse.masks import make_identity
 
 K, T, S, N, H = 512, 2048, 512, 512, 512
 FLOPS = 2 * K * H * S + 2 * H * N * S
@@ -17,8 +18,7 @@ ALU = mybir.AluOpType
 
 P = 128
 PACK = 4
-WINDOW = 2 * S
-BLOCK = 128
+HALF = S // 2
 
 
 def tile_picked_ljpot_none_p_kernel(tc, x_words, x_scales, w1, q, gn, w2, offs, p1, p2, out):
@@ -58,15 +58,16 @@ def tile_picked_ljpot_none_p_kernel(tc, x_words, x_scales, w1, q, gn, w2, offs, 
         nc.vector.memset(warm_in[:], 1.0)
         nc.scalar.activation(warm_out[:], warm_in[:], ACT.Abs_reciprocal_sqrt)
 
-        windows = [keep.tile([P, WINDOW], F32, name=f"window{t}") for t in range(PACK)]
-        for t in range(PACK):
-            nc.gpsimd.memset(windows[t][:, S:], 0.0)
+        ident = keep.tile([P, P], F32, name="ident")
+        make_identity(nc, ident[:])
+        windows = [keep.tile([P, S], F32, name=f"window{t}") for t in range(PACK)]
 
         w1_bf = keep.tile([P, PACK, P, PACK], BF16, name="w1_bf", align_bytes=64)
-        for half, copy in enumerate((nc.scalar.copy, nc.vector.tensor_copy)):
+        for m0, m1, copy in ((0, 64, nc.scalar.copy), (64, 96, nc.scalar.copy), (96, 128, nc.vector.tensor_copy)):
+            half, base = divmod(m0, P // 2)
             copy(
-                w1_bf[:, :, half * (P // 2) : (half + 1) * (P // 2), :].rearrange("p t m j -> p m j t"),
-                w1_raw[half][:].rearrange("p j (m t) -> p m j t", t=PACK),
+                w1_bf[:, :, m0:m1, :].rearrange("p t m j -> p m j t"),
+                w1_raw[half][:].rearrange("p j (m t) -> p m j t", t=PACK)[:, base : base + m1 - m0],
             )
         xg_s = keep.tile([P, S], U8, name="xg_s", align_bytes=64)
         nc.vector.tensor_copy(xg_s[:], xs[:].indirect(offs_sb[:]))
@@ -101,25 +102,34 @@ def tile_picked_ljpot_none_p_kernel(tc, x_words, x_scales, w1, q, gn, w2, offs, 
                 bank += 1
                 nc.tensor.matmul_mx(acc[:], w1_codes[:, feats].bitcast(FP8X4), w1_scale[:, feats], xg_w[:, cols].bitcast(FP8X4), xg_s[:, cols], start=True, stop=True)
                 nc.scalar.copy(windows[t][:, cols], acc[:])
-                nc.scalar.copy(plain[:, cols], acc[:])
+                second = nc.vector.tensor_copy if (t, c0) == (0, 0) else nc.scalar.copy
+                second(plain[:, cols], acc[:])
             y_sb.append(plain)
 
-        pairs = [(t, i) for t in range(PACK) for i in range(2)]
-        d = {}
-        r = {}
-        for t, i in pairs:
-            d[t, i] = keep.tile([P, S], F32, name=f"d{t}{i}")
-            nc.vector.tensor_tensor(d[t, i][:], windows[t][:].indirect(partners[i][:]), y_sb[t][:], ALU.subtract)
-        for t in range(PACK):
-            e = [work.tile([P, S], F32, name="e") for i in range(2)]
-            w = [work.tile([P, S], F32, name="w") for i in range(2)]
-            for i in range(2):
-                nc.scalar.activation(e[i][:], d[t, i][:], ACT.Square)
-            for i in range(2):
-                nc.scalar.activation(w[i][:], e[i][:], ACT.Abs_reciprocal_sqrt, bias=1.0)
-            for i in range(2):
-                r[t, i] = keep.tile([P, S], F32, name=f"r{t}{i}")
-                nc.scalar.activation(r[t, i][:], w[i][:], ACT.Square)
+        left, right = slice(0, HALF), slice(HALF, S)
+        units = [(cols, tiles) for cols in (left, right) for tiles in ((0, 1), (2, 3))]
+        d, r = {}, {}
+        for cols, tiles in units:
+            for t in tiles:
+                d[cols.start, t] = keep.tile([P, 2, HALF], F32, name=f"d{cols.start}_{t}")
+                for i in range(2):
+                    nc.vector.tensor_tensor(
+                        d[cols.start, t][:, i, :],
+                        windows[t][:].indirect(partners[i][:, cols.start // 16 : cols.stop // 16]),
+                        y_sb[t][:, cols],
+                        ALU.subtract,
+                    )
+        for cols, tiles in units:
+            e = {t: work.tile([P, 2, HALF], F32, name="e") for t in tiles}
+            w = work.tile([P, 2, 2, HALF], F32, name="w")
+            both = keep.tile([P, 2, 2, HALF], F32, name=f"r{cols.start}_{tiles[0]}")
+            for t in tiles:
+                nc.scalar.activation(e[t][:], d[cols.start, t][:], ACT.Square)
+            for u, t in enumerate(tiles):
+                nc.scalar.activation(w[:, u], e[t][:], ACT.Abs_reciprocal_sqrt, bias=1.0)
+            nc.scalar.activation(both[:], w[:], ACT.Square)
+            for u, t in enumerate(tiles):
+                r[cols.start, t] = both[:, u]
 
         w2_bf = keep.tile([P, N, PACK], BF16, name="w2_bf", align_bytes=64)
         nc.scalar.copy(
@@ -127,52 +137,91 @@ def tile_picked_ljpot_none_p_kernel(tc, x_words, x_scales, w1, q, gn, w2, offs, 
             w2_raw[:].rearrange("p j (c i) -> p c j i", i=4),
         )
 
-        terms = [keep.tile([P, PACK, S], F32, name=f"terms{i}") for i in range(2)]
-        for t in range(PACK):
-            s = [work.tile([P, S], F32, name="s") for i in range(2)]
-            a = [work.tile([P, S], F32, name="a") for i in range(2)]
-            for i in range(2):
-                nc.vector.tensor_tensor(s[i][:], r[t, i][:], q_sb[t], ALU.mult)
-            for i in range(2):
-                nc.vector.scalar_tensor_tensor(a[i][:], s[i][:], 1.0, s[i][:], ALU.subtract, ALU.mult)
-            for i in range(2):
-                nc.vector.scalar_tensor_tensor(terms[i][:, t, :], a[i][:], gn_sb[:, t : t + 1], d[t, i][:], ALU.mult, ALU.mult)
+        terms = keep.tile([P, PACK, 2, S], F32, name="terms")
+
+        def pair_terms(tiles, cols, last_step=True):
+            width = cols.stop - cols.start
+            s = {t: work.tile([P, 2, width], F32, name="s") for t in tiles}
+            a = {t: work.tile([P, 2, width], F32, name="a") for t in tiles}
+            for t in tiles:
+                nc.vector.tensor_tensor(s[t][:], r[cols.start, t], q_sb[t][:, cols].unsqueeze(1).to_broadcast([P, 2, width]), ALU.mult)
+            for t in tiles:
+                nc.vector.scalar_tensor_tensor(a[t][:], s[t][:], 1.0, s[t][:], ALU.subtract, ALU.mult)
+            if last_step:
+                weigh(tiles, cols, a, slice(0, width))
+            return a
+
+        def weigh(tiles, cols, a, part):
+            for t in tiles:
+                nc.vector.scalar_tensor_tensor(
+                    terms[:, t, :, cols.start + part.start : cols.start + part.stop],
+                    a[t][:, :, part], gn_sb[:, t : t + 1], d[cols.start, t][:, :, part], ALU.mult, ALU.mult,
+                )
 
         w2_codes = keep.tile([P, N], U32, name="w2_codes", align_bytes=64)
         w2_scale = keep.tile([P, N], U8, name="w2_scale", align_bytes=64)
-        nc.vector.quantize_mx(w2_codes[:].bitcast(FP8X4), w2_scale[:], w2_bf[:].rearrange("p m j -> p (m j)"))
-
         out_rows = out.rearrange("(mt p) j -> p mt j", p=P)
-        blocks = S // BLOCK
 
-        def add_terms(b):
-            cols = slice(b * BLOCK, (b + 1) * BLOCK)
-            zb = keep.tile([P, BLOCK, PACK], BF16, name=f"z_bf{b}", align_bytes=64)
+        def add_terms(cols):
+            width = cols.stop - cols.start
+            zb = keep.tile([P, width, PACK], BF16, name=f"z_bf{cols.start}", align_bytes=64)
             nc.vector.tensor_tensor(
                 zb[:].rearrange("p (c i) t -> p c t i", i=4),
-                terms[0][:, :, cols].rearrange("p t (c i) -> p c t i", i=4),
-                terms[1][:, :, cols].rearrange("p t (c i) -> p c t i", i=4),
+                terms[:, :, 0, cols].rearrange("p t (c i) -> p c t i", i=4),
+                terms[:, :, 1, cols].rearrange("p t (c i) -> p c t i", i=4),
                 ALU.add,
             )
             return zb
 
-        def project(b, zb):
-            cols = slice(b * BLOCK, (b + 1) * BLOCK)
-            z_codes = keep.tile([P, BLOCK], U32, name=f"z_codes{b}", align_bytes=64)
-            z_scale = keep.tile([P, BLOCK], U8, name=f"z_scale{b}", align_bytes=64)
+        def add_terms_on_tensor(cols):
+            blocks = (cols.stop - cols.start) // P
+            zb = keep.tile([P, blocks * P, PACK], BF16, name=f"z_bf{cols.start}", align_bytes=64)
+            back = psum.tile([P, blocks, 2, P], F32, name="bank5")
+            for b in range(blocks):
+                block = slice(cols.start + b * P, cols.start + (b + 1) * P)
+                turned = psum.tile([P, PACK, P], F32, name=f"bank{6 + b}")
+                for t in range(PACK):
+                    for i in range(2):
+                        nc.tensor.matmul(turned[:, t, :], terms[:, t, i, block], ident[:], start=(i == 0), stop=(i == 1), is_transpose=True)
+                rounded = keep.tile([P, P, PACK], BF16, name=f"rounded{b}")
+                nc.scalar.copy(rounded[:], turned[:].rearrange("j t p -> j p t"))
+                words = rounded[:].rearrange("j p t -> j (p t)").bitcast(F32)
+                for u in range(2):
+                    nc.tensor.transpose(back[:, b, u, :], words[:, u : 2 * P : 2], ident[:])
+            nc.scalar.copy(
+                zb[:].rearrange("p c t -> p (c t)").bitcast(F32).rearrange("p (b j u) -> p b j u", b=blocks, u=2),
+                back[:].rearrange("p b u j -> p b j u"),
+            )
+            return zb
+
+        def project(cols, zb, first_bank):
+            width = cols.stop - cols.start
+            last = cols.stop == S
+            z_codes = keep.tile([P, width], U32, name=f"z_codes{cols.start}", align_bytes=64)
+            z_scale = keep.tile([P, width], U8, name=f"z_scale{cols.start}", align_bytes=64)
             nc.vector.quantize_mx(z_codes[:].bitcast(FP8X4), z_scale[:], zb[:].rearrange("p c t -> p (c t)"))
-            res = keep.tile([P, N // P, BLOCK], F32, name=f"res{b}")
             for half in range(2):
-                acc = psum.tile([P, 2, BLOCK], F32, name=f"bank{2 * b + half}")
+                acc = psum.tile([P, 2, width], F32, name=f"bank{first_bank + half}")
+                res = keep.tile([P, 2, width], F32, name=f"res{first_bank + half}")
                 for u in range(2):
                     rows = slice((2 * half + u) * P, (2 * half + u + 1) * P)
                     nc.tensor.matmul_mx(acc[:, u, :], w2_codes[:, rows].bitcast(FP8X4), w2_scale[:, rows], z_codes[:].bitcast(FP8X4), z_scale[:], start=True, stop=True)
-                copy = nc.vector.tensor_copy if (b == blocks - 1 and half == 1) else nc.scalar.copy
-                copy(res[:, 2 * half : 2 * half + 2, :], acc[:])
-            nc.sync.dma_start(out_rows[:, :, cols], res[:])
+                copy = nc.vector.tensor_copy if (last and half == 1) else nc.scalar.copy
+                copy(res[:], acc[:])
+                queue = nc.scalar if (last and half == 0) else nc.sync
+                queue.dma_start(out_rows[:, 2 * half : 2 * half + 2, cols], res[:])
 
-        summed = add_terms(0)
-        for b in range(blocks):
-            ahead = add_terms(b + 1) if b + 1 < blocks else None
-            project(b, summed)
-            summed = ahead
+        third, fourth = slice(S // 2, 3 * S // 4), slice(3 * S // 4, S)
+        pair_terms((0, 1), left)
+        pair_terms((2, 3), left)
+        z_left = add_terms_on_tensor(left)
+        pair_terms((0, 1), right)
+        nc.vector.quantize_mx(w2_codes[:].bitcast(FP8X4), w2_scale[:], w2_bf[:].rearrange("p m j -> p (m j)"))
+        project(left, z_left, 0)
+        a = pair_terms((2, 3), right, last_step=False)
+        weigh((2, 3), right, a, slice(0, P))
+        z_third = add_terms(third)
+        weigh((2, 3), right, a, slice(P, 2 * P))
+        project(third, z_third, 2)
+        z_fourth = add_terms(fourth)
+        project(fourth, z_fourth, 4)

@@ -18,11 +18,16 @@ ALU = mybir.AluOpType
 
 P = 128
 PACK = 4
+GROUP = 16
+QUADRANT = 32
+LINE = 4
+PARTNERS = 2
 HALF = S // 2
 
 
 def tile_picked_ljpot_none_p_kernel(tc, x_words, x_scales, w1, q, gn, w2, offs, p1, p2, out):
     nc = tc.nc
+    left, right = slice(0, HALF), slice(HALF, S)
     with ExitStack() as ctx:
         keep = ctx.enter_context(tc.tile_pool(name="keep", bufs=1))
         work = ctx.enter_context(tc.tile_pool(name="work", bufs=3))
@@ -35,193 +40,209 @@ def tile_picked_ljpot_none_p_kernel(tc, x_words, x_scales, w1, q, gn, w2, offs, 
             nc.sync.dma_start(raw[:], w1_rows[:, :, half * (H // 2) : (half + 1) * (H // 2)])
             return raw
 
-        def load_list(name, lst):
-            sb = keep.tile([P, S // 16], U16, name=name)
-            nc.sync.dma_start(sb[:], lst)
-            return sb
+        def load_list(name, source):
+            offsets = keep.tile([P, S // GROUP], U16, name=name)
+            nc.sync.dma_start(offsets[:], source)
+            return offsets
 
         w1_raw = [load_w1(0)]
-        xs = keep.tile([P, T], U8, name="xs")
-        nc.gpsimd.memset(xs[:].bitcast(I32), 0)
-        for quad in range(4):
-            nc.sync.dma_start(xs[32 * quad : 32 * quad + 4, :].bitcast(I32), x_scales[0, 4 * quad : 4 * quad + 4, :].bitcast(I32))
-        offs_sb = load_list("offs_sb", offs)
+        x_scale_table = keep.tile([P, T], U8, name="x_scale_table")
+        nc.gpsimd.memset(x_scale_table[:].bitcast(I32), 0)
+        for quad in range(P // QUADRANT):
+            nc.sync.dma_start(
+                x_scale_table[QUADRANT * quad : QUADRANT * quad + 4, :].bitcast(I32),
+                x_scales[0, 4 * quad : 4 * quad + 4, :].bitcast(I32),
+            )
+        picks = load_list("picks", offs)
         w1_raw.append(load_w1(1))
-        xw = keep.tile([P, T], I32, name="stage2")
-        nc.sync.dma_start(xw[:], x_words[0].rearrange("p n t -> p (n t)").bitcast(I32))
-        partners = [load_list("p1_sb", p1), load_list("p2_sb", p2)]
-        gn_sb = keep.tile([P, PACK], F32, name="gn_sb")
-        nc.sync.dma_start(gn_sb[:], gn.rearrange("(p t) o -> p (t o)", t=PACK))
+        x_word_table = keep.tile([P, T], I32, name="stage2")
+        nc.sync.dma_start(x_word_table[:], x_words[0].rearrange("p n t -> p (n t)").bitcast(I32))
+        partners = [load_list("partner0", p1), load_list("partner1", p2)]
+        gain = keep.tile([P, PACK], F32, name="gain")
+        nc.sync.dma_start(gain[:], gn.rearrange("(p t) o -> p (t o)", t=PACK))
 
-        warm_in = keep.tile([P, 1], F32, name="warm_in")
-        warm_out = keep.tile([P, 1], F32, name="warm_out")
-        nc.vector.memset(warm_in[:], 1.0)
-        nc.scalar.activation(warm_out[:], warm_in[:], ACT.Abs_reciprocal_sqrt)
+        seed = keep.tile([P, 1], F32, name="seed")
+        root = keep.tile([P, 1], F32, name="root")
+        one = keep.tile([P, 1], F32, name="one")
+        nc.vector.memset(seed[:], 1.0)
+        nc.scalar.activation(root[:], seed[:], ACT.Abs_reciprocal_sqrt)
+        nc.scalar.activation(one[:], root[:], ACT.Sign)
 
         ident = keep.tile([P, P], F32, name="ident")
         make_identity(nc, ident[:])
-        windows = [keep.tile([P, S], F32, name=f"window{t}") for t in range(PACK)]
+
+        windows = [keep.tile([P, S if t == 0 else 2 * S], F32, name=f"window{t}") for t in range(PACK)]
+        last_plain = keep.tile([P, S], F32, name="last_plain")
+        y_plain = [windows[t + 1][:, S:] for t in range(PACK - 1)] + [last_plain[:]]
 
         w1_bf = keep.tile([P, PACK, P, PACK], BF16, name="w1_bf", align_bytes=64)
-        for m0, m1, copy in ((0, 64, nc.scalar.copy), (64, 96, nc.scalar.copy), (96, 128, nc.vector.tensor_copy)):
+        quarter = P // 4
+        for m0, m1, cast in (
+            (0, 2 * quarter, nc.scalar.copy),
+            (2 * quarter, 3 * quarter, nc.scalar.copy),
+            (3 * quarter, P, nc.vector.tensor_copy),
+        ):
             half, base = divmod(m0, P // 2)
-            copy(
+            cast(
                 w1_bf[:, :, m0:m1, :].rearrange("p t m j -> p m j t"),
                 w1_raw[half][:].rearrange("p j (m t) -> p m j t", t=PACK)[:, base : base + m1 - m0],
             )
-        xg_s = keep.tile([P, S], U8, name="xg_s", align_bytes=64)
-        nc.vector.tensor_copy(xg_s[:], xs[:].indirect(offs_sb[:]))
+        x_scale = keep.tile([P, S], U8, name="x_scale", align_bytes=64)
+        nc.vector.tensor_copy(x_scale[:], x_scale_table[:].indirect(picks[:]))
         w1_codes = keep.tile([P, H], U32, name="w1_codes", align_bytes=64)
         w1_scale = keep.tile([P, H], U8, name="w1_scale", align_bytes=64)
         nc.vector.quantize_mx(w1_codes[:].bitcast(FP8X4), w1_scale[:], w1_bf[:].rearrange("p t m j -> p (t m j)"))
-        xg_w = keep.tile([P, S], U32, name="xg_w", align_bytes=64)
-        for half in range(2):
+        x_codes = keep.tile([P, S], U32, name="x_codes", align_bytes=64)
+        for cols in (left, right):
             nc.vector.tensor_copy(
-                xg_w[:, half * (S // 2) : (half + 1) * (S // 2)],
-                xw[:].bitcast(U32).indirect(offs_sb[:, half * (S // 32) : (half + 1) * (S // 32)]),
+                x_codes[:, cols],
+                x_word_table[:].bitcast(U32).indirect(picks[:, cols.start // GROUP : cols.stop // GROUP]),
             )
 
         q_rows = q.rearrange("(p t) s -> p t s", t=PACK)
-        q_sb = []
+        strength = []
         for half in range(2):
-            qh = keep.tile([P, 2, S], F32, name=f"stage{half}")
-            nc.sync.dma_start(qh[:], q_rows[:, 2 * half : 2 * half + 2, :])
-            q_sb.extend([qh[:, 0, :], qh[:, 1, :]])
+            two_tiles = keep.tile([P, 2, S], F32, name=f"stage{half}")
+            nc.sync.dma_start(two_tiles[:], q_rows[:, 2 * half : 2 * half + 2, :])
+            strength.extend([two_tiles[:, 0, :], two_tiles[:, 1, :]])
         w2_raw = keep.tile([P, PACK, N], F32, name="stage2")
         nc.sync.dma_start(w2_raw[:], w2.rearrange("(p j) m -> p j m", j=PACK))
 
-        y_sb = []
         bank = 0
         for t in range(PACK):
-            plain = keep.tile([P, S], F32, name=f"y_sb{t}")
             feats = slice(t * P, (t + 1) * P)
-            width = S // 2 if t == 0 else S
-            for c0 in range(0, S, width):
-                cols = slice(c0, c0 + width)
-                acc = psum.tile([P, width], F32, name=f"bank{bank}")
+            for cols in (left, right) if t == 0 else (slice(0, S),):
+                y_acc = psum.tile([P, cols.stop - cols.start], F32, name=f"bank{bank}")
                 bank += 1
-                nc.tensor.matmul_mx(acc[:], w1_codes[:, feats].bitcast(FP8X4), w1_scale[:, feats], xg_w[:, cols].bitcast(FP8X4), xg_s[:, cols], start=True, stop=True)
-                nc.scalar.copy(windows[t][:, cols], acc[:])
-                second = nc.vector.tensor_copy if (t, c0) == (0, 0) else nc.scalar.copy
-                second(plain[:, cols], acc[:])
-            y_sb.append(plain)
+                nc.tensor.matmul_mx(
+                    y_acc[:], w1_codes[:, feats].bitcast(FP8X4), w1_scale[:, feats],
+                    x_codes[:, cols].bitcast(FP8X4), x_scale[:, cols], start=True, stop=True,
+                )
+                nc.scalar.copy(windows[t][:, cols], y_acc[:])
+                second_copy = nc.vector.tensor_copy if t == 0 and cols == left else nc.scalar.copy
+                second_copy(y_plain[t][:, cols], y_acc[:])
 
-        left, right = slice(0, HALF), slice(HALF, S)
-        units = [(cols, tiles) for cols in (left, right) for tiles in ((0, 1), (2, 3))]
-        d, r = {}, {}
-        for cols, tiles in units:
-            for t in tiles:
-                d[cols.start, t] = keep.tile([P, 2, HALF], F32, name=f"d{cols.start}_{t}")
-                for i in range(2):
+        d = [keep.tile([P, PARTNERS, S], F32, name=f"d{t}") for t in range(PACK)]
+        for t in range(PACK):
+            for cols in (left, right) if t == 0 else (slice(0, S),):
+                for i in range(PARTNERS):
                     nc.vector.tensor_tensor(
-                        d[cols.start, t][:, i, :],
-                        windows[t][:].indirect(partners[i][:, cols.start // 16 : cols.stop // 16]),
-                        y_sb[t][:, cols],
+                        d[t][:, i, cols],
+                        windows[t][:].indirect(partners[i][:, cols.start // GROUP : cols.stop // GROUP]),
+                        y_plain[t][:, cols],
                         ALU.subtract,
                     )
-        for cols, tiles in units:
-            e = {t: work.tile([P, 2, HALF], F32, name="e") for t in tiles}
-            w = work.tile([P, 2, 2, HALF], F32, name="w")
-            both = keep.tile([P, 2, 2, HALF], F32, name=f"r{cols.start}_{tiles[0]}")
-            for t in tiles:
-                nc.scalar.activation(e[t][:], d[cols.start, t][:], ACT.Square)
-            for u, t in enumerate(tiles):
-                nc.scalar.activation(w[:, u], e[t][:], ACT.Abs_reciprocal_sqrt, bias=1.0)
-            nc.scalar.activation(both[:], w[:], ACT.Square)
-            for u, t in enumerate(tiles):
-                r[cols.start, t] = both[:, u]
+
+        pieces = [(0, left), (0, right)] + [(t, cols) for cols in (left, right) for t in range(1, PACK)]
+        pairs = [pieces[n : n + 2] for n in range(0, len(pieces), 2)]
+
+        soft = []
+        for n, pair in enumerate(pairs):
+            squared = [work.tile([P, PARTNERS, HALF], F32, name="squared") for piece in pair]
+            inv_root = work.tile([P, 2, PARTNERS, HALF], F32, name="inv_root")
+            soft_pair = keep.tile([P, 2, PARTNERS, HALF], F32, name=f"soft{n}")
+            for u, (t, cols) in enumerate(pair):
+                nc.scalar.activation(squared[u][:], d[t][:, :, cols], ACT.Square)
+            for u in range(2):
+                nc.scalar.activation(inv_root[:, u], squared[u][:], ACT.Abs_reciprocal_sqrt, bias=one[:])
+            nc.scalar.activation(soft_pair[:], inv_root[:], ACT.Square)
+            soft.append(soft_pair)
 
         w2_bf = keep.tile([P, N, PACK], BF16, name="w2_bf", align_bytes=64)
         nc.scalar.copy(
-            w2_bf[:].rearrange("p (c i) j -> p c j i", i=4),
-            w2_raw[:].rearrange("p j (c i) -> p c j i", i=4),
+            w2_bf[:].rearrange("p (c i) j -> p c j i", i=LINE),
+            w2_raw[:].rearrange("p j (c i) -> p c j i", i=LINE),
         )
 
-        terms = keep.tile([P, PACK, 2, S], F32, name="terms")
+        terms = keep.tile([P, PACK, PARTNERS, S], F32, name="terms")
 
-        def pair_terms(tiles, cols, last_step=True):
-            width = cols.stop - cols.start
-            s = {t: work.tile([P, 2, width], F32, name="s") for t in tiles}
-            a = {t: work.tile([P, 2, width], F32, name="a") for t in tiles}
-            for t in tiles:
-                nc.vector.tensor_tensor(s[t][:], r[cols.start, t], q_sb[t][:, cols].unsqueeze(1).to_broadcast([P, 2, width]), ALU.mult)
-            for t in tiles:
-                nc.vector.scalar_tensor_tensor(a[t][:], s[t][:], 1.0, s[t][:], ALU.subtract, ALU.mult)
-            if last_step:
-                weigh(tiles, cols, a, slice(0, width))
-            return a
+        def force_factors(n):
+            s = [work.tile([P, PARTNERS, HALF], F32, name="s") for piece in pairs[n]]
+            factor = [work.tile([P, PARTNERS, HALF], F32, name="factor") for piece in pairs[n]]
+            for u, (t, cols) in enumerate(pairs[n]):
+                q_both = strength[t][:, cols].unsqueeze(1).to_broadcast([P, PARTNERS, HALF])
+                nc.vector.tensor_tensor(s[u][:], soft[n][:, u], q_both, ALU.mult)
+            for u in range(2):
+                nc.vector.scalar_tensor_tensor(factor[u][:], s[u][:], 1.0, s[u][:], ALU.subtract, ALU.mult)
+            return factor
 
-        def weigh(tiles, cols, a, part):
-            for t in tiles:
+        def make_terms(n, factor, part):
+            for u, (t, cols) in enumerate(pairs[n]):
+                where = slice(cols.start + part.start, cols.start + part.stop)
                 nc.vector.scalar_tensor_tensor(
-                    terms[:, t, :, cols.start + part.start : cols.start + part.stop],
-                    a[t][:, :, part], gn_sb[:, t : t + 1], d[cols.start, t][:, :, part], ALU.mult, ALU.mult,
+                    terms[:, t, :, where], factor[u][:, :, part], gain[:, t : t + 1], d[t][:, :, where], ALU.mult, ALU.mult
                 )
 
         w2_codes = keep.tile([P, N], U32, name="w2_codes", align_bytes=64)
         w2_scale = keep.tile([P, N], U8, name="w2_scale", align_bytes=64)
         out_rows = out.rearrange("(mt p) j -> p mt j", p=P)
 
-        def add_terms(cols):
-            width = cols.stop - cols.start
-            zb = keep.tile([P, width, PACK], BF16, name=f"z_bf{cols.start}", align_bytes=64)
+        def sum_on_vector(cols, name):
+            z_bf = keep.tile([P, cols.stop - cols.start, PACK], BF16, name=name, align_bytes=64)
             nc.vector.tensor_tensor(
-                zb[:].rearrange("p (c i) t -> p c t i", i=4),
-                terms[:, :, 0, cols].rearrange("p t (c i) -> p c t i", i=4),
-                terms[:, :, 1, cols].rearrange("p t (c i) -> p c t i", i=4),
+                z_bf[:].rearrange("p (c i) t -> p c t i", i=LINE),
+                terms[:, :, 0, cols].rearrange("p t (c i) -> p c t i", i=LINE),
+                terms[:, :, 1, cols].rearrange("p t (c i) -> p c t i", i=LINE),
                 ALU.add,
             )
-            return zb
+            return z_bf
 
-        def add_terms_on_tensor(cols):
+        def sum_on_tensor(cols, name):
             blocks = (cols.stop - cols.start) // P
-            zb = keep.tile([P, blocks * P, PACK], BF16, name=f"z_bf{cols.start}", align_bytes=64)
+            z_bf = keep.tile([P, blocks * P, PACK], BF16, name=name, align_bytes=64)
             back = psum.tile([P, blocks, 2, P], F32, name="bank5")
             for b in range(blocks):
                 block = slice(cols.start + b * P, cols.start + (b + 1) * P)
                 turned = psum.tile([P, PACK, P], F32, name=f"bank{6 + b}")
                 for t in range(PACK):
-                    for i in range(2):
-                        nc.tensor.matmul(turned[:, t, :], terms[:, t, i, block], ident[:], start=(i == 0), stop=(i == 1), is_transpose=True)
+                    for i in range(PARTNERS):
+                        nc.tensor.matmul(
+                            turned[:, t, :], terms[:, t, i, block], ident[:],
+                            start=(i == 0), stop=(i == PARTNERS - 1), is_transpose=True,
+                        )
                 rounded = keep.tile([P, P, PACK], BF16, name=f"rounded{b}")
                 nc.scalar.copy(rounded[:], turned[:].rearrange("j t p -> j p t"))
                 words = rounded[:].rearrange("j p t -> j (p t)").bitcast(F32)
                 for u in range(2):
                     nc.tensor.transpose(back[:, b, u, :], words[:, u : 2 * P : 2], ident[:])
             nc.scalar.copy(
-                zb[:].rearrange("p c t -> p (c t)").bitcast(F32).rearrange("p (b j u) -> p b j u", b=blocks, u=2),
+                z_bf[:].rearrange("p c t -> p (c t)").bitcast(F32).rearrange("p (b j u) -> p b j u", b=blocks, u=2),
                 back[:].rearrange("p b u j -> p b j u"),
             )
-            return zb
+            return z_bf
 
-        def project(cols, zb, first_bank):
+        def project(cols, z_bf, first_bank):
             width = cols.stop - cols.start
             last = cols.stop == S
             z_codes = keep.tile([P, width], U32, name=f"z_codes{cols.start}", align_bytes=64)
             z_scale = keep.tile([P, width], U8, name=f"z_scale{cols.start}", align_bytes=64)
-            nc.vector.quantize_mx(z_codes[:].bitcast(FP8X4), z_scale[:], zb[:].rearrange("p c t -> p (c t)"))
+            nc.vector.quantize_mx(z_codes[:].bitcast(FP8X4), z_scale[:], z_bf[:].rearrange("p c t -> p (c t)"))
             for half in range(2):
-                acc = psum.tile([P, 2, width], F32, name=f"bank{first_bank + half}")
-                res = keep.tile([P, 2, width], F32, name=f"res{first_bank + half}")
+                out_acc = psum.tile([P, 2, width], F32, name=f"bank{first_bank + half}")
+                result = keep.tile([P, 2, width], F32, name=f"result{first_bank + half}")
                 for u in range(2):
                     rows = slice((2 * half + u) * P, (2 * half + u + 1) * P)
-                    nc.tensor.matmul_mx(acc[:, u, :], w2_codes[:, rows].bitcast(FP8X4), w2_scale[:, rows], z_codes[:].bitcast(FP8X4), z_scale[:], start=True, stop=True)
-                copy = nc.vector.tensor_copy if (last and half == 1) else nc.scalar.copy
-                copy(res[:], acc[:])
-                queue = nc.scalar if (last and half == 0) else nc.sync
-                queue.dma_start(out_rows[:, 2 * half : 2 * half + 2, cols], res[:])
+                    nc.tensor.matmul_mx(
+                        out_acc[:, u, :], w2_codes[:, rows].bitcast(FP8X4), w2_scale[:, rows],
+                        z_codes[:].bitcast(FP8X4), z_scale[:], start=True, stop=True,
+                    )
+                copy_out = nc.vector.tensor_copy if last and half == 1 else nc.scalar.copy
+                copy_out(result[:], out_acc[:])
+                queue = nc.scalar if last and half == 0 else nc.sync
+                queue.dma_start(out_rows[:, 2 * half : 2 * half + 2, cols], result[:])
 
-        third, fourth = slice(S // 2, 3 * S // 4), slice(3 * S // 4, S)
-        pair_terms((0, 1), left)
-        pair_terms((2, 3), left)
-        z_left = add_terms_on_tensor(left)
-        pair_terms((0, 1), right)
+        last_pair = len(pairs) - 1
+        for n in range(last_pair):
+            make_terms(n, force_factors(n), slice(0, HALF))
+        z_left = sum_on_tensor(left, "z_bf")
         nc.vector.quantize_mx(w2_codes[:].bitcast(FP8X4), w2_scale[:], w2_bf[:].rearrange("p m j -> p (m j)"))
-        project(left, z_left, 0)
-        a = pair_terms((2, 3), right, last_step=False)
-        weigh((2, 3), right, a, slice(0, P))
-        z_third = add_terms(third)
-        weigh((2, 3), right, a, slice(P, 2 * P))
-        project(third, z_third, 2)
-        z_fourth = add_terms(fourth)
-        project(fourth, z_fourth, 4)
+        project(left, z_left, first_bank=0)
+
+        third, fourth = slice(HALF, HALF + P), slice(HALF + P, S)
+        factor = force_factors(last_pair)
+        make_terms(last_pair, factor, slice(0, P))
+        z_third = sum_on_vector(third, "z_bf")
+        make_terms(last_pair, factor, slice(P, HALF))
+        project(third, z_third, first_bank=2)
+        z_fourth = sum_on_vector(fourth, "z_bf_last")
+        project(fourth, z_fourth, first_bank=4)

@@ -30,7 +30,7 @@ def tile_picked_ljpot_none_p_kernel(tc, x_words, x_scales, w1, q, gn, w2, offs, 
     left, right = slice(0, HALF), slice(HALF, S)
     with ExitStack() as ctx:
         keep = ctx.enter_context(tc.tile_pool(name="keep", bufs=1))
-        work = ctx.enter_context(tc.tile_pool(name="work", bufs=3))
+        work = ctx.enter_context(tc.tile_pool(name="work", bufs=4))
         psum = ctx.enter_context(tc.psum_pool(name="psum", bufs=1))
 
         w1_rows = w1.rearrange("(p j) c -> p j c", j=PACK)
@@ -71,10 +71,6 @@ def tile_picked_ljpot_none_p_kernel(tc, x_words, x_scales, w1, q, gn, w2, offs, 
         ident = keep.tile([P, P], F32, name="ident")
         make_identity(nc, ident[:])
 
-        windows = [keep.tile([P, S if t == 0 else 2 * S], F32, name=f"window{t}") for t in range(PACK)]
-        last_plain = keep.tile([P, S], F32, name="last_plain")
-        y_plain = [windows[t + 1][:, S:] for t in range(PACK - 1)] + [last_plain[:]]
-
         w1_bf = keep.tile([P, PACK, P, PACK], BF16, name="w1_bf", align_bytes=64)
         quarter = P // 4
         for m0, m1, cast in (
@@ -107,119 +103,103 @@ def tile_picked_ljpot_none_p_kernel(tc, x_words, x_scales, w1, q, gn, w2, offs, 
             strength.extend([two_tiles[:, 0, :], two_tiles[:, 1, :]])
         w2_raw = keep.tile([P, PACK, N], F32, name="stage2")
         nc.sync.dma_start(w2_raw[:], w2.rearrange("(p j) m -> p j m", j=PACK))
+        minus_gain = keep.tile([P, PACK], F32, name="minus_gain")
+        nc.vector.tensor_scalar(minus_gain[:], gain[:], -1.0, None, ALU.mult)
 
+        y = [keep.tile([P, S], F32, name=f"y{t}") for t in range(PACK)]
+        y_banks = ["e3", "e4", "q0", "q1", "e5"]
         bank = 0
         for t in range(PACK):
             feats = slice(t * P, (t + 1) * P)
             for cols in (left, right) if t == 0 else (slice(0, S),):
-                y_acc = psum.tile([P, cols.stop - cols.start], F32, name=f"bank{bank}")
+                y_acc = psum.tile([P, cols.stop - cols.start], F32, name=y_banks[bank])
                 bank += 1
                 nc.tensor.matmul_mx(
                     y_acc[:], w1_codes[:, feats].bitcast(FP8X4), w1_scale[:, feats],
                     x_codes[:, cols].bitcast(FP8X4), x_scale[:, cols], start=True, stop=True,
                 )
-                nc.scalar.copy(windows[t][:, cols], y_acc[:])
-                second_copy = nc.vector.tensor_copy if t == 0 and cols == left else nc.scalar.copy
-                second_copy(y_plain[t][:, cols], y_acc[:])
+                copy_out = nc.vector.tensor_copy if t == 0 and cols == right else nc.scalar.copy
+                copy_out(y[t][:, cols], y_acc[:])
 
-        d = [keep.tile([P, PARTNERS, S], F32, name=f"d{t}") for t in range(PACK)]
+        minus_partner = [keep.tile([P, PARTNERS, S], F32, name=f"minus_partner{t}") for t in range(PACK)]
         for t in range(PACK):
-            for cols in (left, right) if t == 0 else (slice(0, S),):
+            for cols in (left, right):
                 for i in range(PARTNERS):
-                    nc.vector.tensor_tensor(
-                        d[t][:, i, cols],
-                        windows[t][:].indirect(partners[i][:, cols.start // GROUP : cols.stop // GROUP]),
-                        y_plain[t][:, cols],
-                        ALU.subtract,
-                    )
+                    looked_up = y[t][:].indirect(partners[i][:, cols.start // GROUP : cols.stop // GROUP])
+                    if cols == right and t == PACK - 1:
+                        nc.scalar.activation(minus_partner[t][:, i, cols], looked_up, ACT.Copy, scale=-1.0)
+                    else:
+                        nc.vector.tensor_scalar(minus_partner[t][:, i, cols], looked_up, -1.0, 0.0, ALU.mult, ALU.add)
 
-        pieces = [(0, left), (0, right)] + [(t, cols) for cols in (left, right) for t in range(1, PACK)]
+        pieces = [[(t, b), (t, b + 1)] for t in range(PACK) for b in (0, 2)]
         pairs = [pieces[n : n + 2] for n in range(0, len(pieces), 2)]
-
-        soft = []
-        for n, pair in enumerate(pairs):
-            squared = [work.tile([P, PARTNERS, HALF], F32, name="squared") for piece in pair]
-            inv_root = work.tile([P, 2, PARTNERS, HALF], F32, name="inv_root")
-            soft_pair = keep.tile([P, 2, PARTNERS, HALF], F32, name=f"soft{n}")
-            for u, (t, cols) in enumerate(pair):
-                nc.scalar.activation(squared[u][:], d[t][:, :, cols], ACT.Square)
-            for u in range(2):
-                nc.scalar.activation(inv_root[:, u], squared[u][:], ACT.Abs_reciprocal_sqrt, bias=one[:])
-            nc.scalar.activation(soft_pair[:], inv_root[:], ACT.Square)
-            soft.append(soft_pair)
-
-        w2_bf = keep.tile([P, N, PACK], BF16, name="w2_bf", align_bytes=64)
-        nc.scalar.copy(
-            w2_bf[:].rearrange("p (c i) j -> p c j i", i=LINE),
-            w2_raw[:].rearrange("p j (c i) -> p c j i", i=LINE),
-        )
-
-        terms = keep.tile([P, PACK, PARTNERS, S], F32, name="terms")
-
-        def force_factors(n):
-            s = [work.tile([P, PARTNERS, HALF], F32, name="s") for piece in pairs[n]]
-            factor = [work.tile([P, PARTNERS, HALF], F32, name="factor") for piece in pairs[n]]
-            for u, (t, cols) in enumerate(pairs[n]):
-                q_both = strength[t][:, cols].unsqueeze(1).to_broadcast([P, PARTNERS, HALF])
-                nc.vector.tensor_tensor(s[u][:], soft[n][:, u], q_both, ALU.mult)
-            for u in range(2):
-                nc.vector.scalar_tensor_tensor(factor[u][:], s[u][:], 1.0, s[u][:], ALU.subtract, ALU.mult)
-            return factor
-
-        def make_terms(n, factor, part):
-            for u, (t, cols) in enumerate(pairs[n]):
-                where = slice(cols.start + part.start, cols.start + part.stop)
-                nc.vector.scalar_tensor_tensor(
-                    terms[:, t, :, where], factor[u][:, :, part], gain[:, t : t + 1], d[t][:, :, where], ALU.mult, ALU.mult
-                )
-
-        w2_codes = keep.tile([P, N], U32, name="w2_codes", align_bytes=64)
-        w2_scale = keep.tile([P, N], U8, name="w2_scale", align_bytes=64)
         out_rows = out.rearrange("(mt p) j -> p mt j", p=P)
 
-        def sum_on_vector(cols, name):
-            z_bf = keep.tile([P, cols.stop - cols.start, PACK], BF16, name=name, align_bytes=64)
-            nc.vector.tensor_tensor(
-                z_bf[:].rearrange("p (c i) t -> p c t i", i=LINE),
-                terms[:, :, 0, cols].rearrange("p t (c i) -> p c t i", i=LINE),
-                terms[:, :, 1, cols].rearrange("p t (c i) -> p c t i", i=LINE),
-                ALU.add,
-            )
-            return z_bf
+        def block(b):
+            return slice(b * P, (b + 1) * P)
 
-        def sum_on_tensor(cols, name):
-            blocks = (cols.stop - cols.start) // P
-            z_bf = keep.tile([P, blocks * P, PACK], BF16, name=name, align_bytes=64)
-            back = psum.tile([P, blocks, 2, P], F32, name="bank5")
-            for b in range(blocks):
-                block = slice(cols.start + b * P, cols.start + (b + 1) * P)
-                turned = psum.tile([P, PACK, P], F32, name=f"bank{6 + b}")
-                for t in range(PACK):
+        terms = {}
+
+        def do_pair(n, pair):
+            minus_d = []
+            inv_root = keep.tile([P, 2, 4 * P], F32, name=f"inv_root{n}", align_bytes=64)
+            soft = keep.tile([P, 2, 2, PARTNERS, P], F32, name=f"soft{n}", align_bytes=64)
+            q_turned = psum.tile([P, 2, 2, P], F32, name=f"q{n % 2}")
+            for v, piece in enumerate(pair):
+                e = psum.tile([P, 2, PARTNERS, P], F32, name=f"e{(2 * n + v) % 6}")
+                for u, (t, b) in enumerate(piece):
                     for i in range(PARTNERS):
+                        nc.tensor.matmul(e[:, u, i, :], y[t][:, block(b)], ident[:], start=True, stop=False, is_transpose=True)
                         nc.tensor.matmul(
-                            turned[:, t, :], terms[:, t, i, block], ident[:],
-                            start=(i == 0), stop=(i == PARTNERS - 1), is_transpose=True,
+                            e[:, u, i, :], minus_partner[t][:, i, block(b)], ident[:], start=False, stop=True, is_transpose=True
                         )
-                rounded = keep.tile([P, P, PACK], BF16, name=f"rounded{b}")
-                nc.scalar.copy(rounded[:], turned[:].rearrange("j t p -> j p t"))
-                words = rounded[:].rearrange("j p t -> j (p t)").bitcast(F32)
-                for u in range(2):
-                    nc.tensor.transpose(back[:, b, u, :], words[:, u : 2 * P : 2], ident[:])
-            nc.scalar.copy(
-                z_bf[:].rearrange("p c t -> p (c t)").bitcast(F32).rearrange("p (b j u) -> p b j u", b=blocks, u=2),
-                back[:].rearrange("p b u j -> p b j u"),
-            )
-            return z_bf
+                minus_d.append(e)
+            for v, piece in enumerate(pair):
+                for u, (t, b) in enumerate(piece):
+                    nc.tensor.transpose(q_turned[:, v, u, :], strength[t][:, block(b)], ident[:])
+            squared = [work.tile([P, 4 * P], F32, name="squared") for v in range(2)]
+            for v in range(2):
+                nc.scalar.activation(squared[v][:], minus_d[v][:].rearrange("p u i f -> p (u i f)"), ACT.Square)
+            for v in range(2):
+                nc.scalar.activation(inv_root[:, v], squared[v][:], ACT.Abs_reciprocal_sqrt, bias=one[:])
+            nc.scalar.activation(soft[:].rearrange("p v u i f -> p v (u i f)"), inv_root[:], ACT.Square)
+            s = [keep.tile([P, 2, PARTNERS, P], F32, name=f"s{n}_{v}") for v in range(2)]
+            pull = [keep.tile([P, 2, PARTNERS, P], F32, name=f"pull{n}_{v}") for v in range(2)]
+            for v in range(2):
+                q_both = q_turned[:, v].unsqueeze(2).to_broadcast([P, 2, PARTNERS, P])
+                nc.vector.tensor_tensor(s[v][:], q_both, soft[:, v], ALU.mult)
+            for v in range(2):
+                nc.vector.scalar_tensor_tensor(
+                    pull[v][:].rearrange("p u i f -> p (u i f)"), s[v][:].rearrange("p u i f -> p (u i f)"), 1.0,
+                    minus_d[v][:].rearrange("p u i f -> p (u i f)"), ALU.subtract, ALU.mult,
+                )
+            for v, piece in enumerate(pair):
+                term = keep.tile([P, 2, PARTNERS, P], F32, name=f"term{2 * n + v}")
+                engine = nc.vector if n == len(pairs) - 1 and v == 1 else nc.gpsimd
+                engine.tensor_tensor(term[:], s[v][:], pull[v][:], ALU.mult)
+                for u, unit in enumerate(piece):
+                    terms[unit] = term[:, u]
 
-        def project(cols, z_bf, first_bank):
+        def turn_back(b, z_bf):
+            back = psum.tile([P, PACK, P], F32, name=f"e{2 + b}")
+            for t in range(PACK):
+                for i in range(PARTNERS):
+                    nc.tensor.matmul(
+                        back[:, t, :], terms[(t, b)][:, i, :], ident[:], start=(i == 0), stop=(i == PARTNERS - 1), is_transpose=True
+                    )
+            nc.vector.tensor_tensor(
+                z_bf, back[:].rearrange("p t j -> p j t"), minus_gain[:].unsqueeze(1).to_broadcast([P, P, PACK]), ALU.mult
+            )
+
+        def project(cols, z_bf, banks):
             width = cols.stop - cols.start
             last = cols.stop == S
             z_codes = keep.tile([P, width], U32, name=f"z_codes{cols.start}", align_bytes=64)
             z_scale = keep.tile([P, width], U8, name=f"z_scale{cols.start}", align_bytes=64)
             nc.vector.quantize_mx(z_codes[:].bitcast(FP8X4), z_scale[:], z_bf[:].rearrange("p c t -> p (c t)"))
             for half in range(2):
-                out_acc = psum.tile([P, 2, width], F32, name=f"bank{first_bank + half}")
-                result = keep.tile([P, 2, width], F32, name=f"result{first_bank + half}")
+                out_acc = psum.tile([P, 2, width], F32, name=banks[half])
+                result = keep.tile([P, 2, width], F32, name=f"result{cols.start}_{half}")
                 for u in range(2):
                     rows = slice((2 * half + u) * P, (2 * half + u + 1) * P)
                     nc.tensor.matmul_mx(
@@ -231,18 +211,23 @@ def tile_picked_ljpot_none_p_kernel(tc, x_words, x_scales, w1, q, gn, w2, offs, 
                 queue = nc.scalar if last and half == 0 else nc.sync
                 queue.dma_start(out_rows[:, 2 * half : 2 * half + 2, cols], result[:])
 
-        last_pair = len(pairs) - 1
-        for n in range(last_pair):
-            make_terms(n, force_factors(n), slice(0, HALF))
-        z_left = sum_on_tensor(left, "z_bf")
+        for n, pair in enumerate(pairs):
+            do_pair(n, pair)
+        w2_bf = keep.tile([P, N, PACK], BF16, name=f"inv_root{len(pairs) - 1}", align_bytes=64)
+        for half in range(2):
+            nc.scalar.copy(
+                w2_bf[:, half * (N // 2) : (half + 1) * (N // 2), :].rearrange("p (c i) j -> p c j i", i=LINE),
+                w2_raw[:, :, half * (N // 2) : (half + 1) * (N // 2)].rearrange("p j (c i) -> p c j i", i=LINE),
+            )
+        z_left = keep.tile([P, HALF, PACK], BF16, name=f"soft{len(pairs) - 1}", align_bytes=64)
+        for b in range(2):
+            turn_back(b, z_left[:, block(b), :])
+        w2_codes = keep.tile([P, N], U32, name="w2_codes", align_bytes=64)
+        w2_scale = keep.tile([P, N], U8, name="w2_scale", align_bytes=64)
         nc.vector.quantize_mx(w2_codes[:].bitcast(FP8X4), w2_scale[:], w2_bf[:].rearrange("p m j -> p (m j)"))
-        project(left, z_left, first_bank=0)
 
-        third, fourth = slice(HALF, HALF + P), slice(HALF + P, S)
-        factor = force_factors(last_pair)
-        make_terms(last_pair, factor, slice(0, P))
-        z_third = sum_on_vector(third, "z_bf")
-        make_terms(last_pair, factor, slice(P, HALF))
-        project(third, z_third, first_bank=2)
-        z_fourth = sum_on_vector(fourth, "z_bf_last")
-        project(fourth, z_fourth, first_bank=4)
+        project(left, z_left, ["e2", "e3"])
+        for b in (2, 3):
+            z_block = keep.tile([P, P, PACK], BF16, name=f"z_block{b}", align_bytes=64)
+            turn_back(b, z_block[:])
+            project(block(b), z_block, ["q0", "q1"] if b == 2 else ["e0", "e1"])

@@ -121,17 +121,34 @@ def tile_picked_ljpot_none_p_kernel(tc, x_words, x_scales, w1, q, gn, w2, offs, 
                 copy_out = nc.vector.tensor_copy if t == 0 and cols == right else nc.scalar.copy
                 copy_out(y[t][:, cols], y_acc[:])
 
-        minus_partner = [keep.tile([P, PARTNERS, S], F32, name=f"minus_partner{t}") for t in range(PACK)]
-        for t in range(PACK):
-            for cols in (left, right):
-                for i in range(PARTNERS):
-                    looked_up = y[t][:].indirect(partners[i][:, cols.start // GROUP : cols.stop // GROUP])
-                    if cols == right and t == PACK - 1:
-                        nc.scalar.activation(minus_partner[t][:, i, cols], looked_up, ACT.Copy, scale=-1.0)
-                    else:
-                        nc.vector.tensor_scalar(minus_partner[t][:, i, cols], looked_up, -1.0, 0.0, ALU.mult, ALU.add)
+        minus_partner = {}
 
-        pieces = [[(t, b), (t, b + 1)] for t in range(PACK) for b in (0, 2)]
+        def look_up(t, h, i, on_scalar, name):
+            gathered = keep.tile([P, HALF], F32, name=name)
+            looked_up = y[t][:].indirect(partners[i][:, h * HALF // GROUP : (h + 1) * HALF // GROUP])
+            if on_scalar:
+                nc.scalar.activation(gathered[:], looked_up, ACT.Copy, scale=-1.0)
+            else:
+                nc.vector.tensor_scalar(gathered[:], looked_up, -1.0, 0.0, ALU.mult, ALU.add)
+            for b in range(2):
+                minus_partner[(t, 2 * h + b, i)] = gathered[:, b * P : (b + 1) * P]
+
+        for t in range(PACK):
+            for h in range(2):
+                for i in range(PARTNERS):
+                    if (t, h, i) != (3, 1, 1):
+                        look_up(t, h, i, (t, h) == (3, 0), f"gathered{t}{h}{i}")
+
+        w2_bf = keep.tile([P, N, PACK], BF16, name="w2_bf", align_bytes=64)
+        for half in range(2):
+            nc.gpsimd.tensor_scalar(
+                w2_bf[:, half * (N // 2) : (half + 1) * (N // 2), :],
+                w2_raw[:, :, half * (N // 2) : (half + 1) * (N // 2)].rearrange("p j m -> p m j"),
+                1.0, 0.0, ALU.mult, ALU.add,
+            )
+
+        pieces = [[(t, b), (t, b + 1)] for t in (0, 1) for b in (0, 2)]
+        pieces = pieces + [[(t, 0), (t, 1)] for t in (2, 3)] + [[(2, b), (3, b)] for b in (2, 3)]
         pairs = [pieces[n : n + 2] for n in range(0, len(pieces), 2)]
         out_rows = out.rearrange("(mt p) j -> p mt j", p=P)
 
@@ -151,18 +168,23 @@ def tile_picked_ljpot_none_p_kernel(tc, x_words, x_scales, w1, q, gn, w2, offs, 
                     for i in range(PARTNERS):
                         nc.tensor.matmul(e[:, u, i, :], y[t][:, block(b)], ident[:], start=True, stop=False, is_transpose=True)
                         nc.tensor.matmul(
-                            e[:, u, i, :], minus_partner[t][:, i, block(b)], ident[:], start=False, stop=True, is_transpose=True
+                            e[:, u, i, :], minus_partner[(t, b, i)], ident[:], start=False, stop=True, is_transpose=True
                         )
                 minus_d.append(e)
             for v, piece in enumerate(pair):
                 for u, (t, b) in enumerate(piece):
                     nc.tensor.transpose(q_turned[:, v, u, :], strength[t][:, block(b)], ident[:])
-            squared = [work.tile([P, 4 * P], F32, name="squared") for v in range(2)]
+            squared = [keep.tile([P, 4 * P], F32, name=f"squared{n}_{v}") for v in range(2)]
             for v in range(2):
                 nc.scalar.activation(squared[v][:], minus_d[v][:].rearrange("p u i f -> p (u i f)"), ACT.Square)
             for v in range(2):
                 nc.scalar.activation(inv_root[:, v], squared[v][:], ACT.Abs_reciprocal_sqrt, bias=one[:])
-            nc.scalar.activation(soft[:].rearrange("p v u i f -> p v (u i f)"), inv_root[:], ACT.Square)
+            if n == 0:
+                for v in range(2):
+                    nc.gpsimd.tensor_tensor(soft[:, v].rearrange("p u i f -> p (u i f)"), inv_root[:, v], inv_root[:, v], ALU.mult)
+                look_up(3, 1, 1, True, "squared0_1")
+            else:
+                nc.scalar.activation(soft[:].rearrange("p v u i f -> p v (u i f)"), inv_root[:], ACT.Square)
             s = [keep.tile([P, 2, PARTNERS, P], F32, name=f"s{n}_{v}") for v in range(2)]
             pull = [keep.tile([P, 2, PARTNERS, P], F32, name=f"pull{n}_{v}") for v in range(2)]
             for v in range(2):
@@ -175,7 +197,7 @@ def tile_picked_ljpot_none_p_kernel(tc, x_words, x_scales, w1, q, gn, w2, offs, 
                 )
             for v, piece in enumerate(pair):
                 term = keep.tile([P, 2, PARTNERS, P], F32, name=f"term{2 * n + v}")
-                engine = nc.vector if n == len(pairs) - 1 and v == 1 else nc.gpsimd
+                engine = nc.vector if n == len(pairs) - 1 else nc.gpsimd
                 engine.tensor_tensor(term[:], s[v][:], pull[v][:], ALU.mult)
                 for u, unit in enumerate(piece):
                     terms[unit] = term[:, u]
@@ -213,16 +235,19 @@ def tile_picked_ljpot_none_p_kernel(tc, x_words, x_scales, w1, q, gn, w2, offs, 
 
         for n, pair in enumerate(pairs):
             do_pair(n, pair)
-        w2_bf = keep.tile([P, N, PACK], BF16, name=f"inv_root{len(pairs) - 1}", align_bytes=64)
-        for half in range(2):
-            nc.scalar.copy(
-                w2_bf[:, half * (N // 2) : (half + 1) * (N // 2), :].rearrange("p (c i) j -> p c j i", i=LINE),
-                w2_raw[:, :, half * (N // 2) : (half + 1) * (N // 2)].rearrange("p j (c i) -> p c j i", i=LINE),
-            )
-        z_left = keep.tile([P, HALF, PACK], BF16, name=f"soft{len(pairs) - 1}", align_bytes=64)
-        for b in range(2):
-            turn_back(b, z_left[:, block(b), :])
-        w2_codes = keep.tile([P, N], U32, name="w2_codes", align_bytes=64)
+        z_left = keep.tile([P, HALF, PACK], BF16, name=f"inv_root{len(pairs) - 1}", align_bytes=64)
+        for two in range(2):
+            back = psum.tile([P, 2, HALF], F32, name=f"e{2 + two}")
+            for u in range(2):
+                t = 2 * two + u
+                for b in range(2):
+                    for i in range(PARTNERS):
+                        nc.tensor.matmul(
+                            back[:, u, block(b)], terms[(t, b)][:, i, :], ident[:],
+                            start=(i == 0), stop=(i == PARTNERS - 1), is_transpose=True,
+                        )
+                nc.scalar.activation(z_left[:, :, t], back[:, u, :], ACT.Copy, scale=minus_gain[:, t : t + 1])
+        w2_codes = keep.tile([P, N], U32, name=f"soft{len(pairs) - 1}", align_bytes=64)
         w2_scale = keep.tile([P, N], U8, name="w2_scale", align_bytes=64)
         nc.vector.quantize_mx(w2_codes[:].bitcast(FP8X4), w2_scale[:], w2_bf[:].rearrange("p m j -> p (m j)"))
 

@@ -31,32 +31,30 @@ def tile_picked_ljpot_none_p_kernel(tc, x_words, x_scales, w1, q, gn, w2, offs, 
     with ExitStack() as ctx:
         keep = ctx.enter_context(tc.tile_pool(name="keep", bufs=1))
         work = ctx.enter_context(tc.tile_pool(name="work", bufs=4))
+        shared = ctx.enter_context(tc.tile_pool(name="shared", bufs=1))
         psum = ctx.enter_context(tc.psum_pool(name="psum", bufs=1))
-
-        w1_rows = w1.rearrange("(p j) c -> p j c", j=PACK)
-
-        def load_w1(half):
-            raw = keep.tile([P, PACK, H // 2], F32, name=f"stage{half}")
-            nc.sync.dma_start(raw[:], w1_rows[:, :, half * (H // 2) : (half + 1) * (H // 2)])
-            return raw
 
         def load_list(name, source):
             offsets = keep.tile([P, S // GROUP], U16, name=name)
             nc.sync.dma_start(offsets[:], source)
             return offsets
 
-        w1_raw = [load_w1(0)]
-        x_scale_table = keep.tile([P, T], U8, name="x_scale_table")
+        x_word_table = keep.tile([P, T], I32, name="stage0")
+        nc.sync.dma_start(x_word_table[:], x_words[0].rearrange("p n t -> p (n t)").bitcast(I32))
+        picks = load_list("picks", offs)
+        x_scale_table = keep.tile([P, T], U8, name="stage1")
         nc.gpsimd.memset(x_scale_table[:].bitcast(I32), 0)
         for quad in range(P // QUADRANT):
             nc.sync.dma_start(
                 x_scale_table[QUADRANT * quad : QUADRANT * quad + 4, :].bitcast(I32),
                 x_scales[0, 4 * quad : 4 * quad + 4, :].bitcast(I32),
             )
-        picks = load_list("picks", offs)
-        w1_raw.append(load_w1(1))
-        x_word_table = keep.tile([P, T], I32, name="stage2")
-        nc.sync.dma_start(x_word_table[:], x_words[0].rearrange("p n t -> p (n t)").bitcast(I32))
+        w1_rows = w1.rearrange("(p j) c -> p j c", j=PACK)
+        w1_raw = []
+        for half in range(2):
+            raw = keep.tile([P, PACK, H // 2], F32, name=f"stage{2 + half}")
+            nc.sync.dma_start(raw[:], w1_rows[:, :, half * (H // 2) : (half + 1) * (H // 2)])
+            w1_raw.append(raw)
         partners = [load_list("partner0", p1), load_list("partner1", p2)]
         gain = keep.tile([P, PACK], F32, name="gain")
         nc.sync.dma_start(gain[:], gn.rearrange("(p t) o -> p (t o)", t=PACK))
@@ -71,43 +69,39 @@ def tile_picked_ljpot_none_p_kernel(tc, x_words, x_scales, w1, q, gn, w2, offs, 
         ident = keep.tile([P, P], F32, name="ident")
         make_identity(nc, ident[:])
 
+        x_codes = keep.tile([P, S], U32, name="x_codes", align_bytes=64)
+        nc.vector.tensor_copy(x_codes[:], x_word_table[:].bitcast(U32).indirect(picks[:]))
+        x_scale = keep.tile([P, S], U8, name="x_scale", align_bytes=64)
+        nc.vector.tensor_copy(x_scale[:], x_scale_table[:].indirect(picks[:]))
+
         w1_bf = keep.tile([P, PACK, P, PACK], BF16, name="w1_bf", align_bytes=64)
-        quarter = P // 4
-        for m0, m1, cast in (
-            (0, 2 * quarter, nc.scalar.copy),
-            (2 * quarter, 3 * quarter, nc.scalar.copy),
-            (3 * quarter, P, nc.vector.tensor_copy),
-        ):
+        for m0, m1, cast in ((0, 64, nc.scalar.copy), (64, 88, nc.scalar.copy), (88, P, nc.vector.tensor_copy)):
             half, base = divmod(m0, P // 2)
             cast(
                 w1_bf[:, :, m0:m1, :].rearrange("p t m j -> p m j t"),
                 w1_raw[half][:].rearrange("p j (m t) -> p m j t", t=PACK)[:, base : base + m1 - m0],
             )
-        x_scale = keep.tile([P, S], U8, name="x_scale", align_bytes=64)
-        nc.vector.tensor_copy(x_scale[:], x_scale_table[:].indirect(picks[:]))
         w1_codes = keep.tile([P, H], U32, name="w1_codes", align_bytes=64)
         w1_scale = keep.tile([P, H], U8, name="w1_scale", align_bytes=64)
-        nc.vector.quantize_mx(w1_codes[:].bitcast(FP8X4), w1_scale[:], w1_bf[:].rearrange("p t m j -> p (t m j)"))
-        x_codes = keep.tile([P, S], U32, name="x_codes", align_bytes=64)
-        for cols in (left, right):
-            nc.vector.tensor_copy(
-                x_codes[:, cols],
-                x_word_table[:].bitcast(U32).indirect(picks[:, cols.start // GROUP : cols.stop // GROUP]),
+        for t0, t1 in ((0, 1), (1, 2), (2, 4)):
+            nc.vector.quantize_mx(
+                w1_codes[:, t0 * P : t1 * P].bitcast(FP8X4), w1_scale[:, t0 * P : t1 * P],
+                w1_bf[:, t0:t1].rearrange("p t m j -> p (t m j)"),
             )
 
         q_rows = q.rearrange("(p t) s -> p t s", t=PACK)
+        w2_raw = keep.tile([P, PACK, N], F32, name="stage0")
+        nc.sync.dma_start(w2_raw[:], w2.rearrange("(p j) m -> p j m", j=PACK))
         strength = []
         for half in range(2):
-            two_tiles = keep.tile([P, 2, S], F32, name=f"stage{half}")
+            two_tiles = keep.tile([P, 2, S], F32, name=f"stage{1 + half}")
             nc.sync.dma_start(two_tiles[:], q_rows[:, 2 * half : 2 * half + 2, :])
             strength.extend([two_tiles[:, 0, :], two_tiles[:, 1, :]])
-        w2_raw = keep.tile([P, PACK, N], F32, name="stage2")
-        nc.sync.dma_start(w2_raw[:], w2.rearrange("(p j) m -> p j m", j=PACK))
         minus_gain = keep.tile([P, PACK], F32, name="minus_gain")
         nc.vector.tensor_scalar(minus_gain[:], gain[:], -1.0, None, ALU.mult)
 
         y = [keep.tile([P, S], F32, name=f"y{t}") for t in range(PACK)]
-        y_banks = ["e3", "e4", "q0", "q1", "e5"]
+        y_banks = ["e3", "e4", "q", "e5", "e6"]
         bank = 0
         for t in range(PACK):
             feats = slice(t * P, (t + 1) * P)
@@ -124,7 +118,10 @@ def tile_picked_ljpot_none_p_kernel(tc, x_words, x_scales, w1, q, gn, w2, offs, 
         minus_partner = {}
 
         def look_up(t, h, i, on_scalar, name):
-            gathered = keep.tile([P, HALF], F32, name=name)
+            if name in (0, 1, 2):
+                gathered = shared.tile([P, HALF], F32, name=f"after_w2_{name}", align_bytes=64, offset=1024 * name)
+            else:
+                gathered = keep.tile([P, HALF], F32, name=name)
             looked_up = y[t][:].indirect(partners[i][:, h * HALF // GROUP : (h + 1) * HALF // GROUP])
             if on_scalar:
                 nc.scalar.activation(gathered[:], looked_up, ACT.Copy, scale=-1.0)
@@ -134,12 +131,10 @@ def tile_picked_ljpot_none_p_kernel(tc, x_words, x_scales, w1, q, gn, w2, offs, 
                 minus_partner[(t, 2 * h + b, i)] = gathered[:, b * P : (b + 1) * P]
 
         for t in range(PACK):
-            for h in range(2):
-                for i in range(PARTNERS):
-                    if (t, h, i) != (3, 1, 1):
-                        look_up(t, h, i, (t, h) == (3, 0), f"gathered{t}{h}{i}")
+            for i in range(PARTNERS):
+                look_up(t, 0, i, t == PACK - 1, f"gathered{t}{i}")
 
-        w2_bf = keep.tile([P, N, PACK], BF16, name="w2_bf", align_bytes=64)
+        w2_bf = shared.tile([P, N, PACK], BF16, name="w2_bf", align_bytes=64, offset=0)
         for half in range(2):
             nc.gpsimd.tensor_scalar(
                 w2_bf[:, half * (N // 2) : (half + 1) * (N // 2), :],
@@ -147,8 +142,11 @@ def tile_picked_ljpot_none_p_kernel(tc, x_words, x_scales, w1, q, gn, w2, offs, 
                 1.0, 0.0, ALU.mult, ALU.add,
             )
 
-        pieces = [[(t, b), (t, b + 1)] for t in (0, 1) for b in (0, 2)]
-        pieces = pieces + [[(t, 0), (t, 1)] for t in (2, 3)] + [[(2, b), (3, b)] for b in (2, 3)]
+        w2_codes = keep.tile([P, N], U32, name="w2_codes", align_bytes=64)
+        w2_scale = keep.tile([P, N], U8, name="w2_scale", align_bytes=64)
+        nc.vector.quantize_mx(w2_codes[:].bitcast(FP8X4), w2_scale[:], w2_bf[:].rearrange("p m j -> p (m j)"))
+
+        pieces = [[(t, 0), (t, 1)] for t in range(PACK)] + [[(t, 2), (t, 3)] for t in (0, 1)] + [[(2, b), (3, b)] for b in (2, 3)]
         pairs = [pieces[n : n + 2] for n in range(0, len(pieces), 2)]
         out_rows = out.rearrange("(mt p) j -> p mt j", p=P)
 
@@ -157,50 +155,79 @@ def tile_picked_ljpot_none_p_kernel(tc, x_words, x_scales, w1, q, gn, w2, offs, 
 
         terms = {}
 
-        def do_pair(n, pair):
-            minus_d = []
-            inv_root = keep.tile([P, 2, 4 * P], F32, name=f"inv_root{n}", align_bytes=64)
-            soft = keep.tile([P, 2, 2, PARTNERS, P], F32, name=f"soft{n}", align_bytes=64)
-            q_turned = psum.tile([P, 2, 2, P], F32, name=f"q{n % 2}")
-            for v, piece in enumerate(pair):
-                e = psum.tile([P, 2, PARTNERS, P], F32, name=f"e{(2 * n + v) % 6}")
+        flat = "p u i f -> p (u i f)"
+        last_pair = len(pairs) - 1
+        minus_d = []
+
+        def turn_differences(piece):
+            e = psum.tile([P, 2, PARTNERS, P], F32, name=f"e{len(minus_d) % 7}")
+            for i in range(PARTNERS):
                 for u, (t, b) in enumerate(piece):
-                    for i in range(PARTNERS):
-                        nc.tensor.matmul(e[:, u, i, :], y[t][:, block(b)], ident[:], start=True, stop=False, is_transpose=True)
-                        nc.tensor.matmul(
-                            e[:, u, i, :], minus_partner[(t, b, i)], ident[:], start=False, stop=True, is_transpose=True
-                        )
-                minus_d.append(e)
+                    nc.tensor.matmul(e[:, u, i, :], y[t][:, block(b)], ident[:], start=True, stop=False, is_transpose=True)
+                    nc.tensor.matmul(e[:, u, i, :], minus_partner[(t, b, i)], ident[:], start=False, stop=True, is_transpose=True)
+            minus_d.append(e)
+
+        def do_pair(n, pair):
+            inv_root = keep.tile([P, 2, 4 * P], F32, name=f"inv_root{n}", align_bytes=64)
+            if n == 0:
+                soft = shared.tile([P, 2, 2, PARTNERS, P], F32, name="soft0", align_bytes=64, offset=3072)
+            else:
+                soft = keep.tile([P, 2, 2, PARTNERS, P], F32, name=f"soft{n}", align_bytes=64)
+            q_turned = psum.tile([P, 2, 2, P], F32, name="q")
             for v, piece in enumerate(pair):
                 for u, (t, b) in enumerate(piece):
                     nc.tensor.transpose(q_turned[:, v, u, :], strength[t][:, block(b)], ident[:])
             squared = [keep.tile([P, 4 * P], F32, name=f"squared{n}_{v}") for v in range(2)]
-            for v in range(2):
-                nc.scalar.activation(squared[v][:], minus_d[v][:].rearrange("p u i f -> p (u i f)"), ACT.Square)
-            for v in range(2):
+            s = keep.tile([P, 2, 2, PARTNERS, P], F32, name=f"s{n}")
+            pull = keep.tile([P, 2, 2, PARTNERS, P], F32, name=f"pull{n}", align_bytes=64)
+            term = keep.tile([P, 2, 2, PARTNERS, P], F32, name=f"term{n}")
+
+            def square(v):
+                nc.scalar.activation(squared[v][:], minus_d[2 * n + v][:].rearrange(flat), ACT.Square)
+
+            def inverse_root(v):
                 nc.scalar.activation(inv_root[:, v], squared[v][:], ACT.Abs_reciprocal_sqrt, bias=one[:])
-            if n == 0:
-                for v in range(2):
-                    nc.gpsimd.tensor_tensor(soft[:, v].rearrange("p u i f -> p (u i f)"), inv_root[:, v], inv_root[:, v], ALU.mult)
-                look_up(3, 1, 1, True, "squared0_1")
-            else:
-                nc.scalar.activation(soft[:].rearrange("p v u i f -> p v (u i f)"), inv_root[:], ACT.Square)
-            s = [keep.tile([P, 2, PARTNERS, P], F32, name=f"s{n}_{v}") for v in range(2)]
-            pull = [keep.tile([P, 2, PARTNERS, P], F32, name=f"pull{n}_{v}") for v in range(2)]
-            for v in range(2):
+
+            def make_s(v):
                 q_both = q_turned[:, v].unsqueeze(2).to_broadcast([P, 2, PARTNERS, P])
-                nc.vector.tensor_tensor(s[v][:], q_both, soft[:, v], ALU.mult)
-            for v in range(2):
+                nc.vector.tensor_tensor(s[:, v], q_both, soft[:, v], ALU.mult)
+
+            def make_pull(v):
                 nc.vector.scalar_tensor_tensor(
-                    pull[v][:].rearrange("p u i f -> p (u i f)"), s[v][:].rearrange("p u i f -> p (u i f)"), 1.0,
-                    minus_d[v][:].rearrange("p u i f -> p (u i f)"), ALU.subtract, ALU.mult,
+                    pull[:, v].rearrange(flat), s[:, v].rearrange(flat), 1.0, minus_d[2 * n + v][:].rearrange(flat),
+                    ALU.subtract, ALU.mult,
                 )
+
+            if n < last_pair:
+                for step in (square, inverse_root):
+                    for v in range(2):
+                        step(v)
+                soft_flat = soft[:].rearrange("p v u i f -> p v (u i f)")
+                if n < 2:
+                    nc.gpsimd.tensor_tensor(soft_flat, inv_root[:], inv_root[:], ALU.mult)
+                else:
+                    nc.scalar.activation(soft_flat, inv_root[:], ACT.Square)
+                if n == 1:
+                    for i in range(PARTNERS):
+                        look_up(PACK - 1, 1, i, True, f"squared1_{i}")
+                    turn_differences(pieces[6])
+                    turn_differences(pieces[7])
+                for step in (make_s, make_pull):
+                    for v in range(2):
+                        step(v)
+                both = "p v u i f -> p (v u i f)"
+                nc.gpsimd.tensor_tensor(term[:].rearrange(both), s[:].rearrange(both), pull[:].rearrange(both), ALU.mult)
+            else:
+                for v in range(2):
+                    square(v)
+                    inverse_root(v)
+                    nc.scalar.activation(soft[:, v].rearrange(flat), inv_root[:, v], ACT.Square)
+                    make_s(v)
+                    make_pull(v)
+                    nc.vector.tensor_tensor(term[:, v].rearrange(flat), s[:, v].rearrange(flat), pull[:, v].rearrange(flat), ALU.mult)
             for v, piece in enumerate(pair):
-                term = keep.tile([P, 2, PARTNERS, P], F32, name=f"term{2 * n + v}")
-                engine = nc.vector if n == len(pairs) - 1 else nc.gpsimd
-                engine.tensor_tensor(term[:], s[v][:], pull[v][:], ALU.mult)
                 for u, unit in enumerate(piece):
-                    terms[unit] = term[:, u]
+                    terms[unit] = term[:, v, u]
 
         def turn_back(b, z_bf):
             back = psum.tile([P, PACK, P], F32, name=f"e{2 + b}")
@@ -213,10 +240,10 @@ def tile_picked_ljpot_none_p_kernel(tc, x_words, x_scales, w1, q, gn, w2, offs, 
                 z_bf, back[:].rearrange("p t j -> p j t"), minus_gain[:].unsqueeze(1).to_broadcast([P, P, PACK]), ALU.mult
             )
 
-        def project(cols, z_bf, banks):
+        def project(cols, z_bf, banks, codes_name):
             width = cols.stop - cols.start
             last = cols.stop == S
-            z_codes = keep.tile([P, width], U32, name=f"z_codes{cols.start}", align_bytes=64)
+            z_codes = keep.tile([P, width], U32, name=codes_name, align_bytes=64)
             z_scale = keep.tile([P, width], U8, name=f"z_scale{cols.start}", align_bytes=64)
             nc.vector.quantize_mx(z_codes[:].bitcast(FP8X4), z_scale[:], z_bf[:].rearrange("p c t -> p (c t)"))
             for half in range(2):
@@ -228,11 +255,18 @@ def tile_picked_ljpot_none_p_kernel(tc, x_words, x_scales, w1, q, gn, w2, offs, 
                         out_acc[:, u, :], w2_codes[:, rows].bitcast(FP8X4), w2_scale[:, rows],
                         z_codes[:].bitcast(FP8X4), z_scale[:], start=True, stop=True,
                     )
-                copy_out = nc.vector.tensor_copy if last and half == 1 else nc.scalar.copy
+                copy_out = nc.vector.tensor_copy if cols != left and half == 1 else nc.scalar.copy
                 copy_out(result[:], out_acc[:])
                 queue = nc.scalar if last and half == 0 else nc.sync
                 queue.dma_start(out_rows[:, 2 * half : 2 * half + 2, cols], result[:])
 
+        for piece in pieces[:PACK]:
+            turn_differences(piece)
+        for t in range(PACK - 1):
+            for i in range(PARTNERS):
+                look_up(t, 1, i, False, "gathered00" if (t, i) == (0, 0) else (2 * t + i - 1) % 3)
+            if t < 2:
+                turn_differences(pieces[PACK + t])
         for n, pair in enumerate(pairs):
             do_pair(n, pair)
         z_left = keep.tile([P, HALF, PACK], BF16, name=f"inv_root{len(pairs) - 1}", align_bytes=64)
@@ -246,13 +280,11 @@ def tile_picked_ljpot_none_p_kernel(tc, x_words, x_scales, w1, q, gn, w2, offs, 
                             back[:, u, block(b)], terms[(t, b)][:, i, :], ident[:],
                             start=(i == 0), stop=(i == PARTNERS - 1), is_transpose=True,
                         )
+            for u in range(2):
+                t = 2 * two + u
                 nc.scalar.activation(z_left[:, :, t], back[:, u, :], ACT.Copy, scale=minus_gain[:, t : t + 1])
-        w2_codes = keep.tile([P, N], U32, name=f"soft{len(pairs) - 1}", align_bytes=64)
-        w2_scale = keep.tile([P, N], U8, name="w2_scale", align_bytes=64)
-        nc.vector.quantize_mx(w2_codes[:].bitcast(FP8X4), w2_scale[:], w2_bf[:].rearrange("p m j -> p (m j)"))
-
-        project(left, z_left, ["e2", "e3"])
+        project(left, z_left, ["e2", "e3"], f"pull{last_pair}")
         for b in (2, 3):
             z_block = keep.tile([P, P, PACK], BF16, name=f"z_block{b}", align_bytes=64)
             turn_back(b, z_block[:])
-            project(block(b), z_block, ["q0", "q1"] if b == 2 else ["e0", "e1"])
+            project(block(b), z_block, ["q", "e1"] if b == 2 else ["e6", "e0"], f"z_codes{b}")

@@ -180,7 +180,6 @@ def tile_picked_ljpot_none_p_kernel(tc, x_words, x_scales, w1, q, gn, w2, offs, 
             squared = [keep.tile([P, 4 * P], F32, name=f"squared{n}_{v}") for v in range(2)]
             s = keep.tile([P, 2, 2, PARTNERS, P], F32, name=f"s{n}")
             pull = keep.tile([P, 2, 2, PARTNERS, P], F32, name=f"pull{n}", align_bytes=64)
-            term = keep.tile([P, 2, 2, PARTNERS, P], F32, name=f"term{n}")
 
             def square(v):
                 nc.scalar.activation(squared[v][:], minus_d[2 * n + v][:].rearrange(flat), ACT.Square)
@@ -190,7 +189,7 @@ def tile_picked_ljpot_none_p_kernel(tc, x_words, x_scales, w1, q, gn, w2, offs, 
 
             def make_s(v):
                 q_both = q_turned[:, v].unsqueeze(2).to_broadcast([P, 2, PARTNERS, P])
-                nc.vector.tensor_tensor(s[:, v], q_both, soft[:, v], ALU.mult)
+                nc.vector.tensor_tensor(s[:, v], soft[:, v], q_both, ALU.mult)
 
             def make_pull(v):
                 nc.vector.scalar_tensor_tensor(
@@ -216,6 +215,7 @@ def tile_picked_ljpot_none_p_kernel(tc, x_words, x_scales, w1, q, gn, w2, offs, 
                     for v in range(2):
                         step(v)
                 both = "p v u i f -> p (v u i f)"
+                term = keep.tile([P, 2, 2, PARTNERS, P], F32, name=f"term{n}")
                 nc.gpsimd.tensor_tensor(term[:].rearrange(both), s[:].rearrange(both), pull[:].rearrange(both), ALU.mult)
             else:
                 for v in range(2):
@@ -224,6 +224,8 @@ def tile_picked_ljpot_none_p_kernel(tc, x_words, x_scales, w1, q, gn, w2, offs, 
                     nc.scalar.activation(soft[:, v].rearrange(flat), inv_root[:, v], ACT.Square)
                     make_s(v)
                     make_pull(v)
+                term = keep.tile([P, 2, 2, PARTNERS, P], F32, name=f"soft{n}", align_bytes=64)
+                for v in range(2):
                     nc.vector.tensor_tensor(term[:, v].rearrange(flat), s[:, v].rearrange(flat), pull[:, v].rearrange(flat), ALU.mult)
             for v, piece in enumerate(pair):
                 for u, unit in enumerate(piece):
@@ -237,7 +239,7 @@ def tile_picked_ljpot_none_p_kernel(tc, x_words, x_scales, w1, q, gn, w2, offs, 
                         back[:, t, :], terms[(t, b)][:, i, :], ident[:], start=(i == 0), stop=(i == PARTNERS - 1), is_transpose=True
                     )
             nc.vector.tensor_tensor(
-                z_bf, back[:].rearrange("p t j -> p j t"), minus_gain[:].unsqueeze(1).to_broadcast([P, P, PACK]), ALU.mult
+                z_bf, minus_gain[:].unsqueeze(1).to_broadcast([P, P, PACK]), back[:].rearrange("p t j -> p j t"), ALU.mult
             )
 
         def project(cols, z_bf, banks, codes_name):

@@ -39,9 +39,14 @@ def tile_picked_ljpot_none_p_kernel(tc, x_words, x_scales, w1, q, gn, w2, offs, 
             nc.sync.dma_start(offsets[:], source)
             return offsets
 
-        x_word_table = keep.tile([P, T], I32, name="stage0")
-        nc.sync.dma_start(x_word_table[:], x_words[0].rearrange("p n t -> p (n t)").bitcast(I32))
-        picks = load_list("picks", offs)
+        w1_rows = w1.rearrange("(p j) c -> p j c", j=PACK)
+
+        def load_w1(half):
+            raw = keep.tile([P, PACK, H // 2], F32, name=f"stage{2 * half}")
+            nc.sync.dma_start(raw[:], w1_rows[:, :, half * (H // 2) : (half + 1) * (H // 2)])
+            return raw
+
+        w1_raw = [load_w1(0)]
         x_scale_table = keep.tile([P, T], U8, name="stage1")
         nc.gpsimd.memset(x_scale_table[:].bitcast(I32), 0)
         for quad in range(P // QUADRANT):
@@ -49,12 +54,10 @@ def tile_picked_ljpot_none_p_kernel(tc, x_words, x_scales, w1, q, gn, w2, offs, 
                 x_scale_table[QUADRANT * quad : QUADRANT * quad + 4, :].bitcast(I32),
                 x_scales[0, 4 * quad : 4 * quad + 4, :].bitcast(I32),
             )
-        w1_rows = w1.rearrange("(p j) c -> p j c", j=PACK)
-        w1_raw = []
-        for half in range(2):
-            raw = keep.tile([P, PACK, H // 2], F32, name=f"stage{2 + half}")
-            nc.sync.dma_start(raw[:], w1_rows[:, :, half * (H // 2) : (half + 1) * (H // 2)])
-            w1_raw.append(raw)
+        picks = load_list("picks", offs)
+        x_word_table = keep.tile([P, T], I32, name="x_word_table")
+        nc.sync.dma_start(x_word_table[:], x_words[0].rearrange("p n t -> p (n t)").bitcast(I32))
+        w1_raw.append(load_w1(1))
         partners = [load_list("partner0", p1), load_list("partner1", p2)]
         gain = keep.tile([P, PACK], F32, name="gain")
         nc.sync.dma_start(gain[:], gn.rearrange("(p t) o -> p (t o)", t=PACK))
@@ -69,10 +72,10 @@ def tile_picked_ljpot_none_p_kernel(tc, x_words, x_scales, w1, q, gn, w2, offs, 
         ident = keep.tile([P, P], F32, name="ident")
         make_identity(nc, ident[:])
 
-        x_codes = keep.tile([P, S], U32, name="x_codes", align_bytes=64)
-        nc.vector.tensor_copy(x_codes[:], x_word_table[:].bitcast(U32).indirect(picks[:]))
         x_scale = keep.tile([P, S], U8, name="x_scale", align_bytes=64)
         nc.vector.tensor_copy(x_scale[:], x_scale_table[:].indirect(picks[:]))
+        x_codes = keep.tile([P, S], U32, name="x_codes", align_bytes=64)
+        nc.vector.tensor_copy(x_codes[:], x_word_table[:].bitcast(U32).indirect(picks[:]))
 
         w1_bf = keep.tile([P, PACK, P, PACK], BF16, name="w1_bf", align_bytes=64)
         for m0, m1, cast in ((0, 64, nc.scalar.copy), (64, 88, nc.scalar.copy), (88, P, nc.vector.tensor_copy)):

@@ -31,7 +31,6 @@ def tile_picked_ljpot_none_p_kernel(tc, x_words, x_scales, w1, q, gn, w2, offs, 
     with ExitStack() as ctx:
         keep = ctx.enter_context(tc.tile_pool(name="keep", bufs=1))
         work = ctx.enter_context(tc.tile_pool(name="work", bufs=4))
-        shared = ctx.enter_context(tc.tile_pool(name="shared", bufs=1))
         psum = ctx.enter_context(tc.psum_pool(name="psum", bufs=1))
 
         def load_list(name, source):
@@ -121,10 +120,7 @@ def tile_picked_ljpot_none_p_kernel(tc, x_words, x_scales, w1, q, gn, w2, offs, 
         minus_partner = {}
 
         def look_up(t, h, i, on_scalar, name):
-            if name in (0, 1, 2):
-                gathered = shared.tile([P, HALF], F32, name=f"after_w2_{name}", align_bytes=64, offset=1024 * name)
-            else:
-                gathered = keep.tile([P, HALF], F32, name=name)
+            gathered = keep.tile([P, HALF], F32, name=name)
             looked_up = y[t][:].indirect(partners[i][:, h * HALF // GROUP : (h + 1) * HALF // GROUP])
             if on_scalar:
                 nc.scalar.activation(gathered[:], looked_up, ACT.Copy, scale=-1.0)
@@ -137,17 +133,13 @@ def tile_picked_ljpot_none_p_kernel(tc, x_words, x_scales, w1, q, gn, w2, offs, 
             for i in range(PARTNERS):
                 look_up(t, 0, i, t == PACK - 1, f"gathered{t}{i}")
 
-        w2_bf = shared.tile([P, N, PACK], BF16, name="w2_bf", align_bytes=64, offset=0)
+        w2_bf = keep.tile([P, N, PACK], BF16, name="w2_bf", align_bytes=64)
         for half in range(2):
             nc.gpsimd.tensor_scalar(
                 w2_bf[:, half * (N // 2) : (half + 1) * (N // 2), :],
                 w2_raw[:, :, half * (N // 2) : (half + 1) * (N // 2)].rearrange("p j m -> p m j"),
                 1.0, 0.0, ALU.mult, ALU.add,
             )
-
-        w2_codes = keep.tile([P, N], U32, name="w2_codes", align_bytes=64)
-        w2_scale = keep.tile([P, N], U8, name="w2_scale", align_bytes=64)
-        nc.vector.quantize_mx(w2_codes[:].bitcast(FP8X4), w2_scale[:], w2_bf[:].rearrange("p m j -> p (m j)"))
 
         pieces = [[(t, 0), (t, 1)] for t in range(PACK)] + [[(t, 2), (t, 3)] for t in (0, 1)] + [[(2, b), (3, b)] for b in (2, 3)]
         pairs = [pieces[n : n + 2] for n in range(0, len(pieces), 2)]
@@ -170,12 +162,17 @@ def tile_picked_ljpot_none_p_kernel(tc, x_words, x_scales, w1, q, gn, w2, offs, 
                     nc.tensor.matmul(e[:, u, i, :], minus_partner[(t, b, i)], ident[:], start=False, stop=True, is_transpose=True)
             minus_d.append(e)
 
+        w2_quantised = []
+
+        def quantise_w2():
+            codes = keep.tile([P, N], U32, name="soft2", align_bytes=64)
+            scale = keep.tile([P, N], U8, name="w2_scale", align_bytes=64)
+            nc.vector.quantize_mx(codes[:].bitcast(FP8X4), scale[:], w2_bf[:].rearrange("p m j -> p (m j)"))
+            w2_quantised.extend([codes, scale])
+
         def do_pair(n, pair):
             inv_root = keep.tile([P, 2, 4 * P], F32, name=f"inv_root{n}", align_bytes=64)
-            if n == 0:
-                soft = shared.tile([P, 2, 2, PARTNERS, P], F32, name="soft0", align_bytes=64, offset=3072)
-            else:
-                soft = keep.tile([P, 2, 2, PARTNERS, P], F32, name=f"soft{n}", align_bytes=64)
+            soft = keep.tile([P, 2, 2, PARTNERS, P], F32, name=f"soft{n}", align_bytes=64)
             q_turned = psum.tile([P, 2, 2, P], F32, name="q")
             for v, piece in enumerate(pair):
                 for u, (t, b) in enumerate(piece):
@@ -218,7 +215,9 @@ def tile_picked_ljpot_none_p_kernel(tc, x_words, x_scales, w1, q, gn, w2, offs, 
                     for v in range(2):
                         step(v)
                 both = "p v u i f -> p (v u i f)"
-                term = keep.tile([P, 2, 2, PARTNERS, P], F32, name=f"term{n}")
+                if n == 2:
+                    quantise_w2()
+                term = keep.tile([P, 2, 2, PARTNERS, P], F32, name="w2_bf" if n == 2 else f"term{n}", align_bytes=64)
                 nc.gpsimd.tensor_tensor(term[:].rearrange(both), s[:].rearrange(both), pull[:].rearrange(both), ALU.mult)
             else:
                 for v in range(2):
@@ -248,6 +247,7 @@ def tile_picked_ljpot_none_p_kernel(tc, x_words, x_scales, w1, q, gn, w2, offs, 
         def project(cols, z_bf, banks, codes_name):
             width = cols.stop - cols.start
             last = cols.stop == S
+            w2_codes, w2_scale = w2_quantised
             z_codes = keep.tile([P, width], U32, name=codes_name, align_bytes=64)
             z_scale = keep.tile([P, width], U8, name=f"z_scale{cols.start}", align_bytes=64)
             nc.vector.quantize_mx(z_codes[:].bitcast(FP8X4), z_scale[:], z_bf[:].rearrange("p c t -> p (c t)"))
@@ -269,7 +269,7 @@ def tile_picked_ljpot_none_p_kernel(tc, x_words, x_scales, w1, q, gn, w2, offs, 
             turn_differences(piece)
         for t in range(PACK - 1):
             for i in range(PARTNERS):
-                look_up(t, 1, i, False, "gathered00" if (t, i) == (0, 0) else (2 * t + i - 1) % 3)
+                look_up(t, 1, i, False, f"gathered{t}{i}")
             if t < 2:
                 turn_differences(pieces[PACK + t])
         for n, pair in enumerate(pairs):

@@ -31,6 +31,7 @@ def tile_picked_ljpot_none_p_kernel(tc, x_words, x_scales, w1, q, gn, w2, offs, 
     with ExitStack() as ctx:
         keep = ctx.enter_context(tc.tile_pool(name="keep", bufs=1))
         work = ctx.enter_context(tc.tile_pool(name="work", bufs=4))
+        shared = ctx.enter_context(tc.tile_pool(name="shared", bufs=1))
         psum = ctx.enter_context(tc.psum_pool(name="psum", bufs=1))
 
         def load_list(name, source):
@@ -103,7 +104,7 @@ def tile_picked_ljpot_none_p_kernel(tc, x_words, x_scales, w1, q, gn, w2, offs, 
         nc.vector.tensor_scalar(minus_gain[:], gain[:], -1.0, None, ALU.mult)
 
         y = [keep.tile([P, S], F32, name=f"y{t}") for t in range(PACK)]
-        y_banks = ["e3", "e4", "q", "e5", "e6"]
+        y_banks = ["e3", "e4", "q0", "q1", "e5"]
         bank = 0
         for t in range(PACK):
             feats = slice(t * P, (t + 1) * P)
@@ -119,21 +120,20 @@ def tile_picked_ljpot_none_p_kernel(tc, x_words, x_scales, w1, q, gn, w2, offs, 
 
         minus_partner = {}
 
-        def look_up(t, h, i, on_scalar, name):
-            gathered = keep.tile([P, HALF], F32, name=name)
+        def look_up(t, h, i, on_scalar, gathered):
             looked_up = y[t][:].indirect(partners[i][:, h * HALF // GROUP : (h + 1) * HALF // GROUP])
             if on_scalar:
-                nc.scalar.activation(gathered[:], looked_up, ACT.Copy, scale=-1.0)
+                nc.scalar.activation(gathered, looked_up, ACT.Copy, scale=-1.0)
             else:
-                nc.vector.tensor_scalar(gathered[:], looked_up, -1.0, 0.0, ALU.mult, ALU.add)
+                nc.vector.tensor_scalar(gathered, looked_up, -1.0, 0.0, ALU.mult, ALU.add)
             for b in range(2):
                 minus_partner[(t, 2 * h + b, i)] = gathered[:, b * P : (b + 1) * P]
 
         for t in range(PACK):
             for i in range(PARTNERS):
-                look_up(t, 0, i, t == PACK - 1, f"gathered{t}{i}")
+                look_up(t, 0, i, t == PACK - 1, keep.tile([P, HALF], F32, name=f"gathered{t}{i}")[:])
 
-        w2_bf = keep.tile([P, N, PACK], BF16, name="w2_bf", align_bytes=64)
+        w2_bf = shared.tile([P, N, PACK], BF16, name="w2_bf", align_bytes=64, offset=3072)
         for half in range(2):
             nc.gpsimd.tensor_scalar(
                 w2_bf[:, half * (N // 2) : (half + 1) * (N // 2), :],
@@ -141,7 +141,11 @@ def tile_picked_ljpot_none_p_kernel(tc, x_words, x_scales, w1, q, gn, w2, offs, 
                 1.0, 0.0, ALU.mult, ALU.add,
             )
 
-        pieces = [[(t, 0), (t, 1)] for t in range(PACK)] + [[(t, 2), (t, 3)] for t in (0, 1)] + [[(2, b), (3, b)] for b in (2, 3)]
+        w2_codes = keep.tile([P, N], U32, name="w2_codes", align_bytes=64)
+        w2_scale = keep.tile([P, N], U8, name="w2_scale", align_bytes=64)
+        nc.vector.quantize_mx(w2_codes[:].bitcast(FP8X4), w2_scale[:], w2_bf[:].rearrange("p m j -> p (m j)"))
+
+        pieces = [[(t, 0), (t, 1)] for t in range(PACK)] + [[(t, b), (t + 1, b)] for t in (0, 2) for b in (2, 3)]
         pairs = [pieces[n : n + 2] for n in range(0, len(pieces), 2)]
         out_rows = out.rearrange("(mt p) j -> p mt j", p=P)
 
@@ -155,31 +159,30 @@ def tile_picked_ljpot_none_p_kernel(tc, x_words, x_scales, w1, q, gn, w2, offs, 
         minus_d = []
 
         def turn_differences(piece):
-            e = psum.tile([P, 2, PARTNERS, P], F32, name=f"e{len(minus_d) % 7}")
+            e = psum.tile([P, 2, PARTNERS, P], F32, name=f"e{len(minus_d) % 6}")
             for i in range(PARTNERS):
                 for u, (t, b) in enumerate(piece):
                     nc.tensor.matmul(e[:, u, i, :], y[t][:, block(b)], ident[:], start=True, stop=False, is_transpose=True)
                     nc.tensor.matmul(e[:, u, i, :], minus_partner[(t, b, i)], ident[:], start=False, stop=True, is_transpose=True)
             minus_d.append(e)
 
-        w2_quantised = []
-
-        def quantise_w2():
-            codes = keep.tile([P, N], U32, name="soft2", align_bytes=64)
-            scale = keep.tile([P, N], U8, name="w2_scale", align_bytes=64)
-            nc.vector.quantize_mx(codes[:].bitcast(FP8X4), scale[:], w2_bf[:].rearrange("p m j -> p (m j)"))
-            w2_quantised.extend([codes, scale])
-
         def do_pair(n, pair):
             inv_root = keep.tile([P, 2, 4 * P], F32, name=f"inv_root{n}", align_bytes=64)
-            soft = keep.tile([P, 2, 2, PARTNERS, P], F32, name=f"soft{n}", align_bytes=64)
-            q_turned = psum.tile([P, 2, 2, P], F32, name="q")
+            if n == 0:
+                soft = shared.tile([P, 2, 2, PARTNERS, P], F32, name="soft0", align_bytes=64, offset=5120)
+            else:
+                soft = keep.tile([P, 2, 2, PARTNERS, P], F32, name=f"soft{n}", align_bytes=64)
+            q_turned = psum.tile([P, 2, 2, P], F32, name=f"q{n % 2}")
             for v, piece in enumerate(pair):
                 for u, (t, b) in enumerate(piece):
                     nc.tensor.transpose(q_turned[:, v, u, :], strength[t][:, block(b)], ident[:])
             squared = [keep.tile([P, 4 * P], F32, name=f"squared{n}_{v}") for v in range(2)]
-            s = keep.tile([P, 2, 2, PARTNERS, P], F32, name=f"s{n}")
-            pull = keep.tile([P, 2, 2, PARTNERS, P], F32, name=f"pull{n}", align_bytes=64)
+            s = keep.tile([P, 2, 2, PARTNERS, P], F32, name="soft1" if n == 2 else f"s{n}", align_bytes=64)
+            if n < last_pair:
+                both_pulls = keep.tile([P, 2, 2, PARTNERS, P], F32, name=f"pull{n}", align_bytes=64)
+                pull = [both_pulls[:, v] for v in range(2)]
+            else:
+                pull = [keep.tile([P, 2, PARTNERS, P], F32, name=f"pull{n}_{v}", align_bytes=64)[:] for v in range(2)]
 
             def square(v):
                 nc.scalar.activation(squared[v][:], minus_d[2 * n + v][:].rearrange(flat), ACT.Square)
@@ -193,7 +196,7 @@ def tile_picked_ljpot_none_p_kernel(tc, x_words, x_scales, w1, q, gn, w2, offs, 
 
             def make_pull(v):
                 nc.vector.scalar_tensor_tensor(
-                    pull[:, v].rearrange(flat), s[:, v].rearrange(flat), 1.0, minus_d[2 * n + v][:].rearrange(flat),
+                    pull[v].rearrange(flat), s[:, v].rearrange(flat), 1.0, minus_d[2 * n + v][:].rearrange(flat),
                     ALU.subtract, ALU.mult,
                 )
 
@@ -208,17 +211,19 @@ def tile_picked_ljpot_none_p_kernel(tc, x_words, x_scales, w1, q, gn, w2, offs, 
                     nc.scalar.activation(soft_flat, inv_root[:], ACT.Square)
                 if n == 1:
                     for i in range(PARTNERS):
-                        look_up(PACK - 1, 1, i, True, f"squared1_{i}")
+                        look_up(PACK - 1, 1, i, True, keep.tile([P, HALF], F32, name=f"squared1_{i}")[:])
                     turn_differences(pieces[6])
                     turn_differences(pieces[7])
                 for step in (make_s, make_pull):
                     for v in range(2):
                         step(v)
                 both = "p v u i f -> p (v u i f)"
-                if n == 2:
-                    quantise_w2()
-                term = keep.tile([P, 2, 2, PARTNERS, P], F32, name="w2_bf" if n == 2 else f"term{n}", align_bytes=64)
-                nc.gpsimd.tensor_tensor(term[:].rearrange(both), s[:].rearrange(both), pull[:].rearrange(both), ALU.mult)
+                term = keep.tile([P, 2, 2, PARTNERS, P], F32, name=f"term{n}", align_bytes=64)
+                if n < 2:
+                    nc.gpsimd.tensor_tensor(term[:].rearrange(both), s[:].rearrange(both), both_pulls[:].rearrange(both), ALU.mult)
+                else:
+                    for v in range(2):
+                        nc.gpsimd.tensor_tensor(term[:, v].rearrange(flat), s[:, v].rearrange(flat), pull[v].rearrange(flat), ALU.mult)
             else:
                 for v in range(2):
                     square(v)
@@ -228,7 +233,7 @@ def tile_picked_ljpot_none_p_kernel(tc, x_words, x_scales, w1, q, gn, w2, offs, 
                     make_pull(v)
                 term = keep.tile([P, 2, 2, PARTNERS, P], F32, name=f"soft{n}", align_bytes=64)
                 for v in range(2):
-                    nc.vector.tensor_tensor(term[:, v].rearrange(flat), s[:, v].rearrange(flat), pull[:, v].rearrange(flat), ALU.mult)
+                    nc.vector.tensor_tensor(term[:, v].rearrange(flat), s[:, v].rearrange(flat), pull[v].rearrange(flat), ALU.mult)
             for v, piece in enumerate(pair):
                 for u, unit in enumerate(piece):
                     terms[unit] = term[:, v, u]
@@ -244,13 +249,17 @@ def tile_picked_ljpot_none_p_kernel(tc, x_words, x_scales, w1, q, gn, w2, offs, 
                 z_bf, minus_gain[:].unsqueeze(1).to_broadcast([P, P, PACK]), back[:].rearrange("p t j -> p j t"), ALU.mult
             )
 
-        def project(cols, z_bf, banks, codes_name):
+        def quantise_z(cols, z_bf, codes_name):
             width = cols.stop - cols.start
-            last = cols.stop == S
-            w2_codes, w2_scale = w2_quantised
             z_codes = keep.tile([P, width], U32, name=codes_name, align_bytes=64)
             z_scale = keep.tile([P, width], U8, name=f"z_scale{cols.start}", align_bytes=64)
             nc.vector.quantize_mx(z_codes[:].bitcast(FP8X4), z_scale[:], z_bf[:].rearrange("p c t -> p (c t)"))
+            return z_codes, z_scale
+
+        def project(cols, quantised_z, banks):
+            width = cols.stop - cols.start
+            last = cols.stop == S
+            z_codes, z_scale = quantised_z
             for half in range(2):
                 out_acc = psum.tile([P, 2, width], F32, name=banks[half])
                 result = keep.tile([P, 2, width], F32, name=f"result{cols.start}_{half}")
@@ -267,14 +276,18 @@ def tile_picked_ljpot_none_p_kernel(tc, x_words, x_scales, w1, q, gn, w2, offs, 
 
         for piece in pieces[:PACK]:
             turn_differences(piece)
+        first = keep.tile([P, HALF], F32, name="gathered00")
+        later = shared.tile([P, 5, HALF], F32, name="later", align_bytes=64, offset=0)
         for t in range(PACK - 1):
             for i in range(PARTNERS):
-                look_up(t, 1, i, False, f"gathered{t}{i}")
-            if t < 2:
-                turn_differences(pieces[PACK + t])
+                look_up(t, 1, i, False, first[:] if (t, i) == (0, 0) else later[:, 2 * t + i - 1, :])
+            if t == 1:
+                turn_differences(pieces[PACK])
+                turn_differences(pieces[PACK + 1])
         for n, pair in enumerate(pairs):
             do_pair(n, pair)
-        z_left = keep.tile([P, HALF, PACK], BF16, name=f"inv_root{len(pairs) - 1}", align_bytes=64)
+        z_planes = keep.tile([P, PACK, HALF], BF16, name=f"inv_root{len(pairs) - 1}", align_bytes=64)
+        z_left = keep.tile([P, HALF, PACK], BF16, name="z_left", align_bytes=64)
         for two in range(2):
             back = psum.tile([P, 2, HALF], F32, name=f"e{2 + two}")
             for u in range(2):
@@ -287,9 +300,15 @@ def tile_picked_ljpot_none_p_kernel(tc, x_words, x_scales, w1, q, gn, w2, offs, 
                         )
             for u in range(2):
                 t = 2 * two + u
-                nc.scalar.activation(z_left[:, :, t], back[:, u, :], ACT.Copy, scale=minus_gain[:, t : t + 1])
-        project(left, z_left, ["e2", "e3"], f"pull{last_pair}")
+                nc.scalar.activation(z_planes[:, t, :], back[:, u, :], ACT.Copy, scale=minus_gain[:, t : t + 1])
+        nc.scalar.copy(
+            z_left[:].rearrange("p (c i) t -> p c t i", i=LINE), z_planes[:].rearrange("p t (c i) -> p c t i", i=LINE)
+        )
+        project(left, quantise_z(left, z_left, f"s{last_pair}"), ["e2", "e3"])
+        z_blocks = {}
         for b in (2, 3):
-            z_block = keep.tile([P, P, PACK], BF16, name=f"z_block{b}", align_bytes=64)
-            turn_back(b, z_block[:])
-            project(block(b), z_block, ["q", "e1"] if b == 2 else ["e6", "e0"], f"z_codes{b}")
+            z_blocks[b] = keep.tile([P, P, PACK], BF16, name=f"pull{last_pair}_{3 - b}", align_bytes=64)
+            turn_back(b, z_blocks[b][:])
+        quantised = {b: quantise_z(block(b), z_blocks[b], f"z_codes{b}") for b in (2, 3)}
+        for b in (2, 3):
+            project(block(b), quantised[b], ["q0", "q1"] if b == 2 else ["e0", "e1"])

@@ -133,7 +133,7 @@ def tile_picked_ljpot_none_p_kernel(tc, x_words, x_scales, w1, q, gn, w2, offs, 
             for i in range(PARTNERS):
                 look_up(t, 0, i, t == PACK - 1, keep.tile([P, HALF], F32, name=f"gathered{t}{i}")[:])
 
-        w2_bf = shared.tile([P, N, PACK], BF16, name="w2_bf", align_bytes=64, offset=3072)
+        w2_bf = shared.tile([P, N, PACK], BF16, name="w2_bf", align_bytes=64, offset=4096)
         for half in range(2):
             nc.gpsimd.tensor_scalar(
                 w2_bf[:, half * (N // 2) : (half + 1) * (N // 2), :],
@@ -169,7 +169,7 @@ def tile_picked_ljpot_none_p_kernel(tc, x_words, x_scales, w1, q, gn, w2, offs, 
         def do_pair(n, pair):
             inv_root = keep.tile([P, 2, 4 * P], F32, name=f"inv_root{n}", align_bytes=64)
             if n == 0:
-                soft = shared.tile([P, 2, 2, PARTNERS, P], F32, name="soft0", align_bytes=64, offset=5120)
+                soft = shared.tile([P, 2, 2, PARTNERS, P], F32, name="soft0", align_bytes=64, offset=6144)
             else:
                 soft = keep.tile([P, 2, 2, PARTNERS, P], F32, name=f"soft{n}", align_bytes=64)
             q_turned = psum.tile([P, 2, 2, P], F32, name=f"q{n % 2}")
@@ -210,8 +210,7 @@ def tile_picked_ljpot_none_p_kernel(tc, x_words, x_scales, w1, q, gn, w2, offs, 
                 else:
                     nc.scalar.activation(soft_flat, inv_root[:], ACT.Square)
                 if n == 1:
-                    for i in range(PARTNERS):
-                        look_up(PACK - 1, 1, i, True, keep.tile([P, HALF], F32, name=f"squared1_{i}")[:])
+                    look_up(PACK - 1, 1, 0, True, keep.tile([P, HALF], F32, name="squared1_1")[:])
                     turn_differences(pieces[6])
                     turn_differences(pieces[7])
                 for step in (make_s, make_pull):
@@ -277,13 +276,14 @@ def tile_picked_ljpot_none_p_kernel(tc, x_words, x_scales, w1, q, gn, w2, offs, 
         for piece in pieces[:PACK]:
             turn_differences(piece)
         first = keep.tile([P, HALF], F32, name="gathered00")
-        later = shared.tile([P, 5, HALF], F32, name="later", align_bytes=64, offset=0)
+        later = shared.tile([P, 6, HALF], F32, name="later", align_bytes=64, offset=0)
         for t in range(PACK - 1):
             for i in range(PARTNERS):
                 look_up(t, 1, i, False, first[:] if (t, i) == (0, 0) else later[:, 2 * t + i - 1, :])
             if t == 1:
                 turn_differences(pieces[PACK])
                 turn_differences(pieces[PACK + 1])
+        look_up(PACK - 1, 1, 1, False, later[:, 5, :])
         for n, pair in enumerate(pairs):
             do_pair(n, pair)
         z_planes = keep.tile([P, PACK, HALF], BF16, name=f"inv_root{len(pairs) - 1}", align_bytes=64)

@@ -238,7 +238,7 @@ def tile_picked_ljpot_none_p_kernel(tc, x_words, x_scales, w1, q, gn, w2, offs, 
                     terms[unit] = term[:, v, u]
 
         def turn_back(b, z_bf):
-            back = psum.tile([P, PACK, P], F32, name=f"e{2 + b}")
+            back = psum.tile([P, PACK, P], F32, name="e4" if b == 2 else "q1")
             for t in range(PACK):
                 for i in range(PARTNERS):
                     nc.tensor.matmul(
@@ -304,6 +304,12 @@ def tile_picked_ljpot_none_p_kernel(tc, x_words, x_scales, w1, q, gn, w2, offs, 
         nc.scalar.copy(
             z_left[:].rearrange("p (c i) t -> p c t i", i=LINE), z_planes[:].rearrange("p t (c i) -> p c t i", i=LINE)
         )
+        idle_bank = psum.tile([P, S], F32, name="q1")
+        for t in range(2):
+            nc.tensor.matmul_mx(
+                idle_bank[:], w1_codes[:, block(t)].bitcast(FP8X4), w1_scale[:, block(t)],
+                x_codes[:].bitcast(FP8X4), x_scale[:], start=True, stop=True,
+            )
         project(left, quantise_z(left, z_left, f"s{last_pair}"), ["e2", "e3"])
         z_blocks = {}
         for b in (2, 3):
@@ -311,4 +317,4 @@ def tile_picked_ljpot_none_p_kernel(tc, x_words, x_scales, w1, q, gn, w2, offs, 
             turn_back(b, z_blocks[b][:])
         quantised = {b: quantise_z(block(b), z_blocks[b], f"z_codes{b}") for b in (2, 3)}
         for b in (2, 3):
-            project(block(b), quantised[b], ["q0", "q1"] if b == 2 else ["e0", "e1"])
+            project(block(b), quantised[b], ["q0", "e5"] if b == 2 else ["e0", "e1"])

@@ -167,7 +167,10 @@ def tile_picked_ljpot_none_p_kernel(tc, x_words, x_scales, w1, q, gn, w2, offs, 
             minus_d.append(e)
 
         def do_pair(n, pair):
-            inv_root = keep.tile([P, 2, 4 * P], F32, name=f"inv_root{n}", align_bytes=64)
+            if n == last_pair:
+                inv_root = shared.tile([P, 2, 4 * P], F32, name="last_root", align_bytes=64, offset=0)
+            else:
+                inv_root = keep.tile([P, 2, 4 * P], F32, name=f"inv_root{n}", align_bytes=64)
             if n == 0:
                 soft = shared.tile([P, 2, 2, PARTNERS, P], F32, name="soft0", align_bytes=64, offset=6144)
             else:
@@ -224,12 +227,14 @@ def tile_picked_ljpot_none_p_kernel(tc, x_words, x_scales, w1, q, gn, w2, offs, 
                     for v in range(2):
                         nc.gpsimd.tensor_tensor(term[:, v].rearrange(flat), s[:, v].rearrange(flat), pull[v].rearrange(flat), ALU.mult)
             else:
+                for step in (square, inverse_root):
+                    for v in range(2):
+                        step(v)
                 for v in range(2):
-                    square(v)
-                    inverse_root(v)
                     nc.scalar.activation(soft[:, v].rearrange(flat), inv_root[:, v], ACT.Square)
-                    make_s(v)
-                    make_pull(v)
+                for step in (make_s, make_pull):
+                    for v in range(2):
+                        step(v)
                 term = keep.tile([P, 2, 2, PARTNERS, P], F32, name=f"soft{n}", align_bytes=64)
                 for v in range(2):
                     nc.vector.tensor_tensor(term[:, v].rearrange(flat), s[:, v].rearrange(flat), pull[v].rearrange(flat), ALU.mult)
@@ -237,13 +242,16 @@ def tile_picked_ljpot_none_p_kernel(tc, x_words, x_scales, w1, q, gn, w2, offs, 
                 for u, unit in enumerate(piece):
                     terms[unit] = term[:, v, u]
 
-        def turn_back(b, z_bf):
+        def turn_back(b):
             back = psum.tile([P, PACK, P], F32, name="e4" if b == 2 else "q1")
             for t in range(PACK):
                 for i in range(PARTNERS):
                     nc.tensor.matmul(
                         back[:, t, :], terms[(t, b)][:, i, :], ident[:], start=(i == 0), stop=(i == PARTNERS - 1), is_transpose=True
                     )
+            return back
+
+        def make_z(back, z_bf):
             nc.vector.tensor_tensor(
                 z_bf, minus_gain[:].unsqueeze(1).to_broadcast([P, P, PACK]), back[:].rearrange("p t j -> p j t"), ALU.mult
             )
@@ -286,7 +294,7 @@ def tile_picked_ljpot_none_p_kernel(tc, x_words, x_scales, w1, q, gn, w2, offs, 
         look_up(PACK - 1, 1, 1, False, later[:, 5, :])
         for n, pair in enumerate(pairs):
             do_pair(n, pair)
-        z_planes = keep.tile([P, PACK, HALF], BF16, name=f"inv_root{len(pairs) - 1}", align_bytes=64)
+        z_planes = shared.tile([P, PACK, HALF], BF16, name="z_planes", align_bytes=64, offset=0)
         z_left = keep.tile([P, HALF, PACK], BF16, name="z_left", align_bytes=64)
         for two in range(2):
             back = psum.tile([P, 2, HALF], F32, name=f"e{2 + two}")
@@ -310,11 +318,13 @@ def tile_picked_ljpot_none_p_kernel(tc, x_words, x_scales, w1, q, gn, w2, offs, 
                 idle_bank[:], w1_codes[:, block(t)].bitcast(FP8X4), w1_scale[:, block(t)],
                 x_codes[:].bitcast(FP8X4), x_scale[:], start=True, stop=True,
             )
-        project(left, quantise_z(left, z_left, f"s{last_pair}"), ["e2", "e3"])
-        z_blocks = {}
+        backs = {b: turn_back(b) for b in (2, 3)}
+        z_blocks = {b: keep.tile([P, P, PACK], BF16, name=f"pull{last_pair}_{3 - b}", align_bytes=64) for b in (2, 3)}
+        make_z(backs[2], z_blocks[2][:])
+        quantised = {0: quantise_z(left, z_left, f"s{last_pair}")}
+        make_z(backs[3], z_blocks[3][:])
         for b in (2, 3):
-            z_blocks[b] = keep.tile([P, P, PACK], BF16, name=f"pull{last_pair}_{3 - b}", align_bytes=64)
-            turn_back(b, z_blocks[b][:])
-        quantised = {b: quantise_z(block(b), z_blocks[b], f"z_codes{b}") for b in (2, 3)}
+            quantised[b] = quantise_z(block(b), z_blocks[b], f"z_codes{b}")
+        project(left, quantised[0], ["e2", "e3"])
         for b in (2, 3):
             project(block(b), quantised[b], ["q0", "e5"] if b == 2 else ["e0", "e1"])

@@ -30,8 +30,6 @@ def tile_picked_ljpot_none_p_kernel(tc, x_words, x_scales, w1, q, gn, w2, offs, 
     left, right = slice(0, HALF), slice(HALF, S)
     with ExitStack() as ctx:
         keep = ctx.enter_context(tc.tile_pool(name="keep", bufs=1))
-        work = ctx.enter_context(tc.tile_pool(name="work", bufs=4))
-        shared = ctx.enter_context(tc.tile_pool(name="shared", bufs=1))
         psum = ctx.enter_context(tc.psum_pool(name="psum", bufs=1))
 
         def load_list(name, source):
@@ -78,11 +76,15 @@ def tile_picked_ljpot_none_p_kernel(tc, x_words, x_scales, w1, q, gn, w2, offs, 
         nc.vector.tensor_copy(x_codes[:], x_word_table[:].bitcast(U32).indirect(picks[:]))
 
         w1_bf = keep.tile([P, PACK, P, PACK], BF16, name="w1_bf", align_bytes=64)
-        for m0, m1, cast in ((0, 64, nc.scalar.copy), (64, 88, nc.scalar.copy), (88, P, nc.vector.tensor_copy)):
-            half, base = divmod(m0, P // 2)
+        for half, t0, t1, cast in (
+            (0, 0, PACK, nc.scalar.copy),
+            (1, 0, 1, nc.vector.tensor_copy),
+            (1, 1, 2, nc.vector.tensor_copy),
+            (1, 2, PACK, nc.scalar.copy),
+        ):
             cast(
-                w1_bf[:, :, m0:m1, :].rearrange("p t m j -> p m j t"),
-                w1_raw[half][:].rearrange("p j (m t) -> p m j t", t=PACK)[:, base : base + m1 - m0],
+                w1_bf[:, t0:t1, half * (P // 2) : (half + 1) * (P // 2), :].rearrange("p t m j -> p m j t"),
+                w1_raw[half][:].rearrange("p j (m t) -> p m j t", t=PACK)[:, :, :, t0:t1],
             )
         w1_codes = keep.tile([P, H], U32, name="w1_codes", align_bytes=64)
         w1_scale = keep.tile([P, H], U8, name="w1_scale", align_bytes=64)
@@ -104,18 +106,18 @@ def tile_picked_ljpot_none_p_kernel(tc, x_words, x_scales, w1, q, gn, w2, offs, 
         nc.vector.tensor_scalar(minus_gain[:], gain[:], -1.0, None, ALU.mult)
 
         y = [keep.tile([P, S], F32, name=f"y{t}") for t in range(PACK)]
-        y_banks = ["e3", "e4", "q0", "q1", "e5"]
+        y_banks = ["e1", "e2", "e3", "e4", "q0", "q1", "e5"]
         bank = 0
         for t in range(PACK):
             feats = slice(t * P, (t + 1) * P)
-            for cols in (left, right) if t == 0 else (slice(0, S),):
+            for cols in [slice(b * P, (b + 1) * P) for b in range(PACK)] if t == 0 else [slice(0, S)]:
                 y_acc = psum.tile([P, cols.stop - cols.start], F32, name=y_banks[bank])
                 bank += 1
                 nc.tensor.matmul_mx(
                     y_acc[:], w1_codes[:, feats].bitcast(FP8X4), w1_scale[:, feats],
                     x_codes[:, cols].bitcast(FP8X4), x_scale[:, cols], start=True, stop=True,
                 )
-                copy_out = nc.vector.tensor_copy if t == 0 and cols == right else nc.scalar.copy
+                copy_out = nc.vector.tensor_copy if t == 0 and bank % 2 == 1 else nc.scalar.copy
                 copy_out(y[t][:, cols], y_acc[:])
 
         minus_partner = {}
@@ -131,9 +133,9 @@ def tile_picked_ljpot_none_p_kernel(tc, x_words, x_scales, w1, q, gn, w2, offs, 
 
         for t in range(PACK):
             for i in range(PARTNERS):
-                look_up(t, 0, i, t == PACK - 1, keep.tile([P, HALF], F32, name=f"gathered{t}{i}")[:])
+                look_up(t, 0, i, t == 2, keep.tile([P, HALF], F32, name=f"gathered{t}{i}")[:])
 
-        w2_bf = shared.tile([P, N, PACK], BF16, name="w2_bf", align_bytes=64, offset=4096)
+        w2_bf = keep.tile([P, N, PACK], BF16, name="w2_bf", align_bytes=64)
         for half in range(2):
             nc.gpsimd.tensor_scalar(
                 w2_bf[:, half * (N // 2) : (half + 1) * (N // 2), :],
@@ -168,11 +170,11 @@ def tile_picked_ljpot_none_p_kernel(tc, x_words, x_scales, w1, q, gn, w2, offs, 
 
         def do_pair(n, pair):
             if n == last_pair:
-                inv_root = shared.tile([P, 2, 4 * P], F32, name="last_root", align_bytes=64, offset=0)
+                inv_root = keep.tile([P, 2, 4 * P], F32, name="stage0")
             else:
                 inv_root = keep.tile([P, 2, 4 * P], F32, name=f"inv_root{n}", align_bytes=64)
             if n == 0:
-                soft = shared.tile([P, 2, 2, PARTNERS, P], F32, name="soft0", align_bytes=64, offset=6144)
+                soft = keep.tile([P, 2, 2, PARTNERS, P], F32, name="w2_bf", align_bytes=64)
             else:
                 soft = keep.tile([P, 2, 2, PARTNERS, P], F32, name=f"soft{n}", align_bytes=64)
             q_turned = psum.tile([P, 2, 2, P], F32, name=f"q{n % 2}")
@@ -284,7 +286,7 @@ def tile_picked_ljpot_none_p_kernel(tc, x_words, x_scales, w1, q, gn, w2, offs, 
         for piece in pieces[:PACK]:
             turn_differences(piece)
         first = keep.tile([P, HALF], F32, name="gathered00")
-        later = shared.tile([P, 6, HALF], F32, name="later", align_bytes=64, offset=0)
+        later = keep.tile([P, 6, HALF], F32, name="stage0")
         for t in range(PACK - 1):
             for i in range(PARTNERS):
                 look_up(t, 1, i, False, first[:] if (t, i) == (0, 0) else later[:, 2 * t + i - 1, :])
@@ -294,7 +296,7 @@ def tile_picked_ljpot_none_p_kernel(tc, x_words, x_scales, w1, q, gn, w2, offs, 
         look_up(PACK - 1, 1, 1, False, later[:, 5, :])
         for n, pair in enumerate(pairs):
             do_pair(n, pair)
-        z_planes = shared.tile([P, PACK, HALF], BF16, name="z_planes", align_bytes=64, offset=0)
+        z_planes = keep.tile([P, PACK, HALF], BF16, name="stage0")
         z_left = keep.tile([P, HALF, PACK], BF16, name="z_left", align_bytes=64)
         for two in range(2):
             back = psum.tile([P, 2, HALF], F32, name=f"e{2 + two}")

@@ -20,7 +20,6 @@ P = 128
 PACK = 4
 GROUP = 16
 QUADRANT = 32
-LINE = 4
 PARTNERS = 2
 HALF = S // 2
 
@@ -30,6 +29,7 @@ def tile_picked_ljpot_none_p_kernel(tc, x_words, x_scales, w1, q, gn, w2, offs, 
     left, right = slice(0, HALF), slice(HALF, S)
     with ExitStack() as ctx:
         keep = ctx.enter_context(tc.tile_pool(name="keep", bufs=1))
+        shared = ctx.enter_context(tc.tile_pool(name="shared", bufs=1))
         psum = ctx.enter_context(tc.psum_pool(name="psum", bufs=1))
 
         def load_list(name, source):
@@ -133,7 +133,10 @@ def tile_picked_ljpot_none_p_kernel(tc, x_words, x_scales, w1, q, gn, w2, offs, 
 
         for t in range(PACK):
             for i in range(PARTNERS):
-                look_up(t, 0, i, t == 2, keep.tile([P, HALF], F32, name=f"gathered{t}{i}")[:])
+                look_up(t, 0, i, False, keep.tile([P, HALF], F32, name=f"gathered{t}{i}")[:])
+        both_partners = shared.tile([P, PARTNERS, HALF], F32, name="both_partners", align_bytes=64, offset=2048)
+        for i in range(PARTNERS):
+            look_up(2, 1, i, True, both_partners[:, i, :])
 
         w2_bf = keep.tile([P, N, PACK], BF16, name="w2_bf", align_bytes=64)
         for half in range(2):
@@ -143,7 +146,9 @@ def tile_picked_ljpot_none_p_kernel(tc, x_words, x_scales, w1, q, gn, w2, offs, 
                 1.0, 0.0, ALU.mult, ALU.add,
             )
 
-        w2_codes = keep.tile([P, N], U32, name="w2_codes", align_bytes=64)
+        made = keep.tile([P, PARTNERS, HALF], F32, name="stage0")
+        nc.gpsimd.tensor_tensor(made[:], y[2][:, right].unsqueeze(1).to_broadcast([P, PARTNERS, HALF]), both_partners[:], ALU.add)
+        w2_codes = shared.tile([P, N], U32, name="w2_codes", align_bytes=64, offset=1024)
         w2_scale = keep.tile([P, N], U8, name="w2_scale", align_bytes=64)
         nc.vector.quantize_mx(w2_codes[:].bitcast(FP8X4), w2_scale[:], w2_bf[:].rearrange("p m j -> p (m j)"))
 
@@ -161,26 +166,34 @@ def tile_picked_ljpot_none_p_kernel(tc, x_words, x_scales, w1, q, gn, w2, offs, 
         minus_d = []
 
         def turn_differences(piece):
-            e = psum.tile([P, 2, PARTNERS, P], F32, name=f"e{len(minus_d) % 6}")
+            e = psum.tile([P, 2, PARTNERS, P], F32, name=("e0", "e1", "e2", "e3", "e4", "e5", "q0", "e1")[len(minus_d)])
             for i in range(PARTNERS):
                 for u, (t, b) in enumerate(piece):
+                    if t == 2 and b >= 2:
+                        nc.tensor.transpose(e[:, u, i, :], made[:, i, block(b - 2)], ident[:])
+                        continue
                     nc.tensor.matmul(e[:, u, i, :], y[t][:, block(b)], ident[:], start=True, stop=False, is_transpose=True)
                     nc.tensor.matmul(e[:, u, i, :], minus_partner[(t, b, i)], ident[:], start=False, stop=True, is_transpose=True)
             minus_d.append(e)
 
+        turned = {}
+
+        def turn_q(n):
+            turned[n] = psum.tile([P, 2, 2, P], F32, name=("q0", "q1", "e0", "q1")[n])
+            for v, piece in enumerate(pairs[n]):
+                for u, (t, b) in enumerate(piece):
+                    nc.tensor.transpose(turned[n][:, v, u, :], strength[t][:, block(b)], ident[:])
+
         def do_pair(n, pair):
             if n == last_pair:
-                inv_root = keep.tile([P, 2, 4 * P], F32, name="stage0")
+                inv_root = shared.tile([P, 2, 4 * P], F32, name="last_root", align_bytes=64, offset=4096)
             else:
                 inv_root = keep.tile([P, 2, 4 * P], F32, name=f"inv_root{n}", align_bytes=64)
             if n == 0:
                 soft = keep.tile([P, 2, 2, PARTNERS, P], F32, name="w2_bf", align_bytes=64)
             else:
                 soft = keep.tile([P, 2, 2, PARTNERS, P], F32, name=f"soft{n}", align_bytes=64)
-            q_turned = psum.tile([P, 2, 2, P], F32, name=f"q{n % 2}")
-            for v, piece in enumerate(pair):
-                for u, (t, b) in enumerate(piece):
-                    nc.tensor.transpose(q_turned[:, v, u, :], strength[t][:, block(b)], ident[:])
+            q_turned = turned[n]
             squared = [keep.tile([P, 4 * P], F32, name=f"squared{n}_{v}") for v in range(2)]
             s = keep.tile([P, 2, 2, PARTNERS, P], F32, name="soft1" if n == 2 else f"s{n}", align_bytes=64)
             if n < last_pair:
@@ -213,14 +226,18 @@ def tile_picked_ljpot_none_p_kernel(tc, x_words, x_scales, w1, q, gn, w2, offs, 
                 if n < 2:
                     nc.gpsimd.tensor_tensor(soft_flat, inv_root[:], inv_root[:], ALU.mult)
                 else:
-                    nc.scalar.activation(soft_flat, inv_root[:], ACT.Square)
+                    for v in range(2):
+                        nc.scalar.activation(soft_flat[:, v], inv_root[:, v], ACT.Square)
                 if n == 1:
                     look_up(PACK - 1, 1, 0, True, keep.tile([P, HALF], F32, name="squared1_1")[:])
                     turn_differences(pieces[6])
+                    turn_q(2)
                     turn_differences(pieces[7])
                 for step in (make_s, make_pull):
                     for v in range(2):
                         step(v)
+                if n == 1:
+                    turn_q(3)
                 both = "p v u i f -> p (v u i f)"
                 term = keep.tile([P, 2, 2, PARTNERS, P], F32, name=f"term{n}", align_bytes=64)
                 if n < 2:
@@ -285,18 +302,16 @@ def tile_picked_ljpot_none_p_kernel(tc, x_words, x_scales, w1, q, gn, w2, offs, 
 
         for piece in pieces[:PACK]:
             turn_differences(piece)
-        first = keep.tile([P, HALF], F32, name="gathered00")
-        later = keep.tile([P, 6, HALF], F32, name="stage0")
-        for t in range(PACK - 1):
-            for i in range(PARTNERS):
-                look_up(t, 1, i, False, first[:] if (t, i) == (0, 0) else later[:, 2 * t + i - 1, :])
-            if t == 1:
-                turn_differences(pieces[PACK])
-                turn_differences(pieces[PACK + 1])
-        look_up(PACK - 1, 1, 1, False, later[:, 5, :])
+        turn_q(0)
+        later = shared.tile([P, 5, HALF], F32, name="later", align_bytes=64, offset=3072)
+        for n, (t, i) in enumerate(((0, 0), (1, 0), (0, 1), (1, 1), (3, 1))):
+            look_up(t, 1, i, False, later[:, n, :])
+        turn_differences(pieces[PACK])
+        turn_differences(pieces[PACK + 1])
+        turn_q(1)
         for n, pair in enumerate(pairs):
             do_pair(n, pair)
-        z_planes = keep.tile([P, PACK, HALF], BF16, name="stage0")
+        z_pairs = shared.tile([P, 2, HALF, 2], BF16, name="z_pairs", align_bytes=64, offset=4096)
         z_left = keep.tile([P, HALF, PACK], BF16, name="z_left", align_bytes=64)
         for two in range(2):
             back = psum.tile([P, 2, HALF], F32, name=f"e{2 + two}")
@@ -310,9 +325,10 @@ def tile_picked_ljpot_none_p_kernel(tc, x_words, x_scales, w1, q, gn, w2, offs, 
                         )
             for u in range(2):
                 t = 2 * two + u
-                nc.scalar.activation(z_planes[:, t, :], back[:, u, :], ACT.Copy, scale=minus_gain[:, t : t + 1])
+                nc.scalar.activation(z_pairs[:, two, :, u], back[:, u, :], ACT.Copy, scale=minus_gain[:, t : t + 1])
         nc.scalar.copy(
-            z_left[:].rearrange("p (c i) t -> p c t i", i=LINE), z_planes[:].rearrange("p t (c i) -> p c t i", i=LINE)
+            z_left[:].rearrange("p j t -> p (j t)").bitcast(U32).rearrange("p (j h) -> p j h", h=2),
+            z_pairs[:].rearrange("p h j e -> p (h j e)").bitcast(U32).rearrange("p (h j) -> p j h", h=2),
         )
         idle_bank = psum.tile([P, S], F32, name="q1")
         for t in range(2):

@@ -29,7 +29,6 @@ def tile_picked_ljpot_none_p_kernel(tc, x_words, x_scales, w1, q, gn, w2, offs, 
     left, right = slice(0, HALF), slice(HALF, S)
     with ExitStack() as ctx:
         keep = ctx.enter_context(tc.tile_pool(name="keep", bufs=1))
-        shared = ctx.enter_context(tc.tile_pool(name="shared", bufs=1))
         psum = ctx.enter_context(tc.psum_pool(name="psum", bufs=1))
 
         def load_list(name, source):
@@ -120,6 +119,12 @@ def tile_picked_ljpot_none_p_kernel(tc, x_words, x_scales, w1, q, gn, w2, offs, 
                 copy_out = nc.vector.tensor_copy if t == 0 and bank % 2 == 1 else nc.scalar.copy
                 copy_out(y[t][:, cols], y_acc[:])
 
+        def block(b):
+            return slice(b * P, (b + 1) * P)
+
+        def floats(name, *shape):
+            return keep.tile([P, *shape], F32, name=name, align_bytes=64)
+
         minus_partner = {}
 
         def look_up(t, h, i, on_scalar, gathered):
@@ -131,149 +136,61 @@ def tile_picked_ljpot_none_p_kernel(tc, x_words, x_scales, w1, q, gn, w2, offs, 
             for b in range(2):
                 minus_partner[(t, 2 * h + b, i)] = gathered[:, b * P : (b + 1) * P]
 
-        for t in range(PACK):
-            for i in range(PARTNERS):
-                look_up(t, 0, i, False, keep.tile([P, HALF], F32, name=f"gathered{t}{i}")[:])
-        both_partners = shared.tile([P, PARTNERS, HALF], F32, name="both_partners", align_bytes=64, offset=2048)
-        for i in range(PARTNERS):
-            look_up(2, 1, i, True, both_partners[:, i, :])
-
-        w2_bf = keep.tile([P, N, PACK], BF16, name="w2_bf", align_bytes=64)
-        for half in range(2):
-            nc.gpsimd.tensor_scalar(
-                w2_bf[:, half * (N // 2) : (half + 1) * (N // 2), :],
-                w2_raw[:, :, half * (N // 2) : (half + 1) * (N // 2)].rearrange("p j m -> p m j"),
-                1.0, 0.0, ALU.mult, ALU.add,
-            )
-
-        made = keep.tile([P, PARTNERS, HALF], F32, name="stage0")
-        nc.gpsimd.tensor_tensor(made[:], y[2][:, right].unsqueeze(1).to_broadcast([P, PARTNERS, HALF]), both_partners[:], ALU.add)
-        w2_codes = shared.tile([P, N], U32, name="w2_codes", align_bytes=64, offset=1024)
-        w2_scale = keep.tile([P, N], U8, name="w2_scale", align_bytes=64)
-        nc.vector.quantize_mx(w2_codes[:].bitcast(FP8X4), w2_scale[:], w2_bf[:].rearrange("p m j -> p (m j)"))
-
         pieces = [[(t, 0), (t, 1)] for t in range(PACK)] + [[(t, b), (t + 1, b)] for t in (0, 2) for b in (2, 3)]
-        pairs = [pieces[n : n + 2] for n in range(0, len(pieces), 2)]
-        out_rows = out.rearrange("(mt p) j -> p mt j", p=P)
-
-        def block(b):
-            return slice(b * P, (b + 1) * P)
-
-        terms = {}
-
         flat = "p u i f -> p (u i f)"
-        last_pair = len(pairs) - 1
-        minus_d = []
+        both = "p v u i f -> p (v u i f)"
+        piece_shape = (2, PARTNERS, P)
+        minus_d, q_turned, squared, inv_root, soft, s, pull, terms = {}, {}, {}, {}, {}, {}, {}, {}
 
-        def turn_differences(piece):
-            e = psum.tile([P, 2, PARTNERS, P], F32, name=("e0", "e1", "e2", "e3", "e4", "e5", "q0", "e1")[len(minus_d)])
+        def pair_tiles(store, first, name):
+            pair = floats(name, 2, *piece_shape)
+            store[first], store[first + 1] = pair[:, 0], pair[:, 1]
+            return pair
+
+        def turn_differences(k, bank_name):
+            minus_d[k] = psum.tile([P, *piece_shape], F32, name=bank_name)
             for i in range(PARTNERS):
-                for u, (t, b) in enumerate(piece):
-                    if t == 2 and b >= 2:
-                        nc.tensor.transpose(e[:, u, i, :], made[:, i, block(b - 2)], ident[:])
-                        continue
-                    nc.tensor.matmul(e[:, u, i, :], y[t][:, block(b)], ident[:], start=True, stop=False, is_transpose=True)
-                    nc.tensor.matmul(e[:, u, i, :], minus_partner[(t, b, i)], ident[:], start=False, stop=True, is_transpose=True)
-            minus_d.append(e)
+                for u, (t, b) in enumerate(pieces[k]):
+                    nc.tensor.matmul(minus_d[k][:, u, i, :], y[t][:, block(b)], ident[:], start=True, stop=False, is_transpose=True)
+                    nc.tensor.matmul(minus_d[k][:, u, i, :], minus_partner[(t, b, i)], ident[:], start=False, stop=True, is_transpose=True)
 
-        turned = {}
+        def turn_q(first, bank_name):
+            pair = psum.tile([P, 2, 2, P], F32, name=bank_name)
+            for v in range(2):
+                for u, (t, b) in enumerate(pieces[first + v]):
+                    nc.tensor.transpose(pair[:, v, u, :], strength[t][:, block(b)], ident[:])
+                q_turned[first + v] = pair[:, v]
 
-        def turn_q(n):
-            turned[n] = psum.tile([P, 2, 2, P], F32, name=("q0", "q1", "e0", "q1")[n])
-            for v, piece in enumerate(pairs[n]):
-                for u, (t, b) in enumerate(piece):
-                    nc.tensor.transpose(turned[n][:, v, u, :], strength[t][:, block(b)], ident[:])
+        def square(k):
+            squared[k] = floats(f"squared{k}", *piece_shape)
+            nc.scalar.activation(squared[k][:].rearrange(flat), minus_d[k][:].rearrange(flat), ACT.Square)
 
-        def do_pair(n, pair):
-            if n == last_pair:
-                inv_root = shared.tile([P, 2, 4 * P], F32, name="last_root", align_bytes=64, offset=4096)
+        def inverse_root(k, name=None):
+            if name:
+                inv_root[k] = floats(name, *piece_shape)[:]
+            nc.scalar.activation(inv_root[k].rearrange(flat), squared[k][:].rearrange(flat), ACT.Abs_reciprocal_sqrt, bias=one[:])
+
+        def soften(k):
+            root_k = inv_root[k].rearrange(flat)
+            if k < PACK:
+                nc.gpsimd.tensor_tensor(soft[k].rearrange(flat), root_k, root_k, ALU.mult)
             else:
-                inv_root = keep.tile([P, 2, 4 * P], F32, name=f"inv_root{n}", align_bytes=64)
-            if n == 0:
-                soft = keep.tile([P, 2, 2, PARTNERS, P], F32, name="w2_bf", align_bytes=64)
-            else:
-                soft = keep.tile([P, 2, 2, PARTNERS, P], F32, name=f"soft{n}", align_bytes=64)
-            q_turned = turned[n]
-            squared = [keep.tile([P, 4 * P], F32, name=f"squared{n}_{v}") for v in range(2)]
-            s = keep.tile([P, 2, 2, PARTNERS, P], F32, name="soft1" if n == 2 else f"s{n}", align_bytes=64)
-            if n < last_pair:
-                both_pulls = keep.tile([P, 2, 2, PARTNERS, P], F32, name=f"pull{n}", align_bytes=64)
-                pull = [both_pulls[:, v] for v in range(2)]
-            else:
-                pull = [keep.tile([P, 2, PARTNERS, P], F32, name=f"pull{n}_{v}", align_bytes=64)[:] for v in range(2)]
+                nc.scalar.activation(soft[k].rearrange(flat), root_k, ACT.Square)
 
-            def square(v):
-                nc.scalar.activation(squared[v][:], minus_d[2 * n + v][:].rearrange(flat), ACT.Square)
-
-            def inverse_root(v):
-                nc.scalar.activation(inv_root[:, v], squared[v][:], ACT.Abs_reciprocal_sqrt, bias=one[:])
-
-            def make_s(v):
-                q_both = q_turned[:, v].unsqueeze(2).to_broadcast([P, 2, PARTNERS, P])
-                nc.vector.tensor_tensor(s[:, v], soft[:, v], q_both, ALU.mult)
-
-            def make_pull(v):
+        def products(first, s_name, pull_name):
+            s_pair = pair_tiles(s, first, s_name)
+            for k in (first, first + 1):
+                nc.vector.tensor_tensor(s[k], soft[k], q_turned[k].unsqueeze(2).to_broadcast([P, *piece_shape]), ALU.mult)
+            pull_pair = pair_tiles(pull, first, pull_name)
+            for k in (first, first + 1):
                 nc.vector.scalar_tensor_tensor(
-                    pull[v].rearrange(flat), s[:, v].rearrange(flat), 1.0, minus_d[2 * n + v][:].rearrange(flat),
-                    ALU.subtract, ALU.mult,
+                    pull[k].rearrange(flat), s[k].rearrange(flat), 1.0, minus_d[k][:].rearrange(flat), ALU.subtract, ALU.mult
                 )
+            return s_pair, pull_pair
 
-            if n < last_pair:
-                for step in (square, inverse_root):
-                    for v in range(2):
-                        step(v)
-                soft_flat = soft[:].rearrange("p v u i f -> p v (u i f)")
-                if n < 2:
-                    nc.gpsimd.tensor_tensor(soft_flat, inv_root[:], inv_root[:], ALU.mult)
-                else:
-                    for v in range(2):
-                        nc.scalar.activation(soft_flat[:, v], inv_root[:, v], ACT.Square)
-                if n == 1:
-                    look_up(PACK - 1, 1, 0, True, keep.tile([P, HALF], F32, name="squared1_1")[:])
-                    turn_differences(pieces[6])
-                    turn_q(2)
-                    turn_differences(pieces[7])
-                for step in (make_s, make_pull):
-                    for v in range(2):
-                        step(v)
-                if n == 1:
-                    turn_q(3)
-                both = "p v u i f -> p (v u i f)"
-                term = keep.tile([P, 2, 2, PARTNERS, P], F32, name=f"term{n}", align_bytes=64)
-                if n < 2:
-                    nc.gpsimd.tensor_tensor(term[:].rearrange(both), s[:].rearrange(both), both_pulls[:].rearrange(both), ALU.mult)
-                else:
-                    for v in range(2):
-                        nc.gpsimd.tensor_tensor(term[:, v].rearrange(flat), s[:, v].rearrange(flat), pull[v].rearrange(flat), ALU.mult)
-            else:
-                for step in (square, inverse_root):
-                    for v in range(2):
-                        step(v)
-                for v in range(2):
-                    nc.scalar.activation(soft[:, v].rearrange(flat), inv_root[:, v], ACT.Square)
-                for step in (make_s, make_pull):
-                    for v in range(2):
-                        step(v)
-                term = keep.tile([P, 2, 2, PARTNERS, P], F32, name=f"soft{n}", align_bytes=64)
-                for v in range(2):
-                    nc.vector.tensor_tensor(term[:, v].rearrange(flat), s[:, v].rearrange(flat), pull[v].rearrange(flat), ALU.mult)
-            for v, piece in enumerate(pair):
-                for u, unit in enumerate(piece):
-                    terms[unit] = term[:, v, u]
-
-        def turn_back(b):
-            back = psum.tile([P, PACK, P], F32, name="e4" if b == 2 else "q1")
-            for t in range(PACK):
-                for i in range(PARTNERS):
-                    nc.tensor.matmul(
-                        back[:, t, :], terms[(t, b)][:, i, :], ident[:], start=(i == 0), stop=(i == PARTNERS - 1), is_transpose=True
-                    )
-            return back
-
-        def make_z(back, z_bf):
-            nc.vector.tensor_tensor(
-                z_bf, minus_gain[:].unsqueeze(1).to_broadcast([P, P, PACK]), back[:].rearrange("p t j -> p j t"), ALU.mult
-            )
+        def turn_back(summed, k, u):
+            for i in range(PARTNERS):
+                nc.tensor.matmul(summed, terms[k][:, u, i, :], ident[:], start=(i == 0), stop=(i == PARTNERS - 1), is_transpose=True)
 
         def quantise_z(cols, z_bf, codes_name):
             width = cols.stop - cols.start
@@ -281,6 +198,8 @@ def tile_picked_ljpot_none_p_kernel(tc, x_words, x_scales, w1, q, gn, w2, offs, 
             z_scale = keep.tile([P, width], U8, name=f"z_scale{cols.start}", align_bytes=64)
             nc.vector.quantize_mx(z_codes[:].bitcast(FP8X4), z_scale[:], z_bf[:].rearrange("p c t -> p (c t)"))
             return z_codes, z_scale
+
+        out_rows = out.rearrange("(mt p) j -> p mt j", p=P)
 
         def project(cols, quantised_z, banks):
             width = cols.stop - cols.start
@@ -290,7 +209,7 @@ def tile_picked_ljpot_none_p_kernel(tc, x_words, x_scales, w1, q, gn, w2, offs, 
                 out_acc = psum.tile([P, 2, width], F32, name=banks[half])
                 result = keep.tile([P, 2, width], F32, name=f"result{cols.start}_{half}")
                 for u in range(2):
-                    rows = slice((2 * half + u) * P, (2 * half + u + 1) * P)
+                    rows = block(2 * half + u)
                     nc.tensor.matmul_mx(
                         out_acc[:, u, :], w2_codes[:, rows].bitcast(FP8X4), w2_scale[:, rows],
                         z_codes[:].bitcast(FP8X4), z_scale[:], start=True, stop=True,
@@ -300,32 +219,86 @@ def tile_picked_ljpot_none_p_kernel(tc, x_words, x_scales, w1, q, gn, w2, offs, 
                 queue = nc.scalar if last and half == 0 else nc.sync
                 queue.dma_start(out_rows[:, 2 * half : 2 * half + 2, cols], result[:])
 
-        for piece in pieces[:PACK]:
-            turn_differences(piece)
-        turn_q(0)
-        later = shared.tile([P, 5, HALF], F32, name="later", align_bytes=64, offset=3072)
-        for n, (t, i) in enumerate(((0, 0), (1, 0), (0, 1), (1, 1), (3, 1))):
+        for t in range(PACK):
+            for i in range(PARTNERS):
+                look_up(t, 0, i, t == 2, floats(f"gathered{t}{i}", HALF)[:])
+        for k in range(PACK):
+            turn_differences(k, f"e{k}")
+        turn_q(0, "q0")
+
+        w2_bf = keep.tile([P, N, PACK], BF16, name="w2_bf", align_bytes=64)
+        for half in range(2):
+            nc.gpsimd.tensor_scalar(
+                w2_bf[:, half * (N // 2) : (half + 1) * (N // 2), :],
+                w2_raw[:, :, half * (N // 2) : (half + 1) * (N // 2)].rearrange("p j m -> p m j"),
+                1.0, 0.0, ALU.mult, ALU.add,
+            )
+        w2_codes = keep.tile([P, N], U32, name="w2_codes", align_bytes=64)
+        w2_scale = keep.tile([P, N], U8, name="w2_scale", align_bytes=64)
+        nc.vector.quantize_mx(w2_codes[:].bitcast(FP8X4), w2_scale[:], w2_bf[:].rearrange("p m j -> p (m j)"))
+
+        look_up(0, 1, 0, False, floats("gathered00", HALF)[:])
+        later = keep.tile([P, 5, HALF], F32, name="stage0")
+        for n, (t, i) in enumerate(((1, 0), (0, 1), (1, 1), (3, 0), (3, 1))):
             look_up(t, 1, i, False, later[:, n, :])
-        turn_differences(pieces[PACK])
-        turn_differences(pieces[PACK + 1])
-        turn_q(1)
-        for n, pair in enumerate(pairs):
-            do_pair(n, pair)
-        z_pairs = shared.tile([P, 2, HALF, 2], BF16, name="z_pairs", align_bytes=64, offset=4096)
+        turn_differences(4, "e4")
+        turn_differences(5, "e5")
+        turn_q(2, "q1")
+
+        pair_tiles(soft, 0, "w2_bf")
+        pair_tiles(soft, 2, "soft2")
+        square(0)
+        look_up(2, 1, 0, True, floats("gathered01", HALF)[:])
+        inverse_root(0, "inv_root0")
+        soften(0)
+        for k, name in ((1, "gathered21"), (2, "gathered31")):
+            if k == 1:
+                square(k)
+            square(k + 1)
+            inverse_root(k, name)
+            soften(k)
+        inverse_root(3, "inv_root3")
+        soften(3)
+        look_up(2, 1, 1, True, floats("squared2", HALF)[:])
+
+        first_products = products(0, "s0", "gathered21")
+        turn_differences(6, "q0")
+        turn_q(4, "e0")
+        turn_differences(7, "e1")
+        second_products = products(2, "s2", "inv_root3")
+        turn_q(6, "q1")
+        for first, (s_pair, pull_pair), name in ((0, first_products, "squared3"), (2, second_products, "term2")):
+            term_pair = pair_tiles(terms, first, name)
+            nc.gpsimd.tensor_tensor(term_pair[:].rearrange(both), s_pair[:].rearrange(both), pull_pair[:].rearrange(both), ALU.mult)
+
+        for first in (4, 6):
+            for k in (first, first + 1):
+                square(k)
+            if first == 4:
+                pair_tiles(inv_root, first, "inv_root4")
+            else:
+                last_roots = keep.tile([P, 2, *piece_shape], F32, name="stage0")
+                inv_root[6], inv_root[7] = last_roots[:, 0], last_roots[:, 1]
+            pair_tiles(soft, first, f"soft{first}")
+            for step in (inverse_root, soften):
+                for k in (first, first + 1):
+                    step(k)
+            products(first, "soft2" if first == 4 else "s6", f"pull{first}")
+            pair_tiles(terms, first, "term4" if first == 4 else "soft6")
+            engine = nc.gpsimd if first == 4 else nc.vector
+            for k in (first, first + 1):
+                engine.tensor_tensor(terms[k].rearrange(flat), s[k].rearrange(flat), pull[k].rearrange(flat), ALU.mult)
+
+        z_pairs = keep.tile([P, 2, HALF, 2], BF16, name="stage0")
         z_left = keep.tile([P, HALF, PACK], BF16, name="z_left", align_bytes=64)
         for two in range(2):
             back = psum.tile([P, 2, HALF], F32, name=f"e{2 + two}")
-            for u in range(2):
-                t = 2 * two + u
+            for e in range(2):
                 for b in range(2):
-                    for i in range(PARTNERS):
-                        nc.tensor.matmul(
-                            back[:, u, block(b)], terms[(t, b)][:, i, :], ident[:],
-                            start=(i == 0), stop=(i == PARTNERS - 1), is_transpose=True,
-                        )
-            for u in range(2):
-                t = 2 * two + u
-                nc.scalar.activation(z_pairs[:, two, :, u], back[:, u, :], ACT.Copy, scale=minus_gain[:, t : t + 1])
+                    turn_back(back[:, e, block(b)], 2 * two + e, b)
+            for e in range(2):
+                t = 2 * two + e
+                nc.scalar.activation(z_pairs[:, two, :, e], back[:, e, :], ACT.Copy, scale=minus_gain[:, t : t + 1])
         nc.scalar.copy(
             z_left[:].rearrange("p j t -> p (j t)").bitcast(U32).rearrange("p (j h) -> p j h", h=2),
             z_pairs[:].rearrange("p h j e -> p (h j e)").bitcast(U32).rearrange("p (h j) -> p j h", h=2),
@@ -336,13 +309,20 @@ def tile_picked_ljpot_none_p_kernel(tc, x_words, x_scales, w1, q, gn, w2, offs, 
                 idle_bank[:], w1_codes[:, block(t)].bitcast(FP8X4), w1_scale[:, block(t)],
                 x_codes[:].bitcast(FP8X4), x_scale[:], start=True, stop=True,
             )
-        backs = {b: turn_back(b) for b in (2, 3)}
-        z_blocks = {b: keep.tile([P, P, PACK], BF16, name=f"pull{last_pair}_{3 - b}", align_bytes=64) for b in (2, 3)}
-        make_z(backs[2], z_blocks[2][:])
-        quantised = {0: quantise_z(left, z_left, f"s{last_pair}")}
-        make_z(backs[3], z_blocks[3][:])
+        backs, z_blocks, quantised = {}, {}, {}
+        for b in (2, 3):
+            backs[b] = psum.tile([P, PACK, P], F32, name="e4" if b == 2 else "q1")
+            for t in range(PACK):
+                turn_back(backs[b][:, t, :], 4 + 2 * (t // 2) + b - 2, t % 2)
+        for b in (2, 3):
+            z_blocks[b] = keep.tile([P, P, PACK], BF16, name="pull6" if b == 2 else "z_block3", align_bytes=64)
+            nc.vector.tensor_tensor(
+                z_blocks[b][:], minus_gain[:].unsqueeze(1).to_broadcast([P, P, PACK]), backs[b][:].rearrange("p t j -> p j t"), ALU.mult
+            )
+            if b == 2:
+                quantised[0] = quantise_z(left, z_left, "s6")
         for b in (2, 3):
             quantised[b] = quantise_z(block(b), z_blocks[b], f"z_codes{b}")
         project(left, quantised[0], ["e2", "e3"])
-        for b in (2, 3):
-            project(block(b), quantised[b], ["q0", "e5"] if b == 2 else ["e0", "e1"])
+        project(block(2), quantised[2], ["q0", "e5"])
+        project(block(3), quantised[3], ["e0", "e1"])

@@ -205,11 +205,12 @@ def tile_picked_ljpot_none_p_kernel(tc, x_words, x_scales, w1, q, gn, w2, offs, 
             width = cols.stop - cols.start
             last = cols.stop == S
             z_codes, z_scale = quantised_z
-            for half in range(2):
-                out_acc = psum.tile([P, 2, width], F32, name=banks[half])
-                result = keep.tile([P, 2, width], F32, name=f"result{cols.start}_{half}")
-                for u in range(2):
-                    rows = block(2 * half + u)
+            each = PACK // len(banks)
+            for half in range(len(banks)):
+                out_acc = psum.tile([P, each, width], F32, name=banks[half])
+                result = keep.tile([P, each, width], F32, name=f"result{cols.start}_{half}")
+                for u in range(each):
+                    rows = block(each * half + u)
                     nc.tensor.matmul_mx(
                         out_acc[:, u, :], w2_codes[:, rows].bitcast(FP8X4), w2_scale[:, rows],
                         z_codes[:].bitcast(FP8X4), z_scale[:], start=True, stop=True,
@@ -217,7 +218,7 @@ def tile_picked_ljpot_none_p_kernel(tc, x_words, x_scales, w1, q, gn, w2, offs, 
                 copy_out = nc.vector.tensor_copy if cols != left and half == 1 else nc.scalar.copy
                 copy_out(result[:], out_acc[:])
                 queue = nc.scalar if last and half == 0 else nc.sync
-                queue.dma_start(out_rows[:, 2 * half : 2 * half + 2, cols], result[:])
+                queue.dma_start(out_rows[:, each * half : each * (half + 1), cols], result[:])
 
         for t in range(PACK):
             for i in range(PARTNERS):
@@ -323,6 +324,6 @@ def tile_picked_ljpot_none_p_kernel(tc, x_words, x_scales, w1, q, gn, w2, offs, 
                 quantised[0] = quantise_z(left, z_left, "s6")
         for b in (2, 3):
             quantised[b] = quantise_z(block(b), z_blocks[b], f"z_codes{b}")
-        project(left, quantised[0], ["e2", "e3"])
+        project(left, quantised[0], ["e2", "e3", "e0", "e1"])
         project(block(2), quantised[2], ["q0", "e5"])
-        project(block(3), quantised[3], ["e0", "e1"])
+        project(block(3), quantised[3], ["e4", "q1"])

@@ -22,14 +22,22 @@ GROUP = 16
 QUADRANT = 32
 PARTNERS = 2
 HALF = S // 2
+SCALAR_TILE = 2
 
 
 def tile_picked_ljpot_none_p_kernel(tc, x_words, x_scales, w1, q, gn, w2, offs, p1, p2, out):
     nc = tc.nc
-    left, right = slice(0, HALF), slice(HALF, S)
+    left = slice(0, HALF)
     with ExitStack() as ctx:
         keep = ctx.enter_context(tc.tile_pool(name="keep", bufs=1))
+        shared = ctx.enter_context(tc.tile_pool(name="shared", bufs=1))
         psum = ctx.enter_context(tc.psum_pool(name="psum", bufs=1))
+
+        def block(b):
+            return slice(b * P, (b + 1) * P)
+
+        def floats(name, *shape):
+            return keep.tile([P, *shape], F32, name=name, align_bytes=64)
 
         def load_list(name, source):
             offsets = keep.tile([P, S // GROUP], U16, name=name)
@@ -38,13 +46,13 @@ def tile_picked_ljpot_none_p_kernel(tc, x_words, x_scales, w1, q, gn, w2, offs, 
 
         w1_rows = w1.rearrange("(p j) c -> p j c", j=PACK)
 
-        def load_w1(half):
-            raw = keep.tile([P, PACK, H // 2], F32, name=f"stage{2 * half}")
-            nc.sync.dma_start(raw[:], w1_rows[:, :, half * (H // 2) : (half + 1) * (H // 2)])
+        def load_w1(e):
+            raw = floats(f"stage{2 * e}", PACK, H // 2)
+            nc.sync.dma_start(raw[:], w1_rows[:, :, e * (H // 2) : (e + 1) * (H // 2)])
             return raw
 
         w1_raw = [load_w1(0)]
-        x_scale_table = keep.tile([P, T], U8, name="stage1")
+        x_scale_table = keep.tile([P, T], U8, name="stage1", align_bytes=64)
         nc.gpsimd.memset(x_scale_table[:].bitcast(I32), 0)
         for quad in range(P // QUADRANT):
             nc.sync.dma_start(
@@ -75,15 +83,15 @@ def tile_picked_ljpot_none_p_kernel(tc, x_words, x_scales, w1, q, gn, w2, offs, 
         nc.vector.tensor_copy(x_codes[:], x_word_table[:].bitcast(U32).indirect(picks[:]))
 
         w1_bf = keep.tile([P, PACK, P, PACK], BF16, name="w1_bf", align_bytes=64)
-        for half, t0, t1, cast in (
+        for e, t0, t1, cast in (
             (0, 0, PACK, nc.scalar.copy),
             (1, 0, 1, nc.vector.tensor_copy),
             (1, 1, 2, nc.vector.tensor_copy),
             (1, 2, PACK, nc.scalar.copy),
         ):
             cast(
-                w1_bf[:, t0:t1, half * (P // 2) : (half + 1) * (P // 2), :].rearrange("p t m j -> p m j t"),
-                w1_raw[half][:].rearrange("p j (m t) -> p m j t", t=PACK)[:, :, :, t0:t1],
+                w1_bf[:, t0:t1, e * (P // 2) : (e + 1) * (P // 2), :].rearrange("p t m j -> p m j t"),
+                w1_raw[e][:].rearrange("p j (m t) -> p m j t", t=PACK)[:, :, :, t0:t1],
             )
         w1_codes = keep.tile([P, H], U32, name="w1_codes", align_bytes=64)
         w1_scale = keep.tile([P, H], U8, name="w1_scale", align_bytes=64)
@@ -93,66 +101,71 @@ def tile_picked_ljpot_none_p_kernel(tc, x_words, x_scales, w1, q, gn, w2, offs, 
                 w1_bf[:, t0:t1].rearrange("p t m j -> p (t m j)"),
             )
 
-        q_rows = q.rearrange("(p t) s -> p t s", t=PACK)
-        w2_raw = keep.tile([P, PACK, N], F32, name="stage0")
-        nc.sync.dma_start(w2_raw[:], w2.rearrange("(p j) m -> p j m", j=PACK))
-        strength = []
+        q_rows = q.rearrange("(p u e) s -> p e u s", u=2, e=2)
+        w2_rows = w2.rearrange("(p j) m -> p j m", j=PACK)
+        w2_halves = [slice(half * (N // 2), (half + 1) * (N // 2)) for half in range(2)]
+        first_two = floats("stage0", 2, 2 * S)
+        w2_raw = [first_two[:, 0, :].rearrange("p (j m) -> p j m", j=PACK), floats("stage1", PACK, N // 2)[:]]
+        q_tiles = [first_two[:, 1, :].rearrange("p (u s) -> p u s", u=2), floats("stage2", 2, S)[:]]
         for half in range(2):
-            two_tiles = keep.tile([P, 2, S], F32, name=f"stage{1 + half}")
-            nc.sync.dma_start(two_tiles[:], q_rows[:, 2 * half : 2 * half + 2, :])
-            strength.extend([two_tiles[:, 0, :], two_tiles[:, 1, :]])
+            nc.sync.dma_start(w2_raw[half], w2_rows[:, :, w2_halves[half]])
+            nc.sync.dma_start(q_tiles[half], q_rows[:, half])
+        strength = [q_tiles[t % 2][:, t // 2, :] for t in range(PACK)]
         minus_gain = keep.tile([P, PACK], F32, name="minus_gain")
         nc.vector.tensor_scalar(minus_gain[:], gain[:], -1.0, None, ALU.mult)
 
-        y = [keep.tile([P, S], F32, name=f"y{t}") for t in range(PACK)]
-        y_banks = ["e1", "e2", "e3", "e4", "q0", "q1", "e5"]
+        y = [floats(f"y{t}", S) for t in range(PACK)]
+        y_banks = ["bank1", "bank2", "bank3", "bank4", "bank6", "bank7", "bank5"]
         bank = 0
-        for t in range(PACK):
-            feats = slice(t * P, (t + 1) * P)
-            for cols in [slice(b * P, (b + 1) * P) for b in range(PACK)] if t == 0 else [slice(0, S)]:
+        for t in (0, 2, 1, 3):
+            for cols in [block(b) for b in range(PACK)] if t == 0 else [slice(0, S)]:
                 y_acc = psum.tile([P, cols.stop - cols.start], F32, name=y_banks[bank])
                 bank += 1
                 nc.tensor.matmul_mx(
-                    y_acc[:], w1_codes[:, feats].bitcast(FP8X4), w1_scale[:, feats],
+                    y_acc[:], w1_codes[:, block(t)].bitcast(FP8X4), w1_scale[:, block(t)],
                     x_codes[:, cols].bitcast(FP8X4), x_scale[:, cols], start=True, stop=True,
                 )
-                copy_out = nc.vector.tensor_copy if t == 0 and bank % 2 == 1 else nc.scalar.copy
-                copy_out(y[t][:, cols], y_acc[:])
-
-        def block(b):
-            return slice(b * P, (b + 1) * P)
-
-        def floats(name, *shape):
-            return keep.tile([P, *shape], F32, name=name, align_bytes=64)
+                if t < 3:
+                    copy_out = nc.vector.tensor_copy if t == 0 and bank % 2 == 1 else nc.scalar.copy
+                    copy_out(y[t][:, cols], y_acc[:])
 
         minus_partner = {}
 
-        def look_up(t, h, i, on_scalar, gathered):
+        def look_up(t, h, i, gathered):
             looked_up = y[t][:].indirect(partners[i][:, h * HALF // GROUP : (h + 1) * HALF // GROUP])
-            if on_scalar:
+            if t == SCALAR_TILE:
                 nc.scalar.activation(gathered, looked_up, ACT.Copy, scale=-1.0)
             else:
                 nc.vector.tensor_scalar(gathered, looked_up, -1.0, 0.0, ALU.mult, ALU.add)
             for b in range(2):
-                minus_partner[(t, 2 * h + b, i)] = gathered[:, b * P : (b + 1) * P]
+                minus_partner[(t, 2 * h + b, i)] = gathered[:, block(b)]
 
-        pieces = [[(t, 0), (t, 1)] for t in range(PACK)] + [[(t, b), (t + 1, b)] for t in (0, 2) for b in (2, 3)]
+        pieces = [[(t, 0), (t, 1)] for t in (0, 2, 1, 3)] + [[(t, b), (t + 1, b)] for t in (0, 2) for b in (2, 3)]
         flat = "p u i f -> p (u i f)"
         both = "p v u i f -> p (v u i f)"
         piece_shape = (2, PARTNERS, P)
         minus_d, q_turned, squared, inv_root, soft, s, pull, terms = {}, {}, {}, {}, {}, {}, {}, {}
 
-        def pair_tiles(store, first, name):
-            pair = floats(name, 2, *piece_shape)
+        piece_bytes = 4 * S
+
+        def pair_tiles(store, first, name, place=None):
+            if place is None:
+                pair = floats(name, 2, *piece_shape)
+            else:
+                pair = shared.tile([P, 2, *piece_shape], F32, name=name, offset=place * piece_bytes, align_bytes=64)
             store[first], store[first + 1] = pair[:, 0], pair[:, 1]
             return pair
 
-        def turn_differences(k, bank_name):
+        def turn_differences(k, bank_name, one_group=True):
             minus_d[k] = psum.tile([P, *piece_shape], F32, name=bank_name)
-            for i in range(PARTNERS):
-                for u, (t, b) in enumerate(pieces[k]):
-                    nc.tensor.matmul(minus_d[k][:, u, i, :], y[t][:, block(b)], ident[:], start=True, stop=False, is_transpose=True)
-                    nc.tensor.matmul(minus_d[k][:, u, i, :], minus_partner[(t, b, i)], ident[:], start=False, stop=True, is_transpose=True)
+            places = [(u, i) for i in range(PARTNERS) for u in range(2)]
+            sources = [y[pieces[k][u][0]][:, block(pieces[k][u][1])] for u, i in places]
+            sources += [minus_partner[(*pieces[k][u], i)] for u, i in places]
+            groups = [range(len(sources))] if one_group else [(n, n + len(places)) for n in range(len(places))]
+            for group in groups:
+                for n in group:
+                    u, i = places[n % len(places)]
+                    nc.tensor.matmul(minus_d[k][:, u, i, :], sources[n], ident[:], start=(n == group[0]), stop=(n == group[-1]), is_transpose=True)
 
         def turn_q(first, bank_name):
             pair = psum.tile([P, 2, 2, P], F32, name=bank_name)
@@ -165,9 +178,7 @@ def tile_picked_ljpot_none_p_kernel(tc, x_words, x_scales, w1, q, gn, w2, offs, 
             squared[k] = floats(f"squared{k}", *piece_shape)
             nc.scalar.activation(squared[k][:].rearrange(flat), minus_d[k][:].rearrange(flat), ACT.Square)
 
-        def inverse_root(k, name=None):
-            if name:
-                inv_root[k] = floats(name, *piece_shape)[:]
+        def inverse_root(k):
             nc.scalar.activation(inv_root[k].rearrange(flat), squared[k][:].rearrange(flat), ACT.Abs_reciprocal_sqrt, bias=one[:])
 
         def soften(k):
@@ -178,7 +189,7 @@ def tile_picked_ljpot_none_p_kernel(tc, x_words, x_scales, w1, q, gn, w2, offs, 
                 nc.scalar.activation(soft[k].rearrange(flat), root_k, ACT.Square)
 
         def products(first, s_name, pull_name):
-            s_pair = pair_tiles(s, first, s_name)
+            s_pair = pair_tiles(s, first, s_name, 2 if first == 4 else None)
             for k in (first, first + 1):
                 nc.vector.tensor_tensor(s[k], soft[k], q_turned[k].unsqueeze(2).to_broadcast([P, *piece_shape]), ALU.mult)
             pull_pair = pair_tiles(pull, first, pull_name)
@@ -187,6 +198,9 @@ def tile_picked_ljpot_none_p_kernel(tc, x_words, x_scales, w1, q, gn, w2, offs, 
                     pull[k].rearrange(flat), s[k].rearrange(flat), 1.0, minus_d[k][:].rearrange(flat), ALU.subtract, ALU.mult
                 )
             return s_pair, pull_pair
+
+        def multiply_term(engine, k):
+            engine.tensor_tensor(terms[k].rearrange(flat), s[k].rearrange(flat), pull[k].rearrange(flat), ALU.mult)
 
         def turn_back(summed, k, u):
             for i in range(PARTNERS):
@@ -201,129 +215,117 @@ def tile_picked_ljpot_none_p_kernel(tc, x_words, x_scales, w1, q, gn, w2, offs, 
 
         out_rows = out.rearrange("(mt p) j -> p mt j", p=P)
 
-        def project(cols, quantised_z, banks):
+        def project(cols, quantised_z, banks, copies, queues):
             width = cols.stop - cols.start
-            last = cols.stop == S
             z_codes, z_scale = quantised_z
             each = PACK // len(banks)
-            for half in range(len(banks)):
-                out_acc = psum.tile([P, each, width], F32, name=banks[half])
-                result = keep.tile([P, each, width], F32, name=f"result{cols.start}_{half}")
+            for n in range(len(banks)):
+                out_acc = psum.tile([P, each, width], F32, name=banks[n])
+                result = keep.tile([P, each, width], F32, name=f"result{cols.start}_{n}")
                 for u in range(each):
-                    rows = block(each * half + u)
+                    rows = block(each * n + u)
                     nc.tensor.matmul_mx(
                         out_acc[:, u, :], w2_codes[:, rows].bitcast(FP8X4), w2_scale[:, rows],
                         z_codes[:].bitcast(FP8X4), z_scale[:], start=True, stop=True,
                     )
-                copy_out = nc.vector.tensor_copy if cols != left and half == 1 else nc.scalar.copy
-                copy_out(result[:], out_acc[:])
-                queue = nc.scalar if last and half == 0 else nc.sync
-                queue.dma_start(out_rows[:, each * half : each * (half + 1), cols], result[:])
+                copies[n](result[:], out_acc[:])
+                queues[n].dma_start(out_rows[:, each * n : each * (n + 1), cols], result[:])
 
-        for t in range(PACK):
+        for t in (0, 2, 1, 3):
             for i in range(PARTNERS):
-                look_up(t, 0, i, t == 2, floats(f"gathered{t}{i}", HALF)[:])
+                look_up(t, 0, i, floats(f"gathered{t}{i}", HALF)[:])
+            if t == 0:
+                nc.vector.tensor_copy(y[3][:], y_acc[:])
         for k in range(PACK):
-            turn_differences(k, f"e{k}")
-        turn_q(0, "q0")
+            turn_differences(k, f"bank{k}")
 
-        w2_bf = keep.tile([P, N, PACK], BF16, name="w2_bf", align_bytes=64)
+        w2_bf = shared.tile([P, N, PACK], BF16, name="w2_bf", offset=piece_bytes, align_bytes=64)
         for half in range(2):
-            nc.gpsimd.tensor_scalar(
-                w2_bf[:, half * (N // 2) : (half + 1) * (N // 2), :],
-                w2_raw[:, :, half * (N // 2) : (half + 1) * (N // 2)].rearrange("p j m -> p m j"),
-                1.0, 0.0, ALU.mult, ALU.add,
-            )
+            nc.gpsimd.tensor_scalar(w2_bf[:, w2_halves[half], :], w2_raw[half].rearrange("p j m -> p m j"), 1.0, 0.0, ALU.mult, ALU.add)
         w2_codes = keep.tile([P, N], U32, name="w2_codes", align_bytes=64)
         w2_scale = keep.tile([P, N], U8, name="w2_scale", align_bytes=64)
         nc.vector.quantize_mx(w2_codes[:].bitcast(FP8X4), w2_scale[:], w2_bf[:].rearrange("p m j -> p (m j)"))
 
-        look_up(0, 1, 0, False, floats("gathered00", HALF)[:])
-        later = keep.tile([P, 5, HALF], F32, name="stage0")
-        for n, (t, i) in enumerate(((1, 0), (0, 1), (1, 1), (3, 0), (3, 1))):
-            look_up(t, 1, i, False, later[:, n, :])
-        turn_differences(4, "e4")
-        turn_differences(5, "e5")
-        turn_q(2, "q1")
+        later = floats("stage1", 4, HALF)
+        for n, (t, i) in enumerate(((0, 0), (1, 0), (0, 1), (1, 1))):
+            look_up(t, 1, i, later[:, n, :])
 
-        pair_tiles(soft, 0, "w2_bf")
-        pair_tiles(soft, 2, "soft2")
-        square(0)
-        look_up(2, 1, 0, True, floats("gathered01", HALF)[:])
-        inverse_root(0, "inv_root0")
-        soften(0)
-        for k, name in ((1, "gathered21"), (2, "gathered31")):
-            if k == 1:
+        pair_tiles(soft, 0, "soft0", 0)
+        pair_tiles(soft, 2, "soft2", 2)
+        for k in range(PACK):
+            inv_root[k] = floats(f"inv_root{k}", *piece_shape)[:]
+        turn_q(0, "bank6")
+        turn_differences(4, "bank4")
+        turn_differences(5, "bank5")
+        for first in (0, 2):
+            for k in (first, first + 1):
                 square(k)
-            square(k + 1)
-            inverse_root(k, name)
-            soften(k)
-        inverse_root(3, "inv_root3")
-        soften(3)
-        look_up(2, 1, 1, True, floats("squared2", HALF)[:])
+            for k in (first, first + 1):
+                inverse_root(k)
+                soften(k)
+        for i in range(PARTNERS):
+            look_up(2, 1, i, floats(f"squared{2 + i}", HALF)[:])
 
-        first_products = products(0, "s0", "gathered21")
-        turn_differences(6, "q0")
-        turn_q(4, "e0")
-        turn_differences(7, "e1")
-        second_products = products(2, "s2", "inv_root3")
-        turn_q(6, "q1")
-        for first, (s_pair, pull_pair), name in ((0, first_products, "squared3"), (2, second_products, "term2")):
-            term_pair = pair_tiles(terms, first, name)
-            nc.gpsimd.tensor_tensor(term_pair[:].rearrange(both), s_pair[:].rearrange(both), pull_pair[:].rearrange(both), ALU.mult)
+        first_products = products(0, "s0", "pull0")
+        last_gathers = shared.tile([P, PARTNERS, HALF], F32, name="last_gathers", offset=piece_bytes, align_bytes=64)
+        for i in range(PARTNERS):
+            look_up(3, 1, i, last_gathers[:, i, :])
+        turn_q(2, "bank6")
+        turn_differences(6, "bank7", one_group=False)
+        turn_differences(7, "bank0")
+        turn_q(4, "bank1")
+        products(2, "s2", "pull2")
+        turn_q(6, "bank6")
+        term_pair = pair_tiles(terms, 0, "inv_root3")
+        nc.gpsimd.tensor_tensor(term_pair[:].rearrange(both), first_products[0][:].rearrange(both), first_products[1][:].rearrange(both), ALU.mult)
+        pair_tiles(terms, 2, "term2")
+        for k in (2, 3):
+            multiply_term(nc.gpsimd, k)
 
         for first in (4, 6):
             for k in (first, first + 1):
                 square(k)
-            if first == 4:
-                pair_tiles(inv_root, first, "inv_root4")
-            else:
-                last_roots = keep.tile([P, 2, *piece_shape], F32, name="stage0")
-                inv_root[6], inv_root[7] = last_roots[:, 0], last_roots[:, 1]
+            pair_tiles(inv_root, first, "inv_root4" if first == 4 else "stage1")
             pair_tiles(soft, first, f"soft{first}")
             for step in (inverse_root, soften):
                 for k in (first, first + 1):
                     step(k)
-            products(first, "soft2" if first == 4 else "s6", f"pull{first}")
-            pair_tiles(terms, first, "term4" if first == 4 else "soft6")
-            engine = nc.gpsimd if first == 4 else nc.vector
-            for k in (first, first + 1):
-                engine.tensor_tensor(terms[k].rearrange(flat), s[k].rearrange(flat), pull[k].rearrange(flat), ALU.mult)
+            products(first, f"s{first}", f"pull{first}")
+        pair_tiles(terms, 4, "term4")
+        for k in (4, 5):
+            multiply_term(nc.gpsimd, k)
 
-        z_pairs = keep.tile([P, 2, HALF, 2], BF16, name="stage0")
+        z_pairs = keep.tile([P, 2, HALF, 2], BF16, name="stage1", align_bytes=64)
         z_left = keep.tile([P, HALF, PACK], BF16, name="z_left", align_bytes=64)
         for two in range(2):
-            back = psum.tile([P, 2, HALF], F32, name=f"e{2 + two}")
-            for e in range(2):
+            back = psum.tile([P, 2, HALF], F32, name=f"bank{2 + two}")
+            for v in range(2):
                 for b in range(2):
-                    turn_back(back[:, e, block(b)], 2 * two + e, b)
-            for e in range(2):
-                t = 2 * two + e
-                nc.scalar.activation(z_pairs[:, two, :, e], back[:, e, :], ACT.Copy, scale=minus_gain[:, t : t + 1])
+                    turn_back(back[:, v, block(b)], 2 * two + v, b)
+            for v in range(2):
+                t = pieces[2 * two + v][0][0]
+                nc.scalar.activation(z_pairs[:, t // 2, :, t % 2], back[:, v, :], ACT.Copy, scale=minus_gain[:, t : t + 1])
         nc.scalar.copy(
             z_left[:].rearrange("p j t -> p (j t)").bitcast(U32).rearrange("p (j h) -> p j h", h=2),
             z_pairs[:].rearrange("p h j e -> p (h j e)").bitcast(U32).rearrange("p (h j) -> p j h", h=2),
         )
-        idle_bank = psum.tile([P, S], F32, name="q1")
-        for t in range(2):
-            nc.tensor.matmul_mx(
-                idle_bank[:], w1_codes[:, block(t)].bitcast(FP8X4), w1_scale[:, block(t)],
-                x_codes[:].bitcast(FP8X4), x_scale[:], start=True, stop=True,
-            )
-        backs, z_blocks, quantised = {}, {}, {}
+        pair_tiles(terms, 6, "soft6")
+        for k in (6, 7):
+            multiply_term(nc.vector, k)
+        backs = {2: psum.tile([P, PACK, P], F32, name="bank4"), 3: psum.tile([P, PACK, P], F32, name="bank6")}
         for b in (2, 3):
-            backs[b] = psum.tile([P, PACK, P], F32, name="e4" if b == 2 else "q1")
             for t in range(PACK):
                 turn_back(backs[b][:, t, :], 4 + 2 * (t // 2) + b - 2, t % 2)
+        z_blocks, quantised = {}, {}
         for b in (2, 3):
             z_blocks[b] = keep.tile([P, P, PACK], BF16, name="pull6" if b == 2 else "z_block3", align_bytes=64)
             nc.vector.tensor_tensor(
                 z_blocks[b][:], minus_gain[:].unsqueeze(1).to_broadcast([P, P, PACK]), backs[b][:].rearrange("p t j -> p j t"), ALU.mult
             )
             if b == 2:
-                quantised[0] = quantise_z(left, z_left, "s6")
+                quantised_left = quantise_z(left, z_left, "s6")
         for b in (2, 3):
             quantised[b] = quantise_z(block(b), z_blocks[b], f"z_codes{b}")
-        project(left, quantised[0], ["e2", "e3", "e0", "e1"])
-        project(block(2), quantised[2], ["q0", "e5"])
-        project(block(3), quantised[3], ["e4", "q1"])
+        project(left, quantised_left, ["bank2", "bank3", "bank1", "bank0"], [nc.scalar.copy] * 4, [nc.sync] * 4)
+        project(block(2), quantised[2], ["bank7", "bank5"], [nc.scalar.copy, nc.vector.tensor_copy], [nc.sync, nc.sync])
+        project(block(3), quantised[3], ["bank4", "bank6"], [nc.scalar.copy, nc.vector.tensor_copy], [nc.scalar, nc.sync])

@@ -252,19 +252,20 @@ def tile_picked_ljpot_none_p_kernel(tc, x_words, x_scales, w1, q, gn, w2, offs, 
 
         pair_tiles(soft, 0, "soft0", 0)
         pair_tiles(soft, 2, "soft2", 2)
-        for k in range(PACK):
-            inv_root[k] = floats(f"inv_root{k}", *piece_shape)[:]
         turn_q(0, "bank6")
         turn_differences(4, "bank4")
         turn_differences(5, "bank5")
-        for first in (0, 2):
-            for k in (first, first + 1):
+        square(0)
+        look_up(2, 1, 0, floats("gathered01", HALF)[:])
+        for k, name in enumerate(("inv_root0", "gathered11", "gathered31", "inv_root3")):
+            if k == 1:
                 square(k)
-            for k in (first, first + 1):
-                inverse_root(k)
-                soften(k)
-        for i in range(PARTNERS):
-            look_up(2, 1, i, floats(f"squared{2 + i}", HALF)[:])
+            if k in (1, 2):
+                square(k + 1)
+            inv_root[k] = floats(name, *piece_shape)[:]
+            inverse_root(k)
+            soften(k)
+        look_up(2, 1, 1, floats("squared2", HALF)[:])
 
         first_products = products(0, "s0", "pull0")
         last_gathers = shared.tile([P, PARTNERS, HALF], F32, name="last_gathers", offset=piece_bytes, align_bytes=64)

@@ -27,7 +27,7 @@ SCALAR_TILE = 2
 
 def tile_picked_ljpot_none_p_kernel(tc, x_words, x_scales, w1, q, gn, w2, offs, p1, p2, out):
     nc = tc.nc
-    left = slice(0, HALF)
+    left, right = slice(0, HALF), slice(HALF, S)
     with ExitStack() as ctx:
         keep = ctx.enter_context(tc.tile_pool(name="keep", bufs=1))
         shared = ctx.enter_context(tc.tile_pool(name="shared", bufs=1))
@@ -115,17 +115,17 @@ def tile_picked_ljpot_none_p_kernel(tc, x_words, x_scales, w1, q, gn, w2, offs, 
         nc.vector.tensor_scalar(minus_gain[:], gain[:], -1.0, None, ALU.mult)
 
         y = [floats(f"y{t}", S) for t in range(PACK)]
-        y_banks = ["bank1", "bank2", "bank3", "bank4", "bank6", "bank7", "bank5"]
+        y_banks = ["bank1", "bank2", "bank3", "bank4", "bank6", "bank7", "bank1", "bank5"]
         bank = 0
         for t in (0, 2, 1, 3):
-            for cols in [block(b) for b in range(PACK)] if t == 0 else [slice(0, S)]:
+            for cols in {0: [block(b) for b in range(PACK)], 3: [left, right]}.get(t, [slice(0, S)]):
                 y_acc = psum.tile([P, cols.stop - cols.start], F32, name=y_banks[bank])
                 bank += 1
                 nc.tensor.matmul_mx(
                     y_acc[:], w1_codes[:, block(t)].bitcast(FP8X4), w1_scale[:, block(t)],
                     x_codes[:, cols].bitcast(FP8X4), x_scale[:, cols], start=True, stop=True,
                 )
-                if t < 3:
+                if (t, cols) != (3, right):
                     copy_out = nc.vector.tensor_copy if t == 0 and bank % 2 == 1 else nc.scalar.copy
                     copy_out(y[t][:, cols], y_acc[:])
 
@@ -235,7 +235,7 @@ def tile_picked_ljpot_none_p_kernel(tc, x_words, x_scales, w1, q, gn, w2, offs, 
             for i in range(PARTNERS):
                 look_up(t, 0, i, floats(f"gathered{t}{i}", HALF)[:])
             if t == 0:
-                nc.vector.tensor_copy(y[3][:], y_acc[:])
+                nc.vector.tensor_copy(y[3][:, right], y_acc[:])
         for k in range(PACK):
             turn_differences(k, f"bank{k}")
 
@@ -256,16 +256,15 @@ def tile_picked_ljpot_none_p_kernel(tc, x_words, x_scales, w1, q, gn, w2, offs, 
         turn_differences(4, "bank4")
         turn_differences(5, "bank5")
         square(0)
-        look_up(2, 1, 0, floats("gathered01", HALF)[:])
-        for k, name in enumerate(("inv_root0", "gathered11", "gathered31", "inv_root3")):
-            if k == 1:
-                square(k)
-            if k in (1, 2):
+        for k, name in enumerate(("gathered21", "gathered11", "gathered31", "inv_root3")):
+            if k + 1 < PACK:
                 square(k + 1)
+            else:
+                look_up(2, 1, 0, floats("squared2", HALF)[:])
             inv_root[k] = floats(name, *piece_shape)[:]
             inverse_root(k)
             soften(k)
-        look_up(2, 1, 1, floats("squared2", HALF)[:])
+        look_up(2, 1, 1, floats("squared3", HALF)[:])
 
         first_products = products(0, "s0", "pull0")
         last_gathers = shared.tile([P, PARTNERS, HALF], F32, name="last_gathers", offset=piece_bytes, align_bytes=64)

@@ -101,7 +101,7 @@ def tile_picked_ljpot_none_p_kernel(tc, x_words, x_scales, w1, q, gn, w2, offs, 
                 w1_bf[:, t0:t1].rearrange("p t m j -> p (t m j)"),
             )
 
-        q_rows = q.rearrange("(p u e) s -> p e u s", u=2, e=2)
+        q_rows = q.rearrange("(p h e) s -> p h e s", h=2, e=2)
         w2_rows = w2.rearrange("(p j) m -> p j m", j=PACK)
         w2_halves = [slice(half * (N // 2), (half + 1) * (N // 2)) for half in range(2)]
         first_two = floats("stage0", 2, 2 * S)
@@ -110,14 +110,14 @@ def tile_picked_ljpot_none_p_kernel(tc, x_words, x_scales, w1, q, gn, w2, offs, 
         for half in range(2):
             nc.sync.dma_start(w2_raw[half], w2_rows[:, :, w2_halves[half]])
             nc.sync.dma_start(q_tiles[half], q_rows[:, half])
-        strength = [q_tiles[t % 2][:, t // 2, :] for t in range(PACK)]
+        strength = [q_tiles[t // 2][:, t % 2, :] for t in range(PACK)]
         minus_gain = keep.tile([P, PACK], F32, name="minus_gain")
         nc.vector.tensor_scalar(minus_gain[:], gain[:], -1.0, None, ALU.mult)
 
         y = [floats(f"y{t}", S) for t in range(PACK)]
         y_banks = ["bank1", "bank2", "bank3", "bank4", "bank6", "bank7", "bank1", "bank5"]
         bank = 0
-        for t in (0, 2, 1, 3):
+        for t in range(PACK):
             for cols in {0: [block(b) for b in range(PACK)], 3: [left, right]}.get(t, [slice(0, S)]):
                 y_acc = psum.tile([P, cols.stop - cols.start], F32, name=y_banks[bank])
                 bank += 1
@@ -140,7 +140,7 @@ def tile_picked_ljpot_none_p_kernel(tc, x_words, x_scales, w1, q, gn, w2, offs, 
             for b in range(2):
                 minus_partner[(t, 2 * h + b, i)] = gathered[:, block(b)]
 
-        pieces = [[(t, 0), (t, 1)] for t in (0, 2, 1, 3)] + [[(t, b), (t + 1, b)] for t in (0, 2) for b in (2, 3)]
+        pieces = [[(t, 0), (t, 1)] for t in range(PACK)] + [[(t, b), (t + 1, b)] for t in (0, 2) for b in (2, 3)]
         flat = "p u i f -> p (u i f)"
         both = "p v u i f -> p (v u i f)"
         piece_shape = (2, PARTNERS, P)
@@ -231,12 +231,17 @@ def tile_picked_ljpot_none_p_kernel(tc, x_words, x_scales, w1, q, gn, w2, offs, 
                 copies[n](result[:], out_acc[:])
                 queues[n].dma_start(out_rows[:, each * n : each * (n + 1), cols], result[:])
 
-        for t in (0, 2, 1, 3):
+        for t in (0, 1, 3):
             for i in range(PARTNERS):
                 look_up(t, 0, i, floats(f"gathered{t}{i}", HALF)[:])
             if t == 0:
                 nc.vector.tensor_copy(y[3][:, right], y_acc[:])
-        for k in range(PACK):
+        look_up(2, 0, 0, floats("gathered20", HALF)[:])
+        for k in range(2):
+            turn_differences(k, f"bank{k}")
+        square(0)
+        look_up(2, 0, 1, floats("gathered01", HALF)[:])
+        for k in (2, 3):
             turn_differences(k, f"bank{k}")
 
         w2_bf = shared.tile([P, N, PACK], BF16, name="w2_bf", offset=piece_bytes, align_bytes=64)
@@ -255,11 +260,12 @@ def tile_picked_ljpot_none_p_kernel(tc, x_words, x_scales, w1, q, gn, w2, offs, 
         turn_q(0, "bank6")
         turn_differences(4, "bank4")
         turn_differences(5, "bank5")
-        square(0)
-        for k, name in enumerate(("gathered21", "gathered11", "gathered31", "inv_root3")):
-            if k + 1 < PACK:
+        for k, name in enumerate(("inv_root0", "gathered01", "gathered31", "inv_root3")):
+            if k == 1:
+                square(k)
+            if k in (1, 2):
                 square(k + 1)
-            else:
+            if k == 3:
                 look_up(2, 1, 0, floats("squared2", HALF)[:])
             inv_root[k] = floats(name, *piece_shape)[:]
             inverse_root(k)

from contextlib import ExitStack

import concourse.mybir as mybir
from concourse.masks import make_identity

K, T, S, N, H = 512, 2048, 512, 512, 512
FLOPS = 2 * K * H * S + 2 * H * N * S

F32 = mybir.dt.float32
BF16 = mybir.dt.bfloat16
I32 = mybir.dt.int32
U32 = mybir.dt.uint32
U16 = mybir.dt.uint16
U8 = mybir.dt.uint8
FP8X4 = mybir.dt.float8_e4m3fn_x4
ACT = mybir.ActivationFunctionType
ALU = mybir.AluOpType

P = 128
PACK = 4
GROUP = 16
QUADRANT = 32
PARTNERS = 2
HALF = S // 2
SCALAR_TILE = 2


def tile_picked_ljpot_none_p_kernel(tc, x_words, x_scales, w1, q, gn, w2, offs, p1, p2, out):
    nc = tc.nc
    left, right = slice(0, HALF), slice(HALF, S)
    with ExitStack() as ctx:
        keep = ctx.enter_context(tc.tile_pool(name="keep", bufs=1))
        shared = ctx.enter_context(tc.tile_pool(name="shared", bufs=1))
        psum = ctx.enter_context(tc.psum_pool(name="psum", bufs=1))

        def block(b):
            return slice(b * P, (b + 1) * P)

        def floats(name, *shape):
            return keep.tile([P, *shape], F32, name=name, align_bytes=64)

        def load_list(name, source):
            offsets = keep.tile([P, S // GROUP], U16, name=name)
            nc.sync.dma_start(offsets[:], source)
            return offsets

        w1_rows = w1.rearrange("(p j) c -> p j c", j=PACK)

        def load_w1(e):
            raw = floats(f"stage{2 * e}", PACK, H // 2)
            nc.sync.dma_start(raw[:], w1_rows[:, :, e * (H // 2) : (e + 1) * (H // 2)])
            return raw

        w1_raw = [load_w1(0)]
        x_scale_table = keep.tile([P, T], U8, name="stage1", align_bytes=64)
        nc.gpsimd.memset(x_scale_table[:].bitcast(I32), 0)
        for quad in range(P // QUADRANT):
            nc.sync.dma_start(
                x_scale_table[QUADRANT * quad : QUADRANT * quad + 4, :].bitcast(I32),
                x_scales[0, 4 * quad : 4 * quad + 4, :].bitcast(I32),
            )
        picks = load_list("picks", offs)
        x_word_table = keep.tile([P, T], I32, name="x_word_table")
        nc.sync.dma_start(x_word_table[:], x_words[0].rearrange("p n t -> p (n t)").bitcast(I32))
        w1_raw.append(load_w1(1))
        partners = [load_list("partner0", p1), load_list("partner1", p2)]
        gain = keep.tile([P, PACK], F32, name="gain")
        nc.sync.dma_start(gain[:], gn.rearrange("(p t) o -> p (t o)", t=PACK))

        seed = keep.tile([P, 1], F32, name="seed")
        root = keep.tile([P, 1], F32, name="root")
        one = keep.tile([P, 1], F32, name="one")
        nc.vector.memset(seed[:], 1.0)
        nc.scalar.activation(root[:], seed[:], ACT.Abs_reciprocal_sqrt)
        nc.scalar.activation(one[:], root[:], ACT.Sign)

        ident = keep.tile([P, P], F32, name="ident")
        make_identity(nc, ident[:])

        x_scale = keep.tile([P, S], U8, name="x_scale", align_bytes=64)
        nc.vector.tensor_copy(x_scale[:], x_scale_table[:].indirect(picks[:]))
        x_codes = keep.tile([P, S], U32, name="x_codes", align_bytes=64)
        nc.vector.tensor_copy(x_codes[:], x_word_table[:].bitcast(U32).indirect(picks[:]))

        w1_bf = keep.tile([P, PACK, P, PACK], BF16, name="w1_bf", align_bytes=64)
        for e, t0, t1, cast in (
            (0, 0, PACK, nc.scalar.copy),
            (1, 0, 1, nc.vector.tensor_copy),
            (1, 1, 2, nc.vector.tensor_copy),
            (1, 2, PACK, nc.scalar.copy),
        ):
            cast(
                w1_bf[:, t0:t1, e * (P // 2) : (e + 1) * (P // 2), :].rearrange("p t m j -> p m j t"),
                w1_raw[e][:].rearrange("p j (m t) -> p m j t", t=PACK)[:, :, :, t0:t1],
            )
        w1_codes = keep.tile([P, H], U32, name="w1_codes", align_bytes=64)
        w1_scale = keep.tile([P, H], U8, name="w1_scale", align_bytes=64)
        for t0, t1 in ((0, 1), (1, 2), (2, 4)):
            nc.vector.quantize_mx(
                w1_codes[:, t0 * P : t1 * P].bitcast(FP8X4), w1_scale[:, t0 * P : t1 * P],
                w1_bf[:, t0:t1].rearrange("p t m j -> p (t m j)"),
            )

        q_rows = q.rearrange("(p h e) s -> p h e s", h=2, e=2)
        w2_rows = w2.rearrange("(p j) m -> p j m", j=PACK)
        w2_halves = [slice(half * (N // 2), (half + 1) * (N // 2)) for half in range(2)]
        first_two = floats("stage0", 2, 2 * S)
        w2_raw = [first_two[:, 0, :].rearrange("p (j m) -> p j m", j=PACK), floats("stage1", PACK, N // 2)[:]]
        q_tiles = [first_two[:, 1, :].rearrange("p (u s) -> p u s", u=2), floats("stage2", 2, S)[:]]
        for half in range(2):
            nc.sync.dma_start(w2_raw[half], w2_rows[:, :, w2_halves[half]])
            nc.sync.dma_start(q_tiles[half], q_rows[:, half])
        strength = [q_tiles[t // 2][:, t % 2, :] for t in range(PACK)]
        minus_gain = keep.tile([P, PACK], F32, name="minus_gain")
        nc.vector.tensor_scalar(minus_gain[:], gain[:], -1.0, None, ALU.mult)

        y = [floats(f"y{t}", S) for t in range(PACK)]
        y_banks = ["bank1", "bank2", "bank3", "bank4", "bank6", "bank7", "bank1", "bank5"]
        bank = 0
        for t in range(PACK):
            for cols in {0: [block(b) for b in range(PACK)], 3: [left, right]}.get(t, [slice(0, S)]):
                y_acc = psum.tile([P, cols.stop - cols.start], F32, name=y_banks[bank])
                bank += 1
                nc.tensor.matmul_mx(
                    y_acc[:], w1_codes[:, block(t)].bitcast(FP8X4), w1_scale[:, block(t)],
                    x_codes[:, cols].bitcast(FP8X4), x_scale[:, cols], start=True, stop=True,
                )
                if (t, cols) != (3, right):
                    copy_out = nc.vector.tensor_copy if t == 0 and bank % 2 == 1 else nc.scalar.copy
                    copy_out(y[t][:, cols], y_acc[:])

        minus_partner = {}

        def look_up(t, h, i, gathered):
            looked_up = y[t][:].indirect(partners[i][:, h * HALF // GROUP : (h + 1) * HALF // GROUP])
            if t == SCALAR_TILE:
                nc.scalar.activation(gathered, looked_up, ACT.Copy, scale=-1.0)
            else:
                nc.vector.tensor_scalar(gathered, looked_up, -1.0, 0.0, ALU.mult, ALU.add)
            for b in range(2):
                minus_partner[(t, 2 * h + b, i)] = gathered[:, block(b)]

        pieces = [[(t, 0), (t, 1)] for t in range(PACK)] + [[(t, b), (t + 1, b)] for t in (0, 2) for b in (2, 3)]
        flat = "p u i f -> p (u i f)"
        both = "p v u i f -> p (v u i f)"
        piece_shape = (2, PARTNERS, P)
        minus_d, q_turned, squared, inv_root, soft, s, pull, terms = {}, {}, {}, {}, {}, {}, {}, {}

        piece_bytes = 4 * S

        def pair_tiles(store, first, name, place=None):
            if place is None:
                pair = floats(name, 2, *piece_shape)
            else:
                pair = shared.tile([P, 2, *piece_shape], F32, name=name, offset=place * piece_bytes, align_bytes=64)
            store[first], store[first + 1] = pair[:, 0], pair[:, 1]
            return pair

        def turn_differences(k, bank_name, one_group=True):
            minus_d[k] = psum.tile([P, *piece_shape], F32, name=bank_name)
            places = [(u, i) for i in range(PARTNERS) for u in range(2)]
            sources = [y[pieces[k][u][0]][:, block(pieces[k][u][1])] for u, i in places]
            sources += [minus_partner[(*pieces[k][u], i)] for u, i in places]
            groups = [range(len(sources))] if one_group else [(n, n + len(places)) for n in range(len(places))]
            for group in groups:
                for n in group:
                    u, i = places[n % len(places)]
                    nc.tensor.matmul(minus_d[k][:, u, i, :], sources[n], ident[:], start=(n == group[0]), stop=(n == group[-1]), is_transpose=True)

        def turn_q(first, bank_name):
            pair = psum.tile([P, 2, 2, P], F32, name=bank_name)
            for v in range(2):
                for u, (t, b) in enumerate(pieces[first + v]):
                    nc.tensor.transpose(pair[:, v, u, :], strength[t][:, block(b)], ident[:])
                q_turned[first + v] = pair[:, v]

        def square(k):
            squared[k] = floats(f"squared{k}", *piece_shape)
            nc.scalar.activation(squared[k][:].rearrange(flat), minus_d[k][:].rearrange(flat), ACT.Square)

        def inverse_root(k):
            nc.scalar.activation(inv_root[k].rearrange(flat), squared[k][:].rearrange(flat), ACT.Abs_reciprocal_sqrt, bias=one[:])

        def soften(k):
            root_k = inv_root[k].rearrange(flat)
            if k < PACK:
                nc.gpsimd.tensor_tensor(soft[k].rearrange(flat), root_k, root_k, ALU.mult)
            else:
                nc.scalar.activation(soft[k].rearrange(flat), root_k, ACT.Square)

        def products(first, s_name, pull_name):
            s_pair = pair_tiles(s, first, s_name, 2 if first == 4 else None)
            for k in (first, first + 1):
                nc.vector.tensor_tensor(s[k], soft[k], q_turned[k].unsqueeze(2).to_broadcast([P, *piece_shape]), ALU.mult)
            pull_pair = pair_tiles(pull, first, pull_name)
            for k in (first, first + 1):
                nc.vector.scalar_tensor_tensor(
                    pull[k].rearrange(flat), s[k].rearrange(flat), 1.0, minus_d[k][:].rearrange(flat), ALU.subtract, ALU.mult
                )
            return s_pair, pull_pair

        def multiply_term(engine, k):
            engine.tensor_tensor(terms[k].rearrange(flat), s[k].rearrange(flat), pull[k].rearrange(flat), ALU.mult)

        def turn_back(summed, k, u):
            for i in range(PARTNERS):
                nc.tensor.matmul(summed, terms[k][:, u, i, :], ident[:], start=(i == 0), stop=(i == PARTNERS - 1), is_transpose=True)

        def quantise_z(cols, z_bf, codes_name):
            width = cols.stop - cols.start
            z_codes = keep.tile([P, width], U32, name=codes_name, align_bytes=64)
            z_scale = keep.tile([P, width], U8, name=f"z_scale{cols.start}", align_bytes=64)
            nc.vector.quantize_mx(z_codes[:].bitcast(FP8X4), z_scale[:], z_bf[:].rearrange("p c t -> p (c t)"))
            return z_codes, z_scale

        out_rows = out.rearrange("(mt p) j -> p mt j", p=P)

        def project(cols, quantised_z, banks, copies, queues):
            width = cols.stop - cols.start
            z_codes, z_scale = quantised_z
            each = PACK // len(banks)
            for n in range(len(banks)):
                out_acc = psum.tile([P, each, width], F32, name=banks[n])
                result = keep.tile([P, each, width], F32, name=f"result{cols.start}_{n}")
                for u in range(each):
                    rows = block(each * n + u)
                    nc.tensor.matmul_mx(
                        out_acc[:, u, :], w2_codes[:, rows].bitcast(FP8X4), w2_scale[:, rows],
                        z_codes[:].bitcast(FP8X4), z_scale[:], start=True, stop=True,
                    )
                copies[n](result[:], out_acc[:])
                queues[n].dma_start(out_rows[:, each * n : each * (n + 1), cols], result[:])

        for t in (0, 1, 3):
            for i in range(PARTNERS):
                look_up(t, 0, i, floats(f"gathered{t}{i}", HALF)[:])
            if t == 0:
                nc.vector.tensor_copy(y[3][:, right], y_acc[:])
        look_up(2, 0, 0, floats("gathered20", HALF)[:])
        for k in range(2):
            turn_differences(k, f"bank{k}")
        square(0)
        look_up(2, 0, 1, floats("gathered01", HALF)[:])
        for k in (2, 3):
            turn_differences(k, f"bank{k}")

        w2_bf = shared.tile([P, N, PACK], BF16, name="w2_bf", offset=piece_bytes, align_bytes=64)
        for half in range(2):
            nc.gpsimd.tensor_scalar(w2_bf[:, w2_halves[half], :], w2_raw[half].rearrange("p j m -> p m j"), 1.0, 0.0, ALU.mult, ALU.add)
        w2_codes = keep.tile([P, N], U32, name="w2_codes", align_bytes=64)
        w2_scale = keep.tile([P, N], U8, name="w2_scale", align_bytes=64)
        nc.vector.quantize_mx(w2_codes[:].bitcast(FP8X4), w2_scale[:], w2_bf[:].rearrange("p m j -> p (m j)"))

        later = floats("stage1", 4, HALF)
        for n, (t, i) in enumerate(((0, 0), (1, 0), (0, 1), (1, 1))):
            look_up(t, 1, i, later[:, n, :])

        pair_tiles(soft, 0, "soft0", 0)
        pair_tiles(soft, 2, "soft2", 2)
        turn_q(0, "bank6")
        turn_differences(4, "bank4")
        turn_differences(5, "bank5")
        for k, name in enumerate(("inv_root0", "gathered01", "gathered31", "inv_root3")):
            if k == 1:
                square(k)
            if k in (1, 2):
                square(k + 1)
            if k == 3:
                look_up(2, 1, 0, floats("squared2", HALF)[:])
            inv_root[k] = floats(name, *piece_shape)[:]
            inverse_root(k)
            soften(k)
        look_up(2, 1, 1, floats("squared3", HALF)[:])

        first_products = products(0, "s0", "pull0")
        last_gathers = shared.tile([P, PARTNERS, HALF], F32, name="last_gathers", offset=piece_bytes, align_bytes=64)
        for i in range(PARTNERS):
            look_up(3, 1, i, last_gathers[:, i, :])
        turn_q(2, "bank6")
        turn_differences(6, "bank7", one_group=False)
        turn_differences(7, "bank0")
        turn_q(4, "bank1")
        products(2, "s2", "pull2")
        turn_q(6, "bank6")
        term_pair = pair_tiles(terms, 0, "inv_root3")
        nc.gpsimd.tensor_tensor(term_pair[:].rearrange(both), first_products[0][:].rearrange(both), first_products[1][:].rearrange(both), ALU.mult)
        pair_tiles(terms, 2, "term2")
        for k in (2, 3):
            multiply_term(nc.gpsimd, k)

        for first in (4, 6):
            for k in (first, first + 1):
                square(k)
            pair_tiles(inv_root, first, "inv_root4" if first == 4 else "stage1")
            pair_tiles(soft, first, f"soft{first}")
            for step in (inverse_root, soften):
                for k in (first, first + 1):
                    step(k)
            products(first, f"s{first}", f"pull{first}")
        pair_tiles(terms, 4, "term4")
        for k in (4, 5):
            multiply_term(nc.gpsimd, k)

        z_pairs = keep.tile([P, 2, HALF, 2], BF16, name="stage1", align_bytes=64)
        z_left = keep.tile([P, HALF, PACK], BF16, name="z_left", align_bytes=64)
        for two in range(2):
            back = psum.tile([P, 2, HALF], F32, name=f"bank{2 + two}")
            for v in range(2):
                for b in range(2):
                    turn_back(back[:, v, block(b)], 2 * two + v, b)
            for v in range(2):
                t = pieces[2 * two + v][0][0]
                nc.scalar.activation(z_pairs[:, t // 2, :, t % 2], back[:, v, :], ACT.Copy, scale=minus_gain[:, t : t + 1])
        nc.scalar.copy(
            z_left[:].rearrange("p j t -> p (j t)").bitcast(U32).rearrange("p (j h) -> p j h", h=2),
            z_pairs[:].rearrange("p h j e -> p (h j e)").bitcast(U32).rearrange("p (h j) -> p j h", h=2),
        )
        pair_tiles(terms, 6, "soft6")
        for k in (6, 7):
            multiply_term(nc.vector, k)
        backs = {2: psum.tile([P, PACK, P], F32, name="bank4"), 3: psum.tile([P, PACK, P], F32, name="bank6")}
        for b in (2, 3):
            for t in range(PACK):
                turn_back(backs[b][:, t, :], 4 + 2 * (t // 2) + b - 2, t % 2)
        z_blocks, quantised = {}, {}
        for b in (2, 3):
            z_blocks[b] = keep.tile([P, P, PACK], BF16, name="pull6" if b == 2 else "z_block3", align_bytes=64)
            nc.vector.tensor_tensor(
                z_blocks[b][:], minus_gain[:].unsqueeze(1).to_broadcast([P, P, PACK]), backs[b][:].rearrange("p t j -> p j t"), ALU.mult
            )
            if b == 2:
                quantised_left = quantise_z(left, z_left, "s6")
        for b in (2, 3):
            quantised[b] = quantise_z(block(b), z_blocks[b], f"z_codes{b}")
        project(left, quantised_left, ["bank2", "bank3", "bank1", "bank0"], [nc.scalar.copy] * 4, [nc.sync] * 4)
        project(block(2), quantised[2], ["bank7", "bank5"], [nc.scalar.copy, nc.vector.tensor_copy], [nc.sync, nc.sync])
        project(block(3), quantised[3], ["bank4", "bank6"], [nc.scalar.copy, nc.vector.tensor_copy], [nc.scalar, nc.sync])
